import numpy as np
import ml_dtypes


def mxq(x, axis, fmt="e4m3"):
    dtype, down = {"e4m3": (ml_dtypes.float8_e4m3fn, 7), "e5m2": (ml_dtypes.float8_e5m2, 14)}[fmt]
    v = np.moveaxis(np.asarray(x, np.float32).astype(ml_dtypes.bfloat16).astype(np.float64), axis, -1)
    blocks = v.reshape(v.shape[:-1] + (-1, 32))
    amax = np.abs(blocks).max(-1, keepdims=True)
    byte = np.maximum(np.where(amax > 0, np.frexp(amax)[1] - 1 + 127, 0) - down, 1)
    scale = np.exp2(byte - 127.0)
    codes = (blocks / scale).astype(np.float32).astype(dtype).astype(np.float64)
    return np.moveaxis((codes * scale).reshape(v.shape), -1, axis)


WIDE = False


def mx_kscale(k):
    if not WIDE:
        return np.ones(k)
    levels = np.array([10, -10, 5, -5, 0])
    if k % 512:
        return np.exp2(np.random.permutation(np.resize(levels, k // 32))).repeat(32)
    a = np.empty((k // 512, 16))
    for p in range(k // 512):
        a[p, :8] = np.random.permutation(np.resize(levels, 8))
        for g in range(8):
            far = levels[np.abs(levels - a[p, g]) >= 10]
            a[p, g + 8] = far[np.random.randint(len(far))]
    return np.exp2(a.ravel()).repeat(32)


def f64(x):
    return np.asarray(x).astype(np.float64)


def striped(idx):
    return np.tile(idx.reshape(-1, 16).T, (8, 1)).astype(np.uint16)


def unstriped(offs):
    return offs[:16].T.reshape(-1).astype(np.int64)


E2M1 = np.array([0.0, 0.5, 1.0, 1.5, 2.0, 3.0, 4.0, 6.0, -0.0, -0.5, -1.0, -1.5, -2.0, -3.0, -4.0, -6.0])


def pack_weight(w, fmt):
    k, n = w.shape
    w = f64(np.asarray(w, np.float32).astype(ml_dtypes.bfloat16)).reshape(k // 32, 32, n)
    amax = np.abs(w).max(1)
    if fmt == "e4m3":
        byte = np.frexp(amax)[1] - 1 + 127 - 7
    else:
        mant, ex = np.frexp(amax / 6.0)
        byte = np.where(mant > 0.5, ex, ex - 1) + 127
    byte = np.clip(np.where(amax > 0, byte, 1), 1, 254)
    scaled = (w * np.exp2(127.0 - byte)[:, None, :]).reshape(k, n).astype(np.float32)
    by_word = np.ascontiguousarray(scaled.reshape(k // 512, 128, 4, n).transpose(0, 1, 3, 2))
    if fmt == "e4m3":
        words = by_word.astype(ml_dtypes.float8_e4m3fn).view(np.uint8)
    else:
        c = by_word.astype(ml_dtypes.float4_e2m1fn).view(np.uint8) & 0xF
        words = (c[..., 0::2] | (c[..., 1::2] << 4)).reshape(k // 512, 128, 2 * n)
    return np.ascontiguousarray(words), np.ascontiguousarray(byte.astype(np.uint8).reshape(k // 512, 16, n))


def unpack_weight(words, scales, fmt):
    g, _, n = scales.shape
    words = np.ascontiguousarray(words).reshape(g, 128, n, -1)
    if fmt == "e4m3":
        vals = words.view(ml_dtypes.float8_e4m3fn).astype(np.float64)
    else:
        nib = np.empty((g, 128, n, 4), np.uint8)
        nib[..., 0::2] = words & 0xF
        nib[..., 1::2] = words >> 4
        vals = E2M1[nib]
    vals = vals * np.repeat(np.exp2(scales.astype(np.float64) - 127.0), 8, axis=1)[..., None]
    return vals.transpose(0, 1, 3, 2).reshape(g * 512, n)


def gelu(v):
    return 0.5 * v * (1.0 + np.tanh(np.sqrt(2.0 / np.pi) * (v + 0.044715 * v**3)))


def striped8(idx):
    return np.concatenate([v.reshape(-1, 16).T for v in idx]).astype(np.uint16)


def unstriped8(offs):
    return np.stack([offs[16 * g:16 * g + 16].T.reshape(-1) for g in range(8)]).astype(np.int64)


def runs(v, idx8):
    k = np.arange(v.shape[0])
    return v[k[:, None], idx8[k % 512 // 64]]


def put_heads(h, wgs, idx8, t2):
    r = np.arange(h.shape[0])
    page = np.zeros((h.shape[0], t2))
    page[r[:, None], idx8[r % 512 // 64]] = wgs[r // 4 % 128] * h
    return page


K, H, N, T, S, T2 = 1024, 1536, 512, 2048, 1024, 2048

def setup_inputs():
    n = np.random.standard_normal
    s = mx_kscale(K)[:, None]
    u = mx_kscale(H)[:, None]
    tab_words, tab_scales = pack_weight(n((K, T)) * s, "e4m3")
    wa = n((K, H)) / np.sqrt(K) / s * u.T
    wa_words, wa_scales = pack_weight(wa, "e2m1")
    wb = n((H, N)) * 1.2 / np.sqrt(H) / u
    wgo = np.repeat(np.random.uniform(0.5, 2.0, (8, S)), 16, axis=0)
    offs = striped8(np.stack([np.random.permutation(T)[:S] for _ in range(8)]))
    offs2 = striped8(np.stack([np.random.permutation(T2)[:S] for _ in range(8)]))
    return {
        "tab_words": tab_words, "tab_scales": tab_scales,
        "wa_words": wa_words, "wa_scales": wa_scales,
        "wb": wb.astype(np.float32),
        "wgo": wgo.astype(np.float32),
        "offs": offs, "offs2": offs2,
    }

def reference(tab_words, tab_scales, wa_words, wa_scales, wb, wgo, offs, offs2):
    v = runs(unpack_weight(tab_words, tab_scales, "e4m3"), unstriped8(offs))
    wa = unpack_weight(wa_words, wa_scales, "e2m1")
    h = np.maximum(wa.T @ v, 0.0)
    q = mxq(f64(wb), 0, "e4m3").T @ mxq(h, 0, "e4m3")
    y = q * (1.0 - np.square(np.tanh(q)))
    return put_heads(y, f64(wgo), unstriped8(offs2), T2)

@@ -1,0 +1,257 @@
+from contextlib import ExitStack
+
+import concourse.mybir as mybir
+
+K, H, N, T, S, T2 = 1024, 1536, 512, 2048, 1024, 2048
+FLOPS = 2 * K * H * S + 2 * H * N * S
+
+F32 = mybir.dt.float32
+BF16 = mybir.dt.bfloat16
+I32 = mybir.dt.int32
+U32 = mybir.dt.uint32
+U16 = mybir.dt.uint16
+U8 = mybir.dt.uint8
+FP8X4 = mybir.dt.float8_e4m3fn_x4
+FP4X4 = mybir.dt.float4_e2m1fn_x4
+ACT = mybir.ActivationFunctionType
+ALU = mybir.AluOpType
+
+P = 128
+PACK = 4
+KP = K // 512
+HP = H // 512
+CH = 256
+NCH = S // CH
+SUB = 128
+CHUNKS = [128,128,256,256,256]
+LEAD = 3
+ON_SCALAR = ((2,1,),)
+
+
+def tile_list_armband_gain_sensitivity_kernel(
+    tc, tab_words, tab_scales, wa_words, wa_scales, wb, wgo, offs, offs2, out
+):
+    nc = tc.nc
+    with ExitStack() as ctx:
+        lists = ctx.enter_context(tc.tile_pool(name="lists", bufs=1))
+        keep = ctx.enter_context(tc.tile_pool(name="keep", bufs=1))
+        head = ctx.enter_context(tc.tile_pool(name="head", bufs=1))
+        ring = ctx.enter_context(tc.tile_pool(name="ring", bufs=2))
+        psum = ctx.enter_context(tc.psum_pool(name="psum", bufs=1))
+
+        pick = lists.tile([P, S // 16], U16, name="pick")
+        place = lists.tile([P, S // 16], U16, name="place")
+
+        sc_win = head.tile([P, T], U8, name="sc_win", align_bytes=64, offset=2048)
+        sc_got = keep.tile([P, S], U8, name="sc_got", align_bytes=64)
+        v_plane = [keep.tile([P, S], U8, name=f"v_plane{a}", align_bytes=64) for a in range(KP)]
+        was_raw = head.tile([P, KP, H], U8, name="was_raw", align_bytes=64, offset=22528)
+        warm = keep.tile([P, 1], F32, name="warm", align_bytes=64)
+        warm2 = keep.tile([P, 1], F32, name="warm2", align_bytes=64)
+
+        nc.vector.memset(sc_win[:].bitcast(I32), 0)
+        nc.gpsimd.memset(was_raw[:].rearrange("p a c -> p (a c)").bitcast(I32), 0)
+        nc.vector.memset(warm[:], 0.0)
+        for a in range(KP):
+            nc.gpsimd.memset(v_plane[a][:].bitcast(I32), 0)
+        nc.scalar.activation(warm2[:], warm[:], ACT.Tanh)
+
+        nc.sync.dma_start(pick[:], offs)
+        nc.sync.dma_start(place[:], offs2)
+        tabw = [keep.tile([P, T], I32, name=f"tabw{a}", tag=("warm", "warm2")[a], align_bytes=64) for a in range(KP)]
+        wa_raw = keep.tile([P, KP, H // 2], I32, name="wa_raw", align_bytes=64)
+        nc.sync.dma_start(wa_raw[:], wa_words.bitcast(I32).rearrange("a p c -> p a c"))
+        ts32 = tab_scales.bitcast(I32)
+        win32 = sc_win[:].bitcast(I32)
+        for q in range(4):
+            nc.sync.dma_start(win32[32 * q + 14 : 32 * q + 18, :], ts32[0, 4 * q : 4 * q + 4, :])
+        nc.sync.dma_start(win32[3:P:8, :], ts32[1])
+        for a in range(KP):
+            nc.sync.dma_start(tabw[a][:], tab_words[a].rearrange("p t i -> p (t i)").bitcast(I32))
+        ws32 = wa_scales.bitcast(I32).rearrange("a q c -> q a c")
+        wasr32 = was_raw[:].bitcast(I32)
+        for q in range(4):
+            nc.gpsimd.dma_start(wasr32[32 * q : 32 * q + 4, :, :], ws32[4 * q : 4 * q + 4, :, :])
+
+        pages = [keep.tile([P, T2], F32, name=f"page{i}") for i in range(PACK)]
+        nc.vector.memset(pages[0][:, 0:1023], 0.0)
+        nc.vector.memset(pages[0][:, 1023:], 0.0)
+        for i in range(1, PACK):
+            for lo in range(0, T2, 1024):
+                nc.gpsimd.memset(pages[i][:, lo : lo + 1024], 0.0)
+
+        wb_rows = wb.rearrange("(b q t s) n -> b t q s n", b=HP, q=16, t=PACK)
+
+        nc.vector.tensor_copy(sc_got[:], sc_win[:].indirect(pick[:]))
+        got32 = sc_got[:].bitcast(I32)
+        nc.sync.dma_start(v_plane[0][:].bitcast(I32)[0:112, :], got32[14:126, :])
+        for r in range(4):
+            nc.sync.dma_start(v_plane[1][:].bitcast(I32)[r:P:32, :], got32[8 * r + 3 : P : 32, :])
+
+        late = head.tile([P, S + PACK * N], F32, name="late", align_bytes=64, offset=3072)
+        weight = late[:, 0:S]
+        wb_raw = [late[:, S:].rearrange("p (t n) -> p t n", t=PACK)]
+        nc.sync.dma_start(weight, wgo)
+
+        def load_wb(b):
+            for t in range(PACK):
+                nc.sync.dma_start(wb_raw[b][:, t, :], wb_rows[b, t])
+
+        load_wb(0)
+
+        v_words = [
+            [keep.tile([P, CH], U32, name=f"v_words{a}_{c}", align_bytes=64) for c in range(NCH)] for a in range(KP)
+        ]
+
+        def gather(c):
+            cols = pick[:, c * CH // 16 : (c + 1) * CH // 16]
+            for a in range(KP):
+                nc.vector.tensor_copy(v_words[a][c][:], tabw[a][:].bitcast(U32).indirect(cols))
+
+        wa_codes = [keep.tile([P, KP, 1024], U8, name=f"wa_codes{b}", align_bytes=64) for b in range(HP)]
+        wa_plane = head.tile([P, KP, H], U8, name="wa_plane", align_bytes=64, offset=0)
+        for b in range(HP):
+            nc.vector.tensor_copy(
+                wa_codes[b][:].bitcast(I32).rearrange("p a (t q w) -> p a t q w", t=PACK, q=16),
+                wa_raw[:, :, 256 * b : 256 * (b + 1)].rearrange("p a (q t w) -> p a t q w", t=PACK, q=16),
+            )
+        nc.vector.tensor_copy(
+            wa_plane[:].bitcast(I32).rearrange("p a (b t q w) -> p (a b) t q w", b=HP, t=PACK, q=16),
+            wasr32.rearrange("p a (b q t w) -> p (a b) t q w", b=HP, t=PACK, q=16),
+        )
+
+        for b, at in ((1, 15360), (2, 23552)):
+            rows = head.tile([P, PACK, N], F32, name=f"wb_raw{b}", align_bytes=64, offset=at)
+            wb_raw.append(rows[:])
+            load_wb(b)
+        for c in range(NCH):
+            gather(c)
+
+        wb_codes = [[keep.tile([P, 256], U32, name=f"wb_codes{b}_{u}", align_bytes=64) for u in range(2)] for b in range(HP)]
+        wb_plane = [[keep.tile([P, 256], U8, name=f"wb_plane{b}_{u}", align_bytes=64) for u in range(2)] for b in range(HP)]
+
+        def cast_wb(b, u):
+            rounded = keep.tile([P, 2, P, PACK], BF16, name=f"wb_bf{b}_{u}", align_bytes=64)
+            dst = rounded[:].rearrange("p e m t -> p m t e")
+            src = wb_raw[b].rearrange("p t (m i) -> p m t i", i=PACK)[:, :, :, 2 * u : 2 * u + 2]
+            if (b, u) in ON_SCALAR:
+                nc.scalar.activation(dst, src, ACT.Copy, scale=-1.0)
+            else:
+                nc.vector.tensor_scalar(dst, src, -1.0, None, ALU.mult)
+            return rounded
+
+        def quant_wb(b, u, rounded):
+            nc.vector.quantize_mx(
+                out=wb_codes[b][u][:].bitcast(FP8X4),
+                scales=wb_plane[b][u][:],
+                in_=rounded[:].rearrange("p e m t -> p (e m t)"),
+            )
+
+        starts = [sum(CHUNKS[:c]) for c in range(len(CHUNKS) + 1)]
+        free_banks = [f"bank{n}" for n in range(8)]
+        h_bf = [
+            [keep.tile([P, w, PACK], BF16, name=f"h_bf{b}_{c}", align_bytes=64) for b in range(HP)]
+            for c, w in enumerate(CHUNKS)
+        ]
+        units = [(c, j, b) for c in range(len(CHUNKS)) for j in range(starts[c], starts[c + 1], SUB) for b in range(HP)]
+
+        def first_product(c, j, b):
+            tag = free_banks.pop(0)
+            bank = psum.tile([P, PACK, SUB], F32, name="h_acc", tag=tag)
+            for t in range(PACK):
+                for a in range(KP):
+                    nc.tensor.matmul_mx(
+                        out=bank[:, t, :],
+                        lhsT=wa_codes[b][:, a, 256 * t : 256 * (t + 1)].bitcast(FP4X4),
+                        lhsT_scale=wa_plane[:, a, 512 * b + 128 * t : 512 * b + 128 * (t + 1)],
+                        rhs=v_words[a][j // CH][:, j % CH : j % CH + SUB].bitcast(FP8X4),
+                        rhs_scale=v_plane[a][:, j : j + SUB],
+                        start=(a == 0),
+                        stop=(a == KP - 1),
+                    )
+            j0 = j - starts[c]
+            nc.scalar.activation(h_bf[c][b][:, j0 : j0 + SUB, :], bank[:].rearrange("p t j -> p j t"), ACT.Relu)
+            free_banks.append(tag)
+
+        def quant_h(c):
+            w = CHUNKS[c]
+            tag = f"wb_bf{c + 1}_1" if c + 1 < HP else f"h_codes{c}"
+            codes = keep.tile([P, HP, w], U32, name="h_codes", tag=tag, align_bytes=64)
+            h_codes = [codes[:, b, :] for b in range(HP)]
+            h_plane = [keep.tile([P, w], U8, name=f"h_plane{b}_{c}", align_bytes=64) for b in range(HP)]
+            for b in range(HP):
+                nc.vector.quantize_mx(
+                    out=h_codes[b].bitcast(FP8X4), scales=h_plane[b][:], in_=h_bf[c][b][:].rearrange("p j t -> p (j t)")
+                )
+            return h_codes, h_plane
+
+        def second_product(c, h_q):
+            w = CHUNKS[c]
+            h_codes, h_plane = h_q
+            halves = []
+            for u in range(2):
+                tag = free_banks.pop()
+                neg_q = psum.tile([P, 2, w], F32, name="neg_q", tag=tag)
+                for e in range(2):
+                    for b in range(HP):
+                        nc.tensor.matmul_mx(
+                            out=neg_q[:, e, :],
+                            lhsT=wb_codes[b][u][:, 128 * e : 128 * (e + 1)].bitcast(FP8X4),
+                            lhsT_scale=wb_plane[b][u][:, 128 * e : 128 * (e + 1)],
+                            rhs=h_codes[b].bitcast(FP8X4),
+                            rhs_scale=h_plane[b][:],
+                            start=(b == 0),
+                            stop=(b == HP - 1),
+                        )
+                drive = ring.tile([P, 2, w], F32, name="drive")
+                nc.scalar.activation(drive[:], neg_q[:], ACT.Tanh)
+                square = ring.tile([P, 2, w], F32, name="square", bufs=4)
+                nc.scalar.activation(square[:], drive[:], ACT.Square)
+                halves.append((neg_q, square, tag))
+            return halves
+
+        def slope(c, half, tag):
+            neg_q, square, bank_tag = half
+            y = keep.tile([P, 2, CHUNKS[c]], F32, name="y", tag=tag, align_bytes=64)
+            nc.vector.scalar_tensor_tensor(
+                y[:].rearrange("p e j -> p (e j)"),
+                square[:].rearrange("p e j -> p (e j)"),
+                1.0,
+                neg_q[:].rearrange("p e j -> p (e j)"),
+                ALU.subtract,
+                ALU.mult,
+            )
+            free_banks.append(bank_tag)
+            return y
+
+        def put(c, u, y):
+            lo, hi = starts[c], starts[c + 1]
+            for e in range(2):
+                i = 2 * u + e
+                nc.vector.tensor_tensor(
+                    pages[i][:].indirect(place[:, lo // 16 : hi // 16]), y[:, e, :], weight[:, lo:hi], ALU.mult
+                )
+                if hi == S:
+                    nc.sync.dma_start(out.rearrange("(p i) t -> i p t", i=PACK)[i], pages[i][:])
+
+        def first_product_until(c):
+            goal = min(len(units), starts[c + 1] // SUB * HP + LEAD)
+            while len(units) - len(todo) < goal:
+                first_product(*todo.pop(0))
+
+        todo = list(units)
+        last = len(CHUNKS) - 1
+        first_product_until(0)
+        for b in range(HP):
+            rounded = [cast_wb(b, u) for u in range(2)]
+            for u in range(2):
+                quant_wb(b, u, rounded[u])
+        halves = second_product(0, quant_h(0))
+        for c in range(len(CHUNKS)):
+            if c < last:
+                first_product_until(c + 1)
+                ahead = second_product(c + 1, quant_h(c + 1))
+            y0 = slope(c, halves[0], f"h_bf0_{c}")
+            put(c, 0, y0)
+            put(c, 1, slope(c, halves[1], f"h_bf2_{(c + 1) % len(CHUNKS)}"))
+            halves = ahead

@@ -25,7 +25,7 @@ NCH = S // CH
 SUB = 128
 CHUNKS = [128,128,256,256,256]
 LEAD = 3
-ON_SCALAR = ((2,1,),)
+ON_SCALAR = ((0,1,),(1,1,),(2,1,),)
 
 
 def tile_list_armband_gain_sensitivity_kernel(
@@ -53,7 +53,7 @@ def tile_list_armband_gain_sensitivity_kernel(
         nc.gpsimd.memset(was_raw[:].rearrange("p a c -> p (a c)").bitcast(I32), 0)
         nc.vector.memset(warm[:], 0.0)
         for a in range(KP):
-            nc.gpsimd.memset(v_plane[a][:].bitcast(I32), 0)
+            nc.vector.memset(v_plane[a][:].bitcast(I32), 0)
         nc.scalar.activation(warm2[:], warm[:], ACT.Tanh)
 
         nc.sync.dma_start(pick[:], offs)
@@ -77,8 +77,7 @@ def tile_list_armband_gain_sensitivity_kernel(
         nc.vector.memset(pages[0][:, 0:1023], 0.0)
         nc.vector.memset(pages[0][:, 1023:], 0.0)
         for i in range(1, PACK):
-            for lo in range(0, T2, 1024):
-                nc.gpsimd.memset(pages[i][:, lo : lo + 1024], 0.0)
+            nc.vector.memset(pages[i][:], 0.0)
 
         wb_rows = wb.rearrange("(b q t s) n -> b t q s n", b=HP, q=16, t=PACK)
 
@@ -91,7 +90,7 @@ def tile_list_armband_gain_sensitivity_kernel(
         late = head.tile([P, S + PACK * N], F32, name="late", align_bytes=64, offset=3072)
         weight = late[:, 0:S]
         wb_raw = [late[:, S:].rearrange("p (t n) -> p t n", t=PACK)]
-        nc.sync.dma_start(weight, wgo)
+        nc.scalar.dma_start(weight, wgo)
 
         def load_wb(b):
             for t in range(PACK):
@@ -132,8 +131,8 @@ def tile_list_armband_gain_sensitivity_kernel(
 
         def cast_wb(b, u):
             rounded = keep.tile([P, 2, P, PACK], BF16, name=f"wb_bf{b}_{u}", align_bytes=64)
-            dst = rounded[:].rearrange("p e m t -> p m t e")
-            src = wb_raw[b].rearrange("p t (m i) -> p m t i", i=PACK)[:, :, :, 2 * u : 2 * u + 2]
+            dst = rounded[:].rearrange("p e m t -> p m e t")
+            src = wb_raw[b].rearrange("p t (m i) -> p m i t", i=PACK)[:, :, 2 * u : 2 * u + 2, :]
             if (b, u) in ON_SCALAR:
                 nc.scalar.activation(dst, src, ACT.Copy, scale=-1.0)
             else:
@@ -175,7 +174,7 @@ def tile_list_armband_gain_sensitivity_kernel(
 
         def quant_h(c):
             w = CHUNKS[c]
-            tag = f"wb_bf{c + 1}_1" if c + 1 < HP else f"h_codes{c}"
+            tag = f"wb_bf{c + 1}_{c}" if c + 1 < HP else f"h_codes{c}"
             codes = keep.tile([P, HP, w], U32, name="h_codes", tag=tag, align_bytes=64)
             h_codes = [codes[:, b, :] for b in range(HP)]
             h_plane = [keep.tile([P, w], U8, name=f"h_plane{b}_{c}", align_bytes=64) for b in range(HP)]

@@ -18,14 +18,11 @@ ALU = mybir.AluOpType
 
 P = 128
 PACK = 4
-KP = K // 512
-HP = H // 512
-CH = 256
-NCH = S // CH
+K_PASSES = K // 512
+H_PASSES = H // 512
+BLOCK = 256
 SUB = 128
-CHUNKS = [128,128,256,256,256]
 LEAD = 3
-ON_SCALAR = ((0,1,),(1,1,),(2,1,),)
 
 
 def tile_list_armband_gain_sensitivity_kernel(
@@ -36,50 +33,53 @@ def tile_list_armband_gain_sensitivity_kernel(
         lists = ctx.enter_context(tc.tile_pool(name="lists", bufs=1))
         keep = ctx.enter_context(tc.tile_pool(name="keep", bufs=1))
         head = ctx.enter_context(tc.tile_pool(name="head", bufs=1))
-        ring = ctx.enter_context(tc.tile_pool(name="ring", bufs=2))
         psum = ctx.enter_context(tc.psum_pool(name="psum", bufs=1))
+
+        wa_codes_at = 0
+        sc_win_at = wa_codes_at + K_PASSES * 2 * H - 64
+        wa_plane_at = sc_win_at + 64
+        late_at = wa_plane_at + K_PASSES * H
+        wb1_at = late_at + 4 * (S + PACK * N)
+        wb2_at = wb1_at + 4 * PACK * N
+        wa_raw_at = wb2_at - 64
 
         pick = lists.tile([P, S // 16], U16, name="pick")
         place = lists.tile([P, S // 16], U16, name="place")
 
-        sc_win = head.tile([P, T], U8, name="sc_win", align_bytes=64, offset=2048)
+        sc_win = head.tile([P, 2 * T], U8, name="sc_win", align_bytes=64, offset=sc_win_at)
+        wa_raw = head.tile([P, K_PASSES, H // 2], I32, name="wa_raw", align_bytes=64, offset=wa_raw_at)
         sc_got = keep.tile([P, S], U8, name="sc_got", align_bytes=64)
-        v_plane = [keep.tile([P, S], U8, name=f"v_plane{a}", align_bytes=64) for a in range(KP)]
-        was_raw = head.tile([P, KP, H], U8, name="was_raw", align_bytes=64, offset=22528)
-        warm = keep.tile([P, 1], F32, name="warm", align_bytes=64)
-        warm2 = keep.tile([P, 1], F32, name="warm2", align_bytes=64)
+        v_plane = [keep.tile([P, S], U8, name=f"v_plane{a}", align_bytes=64) for a in range(K_PASSES)]
+        was_raw = keep.tile([P, K_PASSES, H], U8, name="was_raw", align_bytes=64)
+        warm_in = keep.tile([P, 1], F32, name="warm_in", tag="table0", align_bytes=64)
+        warm_out = keep.tile([P, 1], F32, name="warm_out", tag="table1", align_bytes=64)
 
+        nc.vector.memset(warm_in[:], 0.0)
         nc.vector.memset(sc_win[:].bitcast(I32), 0)
         nc.gpsimd.memset(was_raw[:].rearrange("p a c -> p (a c)").bitcast(I32), 0)
-        nc.vector.memset(warm[:], 0.0)
-        for a in range(KP):
-            nc.vector.memset(v_plane[a][:].bitcast(I32), 0)
-        nc.scalar.activation(warm2[:], warm[:], ACT.Tanh)
+        for a in range(K_PASSES):
+            nc.gpsimd.memset(v_plane[a][:].bitcast(I32), 0)
+        nc.scalar.activation(warm_out[:], warm_in[:], ACT.Tanh)
 
         nc.sync.dma_start(pick[:], offs)
         nc.sync.dma_start(place[:], offs2)
-        tabw = [keep.tile([P, T], I32, name=f"tabw{a}", tag=("warm", "warm2")[a], align_bytes=64) for a in range(KP)]
-        wa_raw = keep.tile([P, KP, H // 2], I32, name="wa_raw", align_bytes=64)
         nc.sync.dma_start(wa_raw[:], wa_words.bitcast(I32).rearrange("a p c -> p a c"))
-        ts32 = tab_scales.bitcast(I32)
-        win32 = sc_win[:].bitcast(I32)
+        tab_rows = tab_scales.bitcast(I32)
+        win32 = sc_win[:].bitcast(I32)[:, 0 : T // 4]
         for q in range(4):
-            nc.sync.dma_start(win32[32 * q + 14 : 32 * q + 18, :], ts32[0, 4 * q : 4 * q + 4, :])
-        nc.sync.dma_start(win32[3:P:8, :], ts32[1])
-        for a in range(KP):
-            nc.sync.dma_start(tabw[a][:], tab_words[a].rearrange("p t i -> p (t i)").bitcast(I32))
-        ws32 = wa_scales.bitcast(I32).rearrange("a q c -> q a c")
-        wasr32 = was_raw[:].bitcast(I32)
+            nc.sync.dma_start(win32[32 * q + 14 : 32 * q + 18, :], tab_rows[0, 4 * q : 4 * q + 4, :])
+        nc.sync.dma_start(win32[3:P:8, :], tab_rows[1])
+        table = [keep.tile([P, T], I32, name="table", tag=f"table{a}", align_bytes=64) for a in range(K_PASSES)]
+        for a in range(K_PASSES):
+            nc.sync.dma_start(table[a][:], tab_words[a].rearrange("p t i -> p (t i)").bitcast(I32))
+        wa_rows = wa_scales.bitcast(I32).rearrange("a q c -> q a c")
+        was32 = was_raw[:].bitcast(I32)
         for q in range(4):
-            nc.gpsimd.dma_start(wasr32[32 * q : 32 * q + 4, :, :], ws32[4 * q : 4 * q + 4, :, :])
+            nc.gpsimd.dma_start(was32[32 * q : 32 * q + 4, :, :], wa_rows[4 * q : 4 * q + 4, :, :])
 
-        pages = [keep.tile([P, T2], F32, name=f"page{i}") for i in range(PACK)]
+        pages = [keep.tile([P, T2], F32, name="page0")]
         nc.vector.memset(pages[0][:, 0:1023], 0.0)
         nc.vector.memset(pages[0][:, 1023:], 0.0)
-        for i in range(1, PACK):
-            nc.vector.memset(pages[i][:], 0.0)
-
-        wb_rows = wb.rearrange("(b q t s) n -> b t q s n", b=HP, q=16, t=PACK)
 
         nc.vector.tensor_copy(sc_got[:], sc_win[:].indirect(pick[:]))
         got32 = sc_got[:].bitcast(I32)
@@ -87,10 +87,11 @@ def tile_list_armband_gain_sensitivity_kernel(
         for r in range(4):
             nc.sync.dma_start(v_plane[1][:].bitcast(I32)[r:P:32, :], got32[8 * r + 3 : P : 32, :])
 
-        late = head.tile([P, S + PACK * N], F32, name="late", align_bytes=64, offset=3072)
+        late = head.tile([P, S + PACK * N], F32, name="late", align_bytes=64, offset=late_at)
         weight = late[:, 0:S]
+        nc.sync.dma_start(weight, wgo)
+        wb_rows = wb.rearrange("(b q t s) n -> b t q s n", b=H_PASSES, q=16, t=PACK)
         wb_raw = [late[:, S:].rearrange("p (t n) -> p t n", t=PACK)]
-        nc.scalar.dma_start(weight, wgo)
 
         def load_wb(b):
             for t in range(PACK):
@@ -98,120 +99,121 @@ def tile_list_armband_gain_sensitivity_kernel(
 
         load_wb(0)
 
-        v_words = [
-            [keep.tile([P, CH], U32, name=f"v_words{a}_{c}", align_bytes=64) for c in range(NCH)] for a in range(KP)
-        ]
-
-        def gather(c):
-            cols = pick[:, c * CH // 16 : (c + 1) * CH // 16]
-            for a in range(KP):
-                nc.vector.tensor_copy(v_words[a][c][:], tabw[a][:].bitcast(U32).indirect(cols))
-
-        wa_codes = [keep.tile([P, KP, 1024], U8, name=f"wa_codes{b}", align_bytes=64) for b in range(HP)]
-        wa_plane = head.tile([P, KP, H], U8, name="wa_plane", align_bytes=64, offset=0)
-        for b in range(HP):
+        wa_codes = head.tile([P, K_PASSES, 2 * H], U8, name="wa_codes", align_bytes=64, offset=wa_codes_at)
+        wa_plane = head.tile([P, K_PASSES, H], U8, name="wa_plane", align_bytes=64, offset=wa_plane_at)
+        for dst, src in ((wa_codes, wa_raw[:]), (wa_plane, was32)):
             nc.vector.tensor_copy(
-                wa_codes[b][:].bitcast(I32).rearrange("p a (t q w) -> p a t q w", t=PACK, q=16),
-                wa_raw[:, :, 256 * b : 256 * (b + 1)].rearrange("p a (q t w) -> p a t q w", t=PACK, q=16),
+                dst[:].bitcast(I32).rearrange("p a (b t q w) -> p (a b) t q w", b=H_PASSES, t=PACK, q=16),
+                src.rearrange("p a (b q t w) -> p (a b) t q w", b=H_PASSES, t=PACK, q=16),
             )
-        nc.vector.tensor_copy(
-            wa_plane[:].bitcast(I32).rearrange("p a (b t q w) -> p (a b) t q w", b=HP, t=PACK, q=16),
-            wasr32.rearrange("p a (b q t w) -> p (a b) t q w", b=HP, t=PACK, q=16),
-        )
-
-        for b, at in ((1, 15360), (2, 23552)):
+        for b, at in ((1, wb1_at), (2, wb2_at)):
             rows = head.tile([P, PACK, N], F32, name=f"wb_raw{b}", align_bytes=64, offset=at)
             wb_raw.append(rows[:])
             load_wb(b)
-        for c in range(NCH):
-            gather(c)
 
-        wb_codes = [[keep.tile([P, 256], U32, name=f"wb_codes{b}_{u}", align_bytes=64) for u in range(2)] for b in range(HP)]
-        wb_plane = [[keep.tile([P, 256], U8, name=f"wb_plane{b}_{u}", align_bytes=64) for u in range(2)] for b in range(HP)]
+        v_words = {}
+        for lo, hi in ((0, BLOCK), (BLOCK, S)):
+            for a in range(K_PASSES):
+                tag = "sc_got" if (lo, a) == (BLOCK, 0) else f"v_words{a}_{lo}"
+                v_words[lo, a] = keep.tile([P, hi - lo], U32, name="v_words", tag=tag, align_bytes=64)
+                nc.vector.tensor_copy(v_words[lo, a][:], table[a][:].bitcast(U32).indirect(pick[:, lo // 16 : hi // 16]))
 
-        def cast_wb(b, u):
-            rounded = keep.tile([P, 2, P, PACK], BF16, name=f"wb_bf{b}_{u}", align_bytes=64)
-            dst = rounded[:].rearrange("p e m t -> p m e t")
-            src = wb_raw[b].rearrange("p t (m i) -> p m i t", i=PACK)[:, :, 2 * u : 2 * u + 2, :]
-            if (b, u) in ON_SCALAR:
-                nc.scalar.activation(dst, src, ACT.Copy, scale=-1.0)
-            else:
-                nc.vector.tensor_scalar(dst, src, -1.0, None, ALU.mult)
-            return rounded
+        pages.append(keep.tile([P, T2], F32, name="page1", tag="table0", align_bytes=64))
+        nc.vector.memset(pages[1][:], 0.0)
 
-        def quant_wb(b, u, rounded):
-            nc.vector.quantize_mx(
-                out=wb_codes[b][u][:].bitcast(FP8X4),
-                scales=wb_plane[b][u][:],
-                in_=rounded[:].rearrange("p e m t -> p (e m t)"),
-            )
-
-        starts = [sum(CHUNKS[:c]) for c in range(len(CHUNKS) + 1)]
+        pieces = [(0, SUB), (SUB, BLOCK)] + [(lo, lo + BLOCK) for lo in range(BLOCK, S, BLOCK)]
+        h_bf = {
+            lo: [keep.tile([P, hi - lo, PACK], BF16, name=f"h_bf{b}_{lo}", align_bytes=64) for b in range(H_PASSES)]
+            for lo, hi in pieces
+        }
+        todo = [(lo, j, b) for lo, hi in pieces for j in range(lo, hi, SUB) for b in range(H_PASSES)]
+        n_units = len(todo)
         free_banks = [f"bank{n}" for n in range(8)]
-        h_bf = [
-            [keep.tile([P, w, PACK], BF16, name=f"h_bf{b}_{c}", align_bytes=64) for b in range(HP)]
-            for c, w in enumerate(CHUNKS)
-        ]
-        units = [(c, j, b) for c in range(len(CHUNKS)) for j in range(starts[c], starts[c + 1], SUB) for b in range(HP)]
 
-        def first_product(c, j, b):
+        def first_product(lo, j, b):
             tag = free_banks.pop(0)
-            bank = psum.tile([P, PACK, SUB], F32, name="h_acc", tag=tag)
+            acc = psum.tile([P, PACK, SUB], F32, name="acc", tag=tag)
+            base = 0 if j < BLOCK else BLOCK
             for t in range(PACK):
-                for a in range(KP):
+                col = 512 * b + P * t
+                for a in range(K_PASSES):
                     nc.tensor.matmul_mx(
-                        out=bank[:, t, :],
-                        lhsT=wa_codes[b][:, a, 256 * t : 256 * (t + 1)].bitcast(FP4X4),
-                        lhsT_scale=wa_plane[:, a, 512 * b + 128 * t : 512 * b + 128 * (t + 1)],
-                        rhs=v_words[a][j // CH][:, j % CH : j % CH + SUB].bitcast(FP8X4),
+                        out=acc[:, t, :],
+                        lhsT=wa_codes[:, a, 2 * col : 2 * (col + P)].bitcast(FP4X4),
+                        lhsT_scale=wa_plane[:, a, col : col + P],
+                        rhs=v_words[base, a][:, j - base : j - base + SUB].bitcast(FP8X4),
                         rhs_scale=v_plane[a][:, j : j + SUB],
                         start=(a == 0),
-                        stop=(a == KP - 1),
+                        stop=(a == K_PASSES - 1),
                     )
-            j0 = j - starts[c]
-            nc.scalar.activation(h_bf[c][b][:, j0 : j0 + SUB, :], bank[:].rearrange("p t j -> p j t"), ACT.Relu)
+            nc.scalar.activation(h_bf[lo][b][:, j - lo : j - lo + SUB, :], acc[:].rearrange("p t j -> p j t"), ACT.Relu)
             free_banks.append(tag)
 
-        def quant_h(c):
-            w = CHUNKS[c]
-            tag = f"wb_bf{c + 1}_{c}" if c + 1 < HP else f"h_codes{c}"
-            codes = keep.tile([P, HP, w], U32, name="h_codes", tag=tag, align_bytes=64)
-            h_codes = [codes[:, b, :] for b in range(HP)]
-            h_plane = [keep.tile([P, w], U8, name=f"h_plane{b}_{c}", align_bytes=64) for b in range(HP)]
-            for b in range(HP):
-                nc.vector.quantize_mx(
-                    out=h_codes[b].bitcast(FP8X4), scales=h_plane[b][:], in_=h_bf[c][b][:].rearrange("p j t -> p (j t)")
-                )
-            return h_codes, h_plane
+        def first_product_through(column, lead):
+            goal = min(n_units, column // SUB * H_PASSES + lead)
+            while n_units - len(todo) < goal:
+                first_product(*todo.pop(0))
 
-        def second_product(c, h_q):
-            w = CHUNKS[c]
-            h_codes, h_plane = h_q
-            halves = []
+        wb_codes, wb_plane = {}, {}
+
+        def quantise_wb(b):
+            rounded = []
             for u in range(2):
-                tag = free_banks.pop()
-                neg_q = psum.tile([P, 2, w], F32, name="neg_q", tag=tag)
-                for e in range(2):
-                    for b in range(HP):
-                        nc.tensor.matmul_mx(
-                            out=neg_q[:, e, :],
-                            lhsT=wb_codes[b][u][:, 128 * e : 128 * (e + 1)].bitcast(FP8X4),
-                            lhsT_scale=wb_plane[b][u][:, 128 * e : 128 * (e + 1)],
-                            rhs=h_codes[b].bitcast(FP8X4),
-                            rhs_scale=h_plane[b][:],
-                            start=(b == 0),
-                            stop=(b == HP - 1),
-                        )
-                drive = ring.tile([P, 2, w], F32, name="drive")
-                nc.scalar.activation(drive[:], neg_q[:], ACT.Tanh)
-                square = ring.tile([P, 2, w], F32, name="square", bufs=4)
-                nc.scalar.activation(square[:], drive[:], ACT.Square)
-                halves.append((neg_q, square, tag))
-            return halves
+                half = keep.tile([P, 2, P, PACK], BF16, name=f"wb_bf{b}_{u}", align_bytes=64)
+                dst = half[:].rearrange("p e m t -> p m e t")
+                src = wb_raw[b].rearrange("p t (m i) -> p m i t", i=PACK)[:, :, 2 * u : 2 * u + 2, :]
+                if u == 0:
+                    nc.vector.tensor_scalar(dst, src, -1.0, None, ALU.mult)
+                else:
+                    nc.scalar.activation(dst, src, ACT.Copy, scale=-1.0)
+                rounded.append(half)
+            for u in range(2):
+                wb_codes[b, u] = keep.tile([P, 2 * P], U32, name=f"wb_codes{b}_{u}", align_bytes=64)
+                wb_plane[b, u] = keep.tile([P, 2 * P], U8, name=f"wb_plane{b}_{u}", align_bytes=64)
+                nc.vector.quantize_mx(
+                    out=wb_codes[b, u][:].bitcast(FP8X4),
+                    scales=wb_plane[b, u][:],
+                    in_=rounded[u][:].rearrange("p e m t -> p (e m t)"),
+                )
 
-        def slope(c, half, tag):
-            neg_q, square, bank_tag = half
-            y = keep.tile([P, 2, CHUNKS[c]], F32, name="y", tag=tag, align_bytes=64)
+        h_codes, h_plane = {}, {}
+
+        def quantise_h(lo, hi, tag):
+            h_codes[lo] = keep.tile([P, H_PASSES, hi - lo], U32, name="h_codes", tag=tag, align_bytes=64)
+            h_plane[lo] = keep.tile([P, H_PASSES, hi - lo], U8, name=f"h_plane{lo}", align_bytes=64)
+            for b in range(H_PASSES):
+                nc.vector.quantize_mx(
+                    out=h_codes[lo][:, b, :].bitcast(FP8X4),
+                    scales=h_plane[lo][:, b, :],
+                    in_=h_bf[lo][b][:].rearrange("p j t -> p (j t)"),
+                )
+
+        def second_product(lo, hi, tiles):
+            tag = free_banks.pop()
+            neg_q = psum.tile([P, len(tiles), hi - lo], F32, name="neg_q", tag=tag)
+            for n, i in enumerate(tiles):
+                u, e = divmod(i, 2)
+                for at, end in pieces:
+                    if lo <= at and end <= hi:
+                        for b in range(H_PASSES):
+                            nc.tensor.matmul_mx(
+                                out=neg_q[:, n, at - lo : end - lo],
+                                lhsT=wb_codes[b, u][:, P * e : P * (e + 1)].bitcast(FP8X4),
+                                lhsT_scale=wb_plane[b, u][:, P * e : P * (e + 1)],
+                                rhs=h_codes[at][:, b, :].bitcast(FP8X4),
+                                rhs_scale=h_plane[at][:, b, :],
+                                start=(b == 0),
+                                stop=(b == H_PASSES - 1),
+                            )
+            drive = keep.tile([P, len(tiles), hi - lo], F32, name=f"drive{lo}_{tiles[0]}", align_bytes=64)
+            nc.scalar.activation(drive[:], neg_q[:], ACT.Tanh)
+            square = keep.tile([P, len(tiles), hi - lo], F32, name=f"square{lo}_{tiles[0]}", align_bytes=64)
+            nc.scalar.activation(square[:], drive[:], ACT.Square)
+            return lo, hi, tiles, neg_q, square, tag
+
+        def slope(step, tag):
+            lo, hi, tiles, neg_q, square, bank = step
+            y = keep.tile([P, len(tiles), hi - lo], F32, name="y", tag=tag, align_bytes=64)
             nc.vector.scalar_tensor_tensor(
                 y[:].rearrange("p e j -> p (e j)"),
                 square[:].rearrange("p e j -> p (e j)"),
@@ -220,37 +222,47 @@ def tile_list_armband_gain_sensitivity_kernel(
                 ALU.subtract,
                 ALU.mult,
             )
-            free_banks.append(bank_tag)
-            return y
+            free_banks.append(bank)
+            return lo, hi, tiles, y
 
-        def put(c, u, y):
-            lo, hi = starts[c], starts[c + 1]
-            for e in range(2):
-                i = 2 * u + e
+        def put(lo, hi, tiles, y):
+            for n, i in enumerate(tiles):
                 nc.vector.tensor_tensor(
-                    pages[i][:].indirect(place[:, lo // 16 : hi // 16]), y[:, e, :], weight[:, lo:hi], ALU.mult
+                    pages[i][:].indirect(place[:, lo // 16 : hi // 16]), y[:, n, :], weight[:, lo:hi], ALU.mult
                 )
                 if hi == S:
                     nc.sync.dma_start(out.rearrange("(p i) t -> i p t", i=PACK)[i], pages[i][:])
 
-        def first_product_until(c):
-            goal = min(len(units), starts[c + 1] // SUB * HP + LEAD)
-            while len(units) - len(todo) < goal:
-                first_product(*todo.pop(0))
+        def next_block(lo):
+            first_product_through(lo + BLOCK, 0)
+            quantise_h(lo, lo + BLOCK, f"h_codes{lo}")
+            first_product_through(lo + BLOCK, LEAD)
 
-        todo = list(units)
-        last = len(CHUNKS) - 1
-        first_product_until(0)
-        for b in range(HP):
-            rounded = [cast_wb(b, u) for u in range(2)]
-            for u in range(2):
-                quant_wb(b, u, rounded[u])
-        halves = second_product(0, quant_h(0))
-        for c in range(len(CHUNKS)):
-            if c < last:
-                first_product_until(c + 1)
-                ahead = second_product(c + 1, quant_h(c + 1))
-            y0 = slope(c, halves[0], f"h_bf0_{c}")
-            put(c, 0, y0)
-            put(c, 1, slope(c, halves[1], f"h_bf2_{(c + 1) % len(CHUNKS)}"))
-            halves = ahead
+        low, high = (0, 1), (2, 3)
+        first_product_through(BLOCK, 0)
+        for b in range(H_PASSES):
+            quantise_wb(b)
+        quantise_h(0, SUB, "wb_bf1_0")
+        quantise_h(SUB, BLOCK, "wb_bf2_0")
+        opening = [second_product(0, SUB, low), second_product(SUB, BLOCK, low)]
+        step = second_product(0, BLOCK, high)
+        sloped = [slope(first, f"h_bf0_{first[0]}") for first in opening]
+        for i, tag in ((2, "drive0_0"), (3, "square0_0")):
+            pages.append(keep.tile([P, T2], F32, name="page", tag=tag, align_bytes=64))
+            for lo in range(0, T2, T2 // 2):
+                nc.gpsimd.memset(pages[i][:, lo : lo + T2 // 2], 0.0)
+        for first in sloped:
+            put(*first)
+
+        next_block(BLOCK)
+        ahead = [second_product(BLOCK, 2 * BLOCK, tiles) for tiles in (low, high)]
+        put(*slope(step, f"h_bf2_{BLOCK}"))
+        put(*slope(ahead[0], f"h_bf0_{BLOCK}"))
+        next_block(2 * BLOCK)
+        step = second_product(2 * BLOCK, 3 * BLOCK, low)
+        put(*slope(ahead[1], f"h_bf2_{2 * BLOCK}"))
+        next_block(3 * BLOCK)
+        ahead = [second_product(3 * BLOCK, S, low)] + [second_product(2 * BLOCK, S, (i,)) for i in high]
+        put(*slope(step, f"h_bf2_{3 * BLOCK}"))
+        for b, step in enumerate(ahead):
+            put(*slope(step, f"h_bf{b % 2}_{(2 + b // 2) * BLOCK}"))

@@ -22,7 +22,7 @@ K_PASSES = K // 512
 H_PASSES = H // 512
 BLOCK = 256
 SUB = 128
-LEAD = 3
+FIRST_BANKS = 4
 
 
 def tile_list_armband_gain_sensitivity_kernel(
@@ -32,237 +32,195 @@ def tile_list_armband_gain_sensitivity_kernel(
     with ExitStack() as ctx:
         lists = ctx.enter_context(tc.tile_pool(name="lists", bufs=1))
         keep = ctx.enter_context(tc.tile_pool(name="keep", bufs=1))
-        head = ctx.enter_context(tc.tile_pool(name="head", bufs=1))
         psum = ctx.enter_context(tc.psum_pool(name="psum", bufs=1))
 
-        wa_codes_at = 0
-        sc_win_at = wa_codes_at + K_PASSES * 2 * H - 64
-        wa_plane_at = sc_win_at + 64
-        late_at = wa_plane_at + K_PASSES * H
-        wb1_at = late_at + 4 * (S + PACK * N)
-        wb2_at = wb1_at + 4 * PACK * N
-        wa_raw_at = wb2_at - 64
+        def sb(shape, dtype, name, tag=None):
+            return keep.tile(shape, dtype, name=name, tag=tag or name, align_bytes=64)
 
         pick = lists.tile([P, S // 16], U16, name="pick")
         place = lists.tile([P, S // 16], U16, name="place")
 
-        sc_win = head.tile([P, 2 * T], U8, name="sc_win", align_bytes=64, offset=sc_win_at)
-        wa_raw = head.tile([P, K_PASSES, H // 2], I32, name="wa_raw", align_bytes=64, offset=wa_raw_at)
-        sc_got = keep.tile([P, S], U8, name="sc_got", align_bytes=64)
-        v_plane = [keep.tile([P, S], U8, name=f"v_plane{a}", align_bytes=64) for a in range(K_PASSES)]
-        was_raw = keep.tile([P, K_PASSES, H], U8, name="was_raw", align_bytes=64)
-        warm_in = keep.tile([P, 1], F32, name="warm_in", tag="table0", align_bytes=64)
-        warm_out = keep.tile([P, 1], F32, name="warm_out", tag="table1", align_bytes=64)
+        sc_win = sb([P, T], U8, "sc_win")
+        wa_raw = sb([P, K_PASSES, H // 2], I32, "wa_raw")
+        was_raw = sb([P, K_PASSES, H], U8, "was_raw")
+        sc_got = sb([P, S], U8, "sc_got")
+        v_plane = [sb([P, S], U8, f"v_plane{a}") for a in range(K_PASSES)]
+        warm_in = sb([P, 1], F32, "warm_in", "table0")
+        warm_out = sb([P, 1], F32, "warm_out", "table1")
 
-        nc.vector.memset(warm_in[:], 0.0)
         nc.vector.memset(sc_win[:].bitcast(I32), 0)
-        nc.gpsimd.memset(was_raw[:].rearrange("p a c -> p (a c)").bitcast(I32), 0)
+        nc.vector.memset(warm_in[:], 0.0)
+        nc.vector.memset(was_raw[:].rearrange("p a c -> p (a c)").bitcast(I32), 0)
         for a in range(K_PASSES):
-            nc.gpsimd.memset(v_plane[a][:].bitcast(I32), 0)
+            nc.vector.memset(v_plane[a][:].bitcast(I32), 0)
         nc.scalar.activation(warm_out[:], warm_in[:], ACT.Tanh)
 
         nc.sync.dma_start(pick[:], offs)
         nc.sync.dma_start(place[:], offs2)
         nc.sync.dma_start(wa_raw[:], wa_words.bitcast(I32).rearrange("a p c -> p a c"))
         tab_rows = tab_scales.bitcast(I32)
-        win32 = sc_win[:].bitcast(I32)[:, 0 : T // 4]
+        win32 = sc_win[:].bitcast(I32)
         for q in range(4):
             nc.sync.dma_start(win32[32 * q + 14 : 32 * q + 18, :], tab_rows[0, 4 * q : 4 * q + 4, :])
         nc.sync.dma_start(win32[3:P:8, :], tab_rows[1])
-        table = [keep.tile([P, T], I32, name="table", tag=f"table{a}", align_bytes=64) for a in range(K_PASSES)]
+        table = [sb([P, T], I32, "table", f"table{a}") for a in range(K_PASSES)]
         for a in range(K_PASSES):
             nc.sync.dma_start(table[a][:], tab_words[a].rearrange("p t i -> p (t i)").bitcast(I32))
         wa_rows = wa_scales.bitcast(I32).rearrange("a q c -> q a c")
         was32 = was_raw[:].bitcast(I32)
         for q in range(4):
-            nc.gpsimd.dma_start(was32[32 * q : 32 * q + 4, :, :], wa_rows[4 * q : 4 * q + 4, :, :])
+            nc.scalar.dma_start(was32[32 * q : 32 * q + 4, :, :], wa_rows[4 * q : 4 * q + 4, :, :])
 
-        pages = [keep.tile([P, T2], F32, name="page0")]
-        nc.vector.memset(pages[0][:, 0:1023], 0.0)
-        nc.vector.memset(pages[0][:, 1023:], 0.0)
+        pages = {}
+
+        def clear_page(i, tag):
+            pages[i] = sb([P, T2], F32, "page", tag)
+            nc.vector.memset(pages[i][:], 0.0)
+
+        clear_page(0, "page0")
+        clear_page(1, "page1")
 
         nc.vector.tensor_copy(sc_got[:], sc_win[:].indirect(pick[:]))
         got32 = sc_got[:].bitcast(I32)
-        nc.sync.dma_start(v_plane[0][:].bitcast(I32)[0:112, :], got32[14:126, :])
         for r in range(4):
             nc.sync.dma_start(v_plane[1][:].bitcast(I32)[r:P:32, :], got32[8 * r + 3 : P : 32, :])
+        nc.sync.dma_start(v_plane[0][:].bitcast(I32)[0:112, :], got32[14:126, :])
 
-        late = head.tile([P, S + PACK * N], F32, name="late", align_bytes=64, offset=late_at)
-        weight = late[:, 0:S]
-        nc.sync.dma_start(weight, wgo)
-        wb_rows = wb.rearrange("(b q t s) n -> b t q s n", b=H_PASSES, q=16, t=PACK)
-        wb_raw = [late[:, S:].rearrange("p (t n) -> p t n", t=PACK)]
-
-        def load_wb(b):
-            for t in range(PACK):
-                nc.sync.dma_start(wb_raw[b][:, t, :], wb_rows[b, t])
-
-        load_wb(0)
-
-        wa_codes = head.tile([P, K_PASSES, 2 * H], U8, name="wa_codes", align_bytes=64, offset=wa_codes_at)
-        wa_plane = head.tile([P, K_PASSES, H], U8, name="wa_plane", align_bytes=64, offset=wa_plane_at)
+        wa_codes = sb([P, K_PASSES, 2 * H], U8, "wa_codes")
+        wa_plane = sb([P, K_PASSES, H], U8, "wa_plane")
         for dst, src in ((wa_codes, wa_raw[:]), (wa_plane, was32)):
             nc.vector.tensor_copy(
                 dst[:].bitcast(I32).rearrange("p a (b t q w) -> p (a b) t q w", b=H_PASSES, t=PACK, q=16),
                 src.rearrange("p a (b q t w) -> p (a b) t q w", b=H_PASSES, t=PACK, q=16),
             )
-        for b, at in ((1, wb1_at), (2, wb2_at)):
-            rows = head.tile([P, PACK, N], F32, name=f"wb_raw{b}", align_bytes=64, offset=at)
-            wb_raw.append(rows[:])
-            load_wb(b)
+
+        wb_rows = wb.rearrange("(b q t s) n -> b t q s n", b=H_PASSES, q=16, t=PACK)
+        wb_raw = []
+        for b, tag in enumerate(("sc_win", "wa_raw", "was_raw")):
+            wb_raw.append(sb([P, PACK, N], F32, "wb_raw", tag))
+            for t in range(PACK):
+                nc.sync.dma_start(wb_raw[b][:, t, :], wb_rows[b, t])
+        weight = sb([P, S], F32, "weight", "sc_got")
+        nc.sync.dma_start(weight[:], wgo)
 
         v_words = {}
-        for lo, hi in ((0, BLOCK), (BLOCK, S)):
-            for a in range(K_PASSES):
-                tag = "sc_got" if (lo, a) == (BLOCK, 0) else f"v_words{a}_{lo}"
-                v_words[lo, a] = keep.tile([P, hi - lo], U32, name="v_words", tag=tag, align_bytes=64)
-                nc.vector.tensor_copy(v_words[lo, a][:], table[a][:].bitcast(U32).indirect(pick[:, lo // 16 : hi // 16]))
+        for a, lo, hi in ((0, 0, S), (1, 0, BLOCK), (1, BLOCK, S)):
+            got = sb([P, hi - lo], U32, f"v_words{a}_{lo}")
+            nc.vector.tensor_copy(got[:], table[a][:].bitcast(U32).indirect(pick[:, lo // 16 : hi // 16]))
+            for j in range(lo, hi, SUB):
+                v_words[a, j] = got[:, j - lo : j - lo + SUB]
 
-        pages.append(keep.tile([P, T2], F32, name="page1", tag="table0", align_bytes=64))
-        nc.vector.memset(pages[1][:], 0.0)
+        h_codes, h_plane = {}, {}
+        units = []
 
-        pieces = [(0, SUB), (SUB, BLOCK)] + [(lo, lo + BLOCK) for lo in range(BLOCK, S, BLOCK)]
-        h_bf = {
-            lo: [keep.tile([P, hi - lo, PACK], BF16, name=f"h_bf{b}_{lo}", align_bytes=64) for b in range(H_PASSES)]
-            for lo, hi in pieces
-        }
-        todo = [(lo, j, b) for lo, hi in pieces for j in range(lo, hi, SUB) for b in range(H_PASSES)]
-        n_units = len(todo)
-        free_banks = [f"bank{n}" for n in range(8)]
-
-        def first_product(lo, j, b):
-            tag = free_banks.pop(0)
-            acc = psum.tile([P, PACK, SUB], F32, name="acc", tag=tag)
-            base = 0 if j < BLOCK else BLOCK
-            for t in range(PACK):
-                col = 512 * b + P * t
-                for a in range(K_PASSES):
-                    nc.tensor.matmul_mx(
-                        out=acc[:, t, :],
-                        lhsT=wa_codes[:, a, 2 * col : 2 * (col + P)].bitcast(FP4X4),
-                        lhsT_scale=wa_plane[:, a, col : col + P],
-                        rhs=v_words[base, a][:, j - base : j - base + SUB].bitcast(FP8X4),
-                        rhs_scale=v_plane[a][:, j : j + SUB],
-                        start=(a == 0),
-                        stop=(a == K_PASSES - 1),
-                    )
-            nc.scalar.activation(h_bf[lo][b][:, j - lo : j - lo + SUB, :], acc[:].rearrange("p t j -> p j t"), ACT.Relu)
-            free_banks.append(tag)
-
-        def first_product_through(column, lead):
-            goal = min(n_units, column // SUB * H_PASSES + lead)
-            while n_units - len(todo) < goal:
-                first_product(*todo.pop(0))
+        def first_product(k):
+            lo = k * BLOCK
+            h_codes[k] = sb([P, H_PASSES, BLOCK], U32, f"h_codes{k}")
+            h_plane[k] = sb([P, H_PASSES, BLOCK], U8, f"h_plane{k}")
+            for b in range(H_PASSES):
+                h_bf = sb([P, BLOCK, PACK], BF16, f"h_bf{k}_{b}")
+                for j in range(lo, lo + BLOCK, SUB):
+                    acc = psum.tile([P, PACK, SUB], F32, name="acc", tag=f"bank{len(units) % FIRST_BANKS}")
+                    units.append(j)
+                    for t in range(PACK):
+                        col = 512 * b + P * t
+                        for a in range(K_PASSES):
+                            nc.tensor.matmul_mx(
+                                out=acc[:, t, :],
+                                lhsT=wa_codes[:, a, 2 * col : 2 * (col + P)].bitcast(FP4X4),
+                                lhsT_scale=wa_plane[:, a, col : col + P],
+                                rhs=v_words[a, j].bitcast(FP8X4),
+                                rhs_scale=v_plane[a][:, j : j + SUB],
+                                start=(a == 0),
+                                stop=(a == K_PASSES - 1),
+                            )
+                    nc.scalar.activation(h_bf[:, j - lo : j - lo + SUB, :], acc[:].rearrange("p t j -> p j t"), ACT.Relu)
+                nc.vector.quantize_mx(
+                    out=h_codes[k][:, b, :].bitcast(FP8X4),
+                    scales=h_plane[k][:, b, :],
+                    in_=h_bf[:].rearrange("p j t -> p (j t)"),
+                )
 
         wb_codes, wb_plane = {}, {}
 
-        def quantise_wb(b):
-            rounded = []
-            for u in range(2):
-                half = keep.tile([P, 2, P, PACK], BF16, name=f"wb_bf{b}_{u}", align_bytes=64)
-                dst = half[:].rearrange("p e m t -> p m e t")
-                src = wb_raw[b].rearrange("p t (m i) -> p m i t", i=PACK)[:, :, 2 * u : 2 * u + 2, :]
-                if u == 0:
-                    nc.vector.tensor_scalar(dst, src, -1.0, None, ALU.mult)
-                else:
-                    nc.scalar.activation(dst, src, ACT.Copy, scale=-1.0)
-                rounded.append(half)
-            for u in range(2):
-                wb_codes[b, u] = keep.tile([P, 2 * P], U32, name=f"wb_codes{b}_{u}", align_bytes=64)
-                wb_plane[b, u] = keep.tile([P, 2 * P], U8, name=f"wb_plane{b}_{u}", align_bytes=64)
-                nc.vector.quantize_mx(
-                    out=wb_codes[b, u][:].bitcast(FP8X4),
-                    scales=wb_plane[b, u][:],
-                    in_=rounded[u][:].rearrange("p e m t -> p (e m t)"),
-                )
-
-        h_codes, h_plane = {}, {}
-
-        def quantise_h(lo, hi, tag):
-            h_codes[lo] = keep.tile([P, H_PASSES, hi - lo], U32, name="h_codes", tag=tag, align_bytes=64)
-            h_plane[lo] = keep.tile([P, H_PASSES, hi - lo], U8, name=f"h_plane{lo}", align_bytes=64)
-            for b in range(H_PASSES):
-                nc.vector.quantize_mx(
-                    out=h_codes[lo][:, b, :].bitcast(FP8X4),
-                    scales=h_plane[lo][:, b, :],
-                    in_=h_bf[lo][b][:].rearrange("p j t -> p (j t)"),
-                )
-
-        def second_product(lo, hi, tiles):
-            tag = free_banks.pop()
-            neg_q = psum.tile([P, len(tiles), hi - lo], F32, name="neg_q", tag=tag)
-            for n, i in enumerate(tiles):
-                u, e = divmod(i, 2)
-                for at, end in pieces:
-                    if lo <= at and end <= hi:
-                        for b in range(H_PASSES):
-                            nc.tensor.matmul_mx(
-                                out=neg_q[:, n, at - lo : end - lo],
-                                lhsT=wb_codes[b, u][:, P * e : P * (e + 1)].bitcast(FP8X4),
-                                lhsT_scale=wb_plane[b, u][:, P * e : P * (e + 1)],
-                                rhs=h_codes[at][:, b, :].bitcast(FP8X4),
-                                rhs_scale=h_plane[at][:, b, :],
-                                start=(b == 0),
-                                stop=(b == H_PASSES - 1),
-                            )
-            drive = keep.tile([P, len(tiles), hi - lo], F32, name=f"drive{lo}_{tiles[0]}", align_bytes=64)
-            nc.scalar.activation(drive[:], neg_q[:], ACT.Tanh)
-            square = keep.tile([P, len(tiles), hi - lo], F32, name=f"square{lo}_{tiles[0]}", align_bytes=64)
-            nc.scalar.activation(square[:], drive[:], ACT.Square)
-            return lo, hi, tiles, neg_q, square, tag
-
-        def slope(step, tag):
-            lo, hi, tiles, neg_q, square, bank = step
-            y = keep.tile([P, len(tiles), hi - lo], F32, name="y", tag=tag, align_bytes=64)
-            nc.vector.scalar_tensor_tensor(
-                y[:].rearrange("p e j -> p (e j)"),
-                square[:].rearrange("p e j -> p (e j)"),
-                1.0,
-                neg_q[:].rearrange("p e j -> p (e j)"),
-                ALU.subtract,
-                ALU.mult,
+        def quantise_wb(b, u):
+            half = sb([P, 2, P, PACK], BF16, f"wb_bf{b}_{u}")
+            dst = half[:].rearrange("p e m t -> p m e t")
+            src = wb_raw[b][:].rearrange("p t (m i) -> p m i t", i=PACK)[:, :, 2 * u : 2 * u + 2, :]
+            if u == 0:
+                nc.vector.tensor_scalar(dst, src, -1.0, None, ALU.mult)
+            else:
+                nc.scalar.activation(dst, src, ACT.Copy, scale=-1.0)
+            wb_codes[b, u] = sb([P, 2 * P], U32, f"wb_codes{b}_{u}")
+            wb_plane[b, u] = sb([P, 2 * P], U8, f"wb_plane{b}_{u}")
+            nc.vector.quantize_mx(
+                out=wb_codes[b, u][:].bitcast(FP8X4),
+                scales=wb_plane[b, u][:],
+                in_=half[:].rearrange("p e m t -> p (e m t)"),
             )
-            free_banks.append(bank)
-            return lo, hi, tiles, y
 
-        def put(lo, hi, tiles, y):
+        steps = []
+
+        def second_product(blocks, tiles):
+            n = len(steps)
+            neg_q = psum.tile([P, 2, BLOCK], F32, name="neg_q", tag=f"bank{FIRST_BANKS + n % (8 - FIRST_BANKS)}")
+            for half, (i, k) in enumerate((i, k) for i in tiles for k in blocks):
+                u, e = divmod(i, 2)
+                for b in range(H_PASSES):
+                    nc.tensor.matmul_mx(
+                        out=neg_q[:, half, :],
+                        lhsT=wb_codes[b, u][:, P * e : P * (e + 1)].bitcast(FP8X4),
+                        lhsT_scale=wb_plane[b, u][:, P * e : P * (e + 1)],
+                        rhs=h_codes[k][:, b, :].bitcast(FP8X4),
+                        rhs_scale=h_plane[k][:, b, :],
+                        start=(b == 0),
+                        stop=(b == H_PASSES - 1),
+                    )
+            flat = neg_q[:].rearrange("p e j -> p (e j)")
+            drive = sb([P, 2 * BLOCK], F32, f"drive{n}")
+            nc.scalar.activation(drive[:], flat, ACT.Tanh)
+            square = sb([P, 2 * BLOCK], F32, f"square{n}")
+            nc.scalar.activation(square[:], drive[:], ACT.Square)
+            steps.append((blocks, tiles, flat, square))
+            return n
+
+        def slope(n, tag=None):
+            blocks, tiles, flat, square = steps[n]
+            y = sb([P, 2 * BLOCK], F32, f"y{n}", tag)
+            nc.vector.scalar_tensor_tensor(y[:], square[:], 1.0, flat, ALU.subtract, ALU.mult)
+            return blocks, tiles, y
+
+        def put(blocks, tiles, y):
+            lo, hi = blocks[0] * BLOCK, (blocks[-1] + 1) * BLOCK
             for n, i in enumerate(tiles):
                 nc.vector.tensor_tensor(
-                    pages[i][:].indirect(place[:, lo // 16 : hi // 16]), y[:, n, :], weight[:, lo:hi], ALU.mult
+                    pages[i][:].indirect(place[:, lo // 16 : hi // 16]),
+                    y[:, n * (hi - lo) : (n + 1) * (hi - lo)],
+                    weight[:, lo:hi],
+                    ALU.mult,
                 )
                 if hi == S:
                     nc.sync.dma_start(out.rearrange("(p i) t -> i p t", i=PACK)[i], pages[i][:])
 
-        def next_block(lo):
-            first_product_through(lo + BLOCK, 0)
-            quantise_h(lo, lo + BLOCK, f"h_codes{lo}")
-            first_product_through(lo + BLOCK, LEAD)
-
         low, high = (0, 1), (2, 3)
-        first_product_through(BLOCK, 0)
+        first_product(0)
         for b in range(H_PASSES):
-            quantise_wb(b)
-        quantise_h(0, SUB, "wb_bf1_0")
-        quantise_h(SUB, BLOCK, "wb_bf2_0")
-        opening = [second_product(0, SUB, low), second_product(SUB, BLOCK, low)]
-        step = second_product(0, BLOCK, high)
-        sloped = [slope(first, f"h_bf0_{first[0]}") for first in opening]
-        for i, tag in ((2, "drive0_0"), (3, "square0_0")):
-            pages.append(keep.tile([P, T2], F32, name="page", tag=tag, align_bytes=64))
-            for lo in range(0, T2, T2 // 2):
-                nc.gpsimd.memset(pages[i][:, lo : lo + T2 // 2], 0.0)
-        for first in sloped:
-            put(*first)
-
-        next_block(BLOCK)
-        ahead = [second_product(BLOCK, 2 * BLOCK, tiles) for tiles in (low, high)]
-        put(*slope(step, f"h_bf2_{BLOCK}"))
-        put(*slope(ahead[0], f"h_bf0_{BLOCK}"))
-        next_block(2 * BLOCK)
-        step = second_product(2 * BLOCK, 3 * BLOCK, low)
-        put(*slope(ahead[1], f"h_bf2_{2 * BLOCK}"))
-        next_block(3 * BLOCK)
-        ahead = [second_product(3 * BLOCK, S, low)] + [second_product(2 * BLOCK, S, (i,)) for i in high]
-        put(*slope(step, f"h_bf2_{3 * BLOCK}"))
-        for b, step in enumerate(ahead):
-            put(*slope(step, f"h_bf{b % 2}_{(2 + b // 2) * BLOCK}"))
+            quantise_wb(b, 0)
+        first = second_product((0,), low)
+        for b in range(H_PASSES):
+            quantise_wb(b, 1)
+        clear_page(2, "wb_bf1_0")
+        clear_page(3, "wb_bf2_0")
+        put(*slope(first))
+        first_product(1)
+        put(*slope(second_product((0,), high)))
+        first_product(2)
+        pair = [second_product((1,), low), second_product((1,), high)]
+        for step in [slope(pair[0], f"drive{pair[1]}"), slope(pair[1])]:
+            put(*step)
+        first_product(3)
+        put(*slope(second_product((2,), low)))
+        pair = [second_product((3,), low), second_product((2, 3), (2,))]
+        last = second_product((2, 3), (3,))
+        for step in [slope(pair[0], f"drive{pair[1]}"), slope(pair[1]), slope(last)]:
+            put(*step)

@@ -41,44 +41,45 @@ def tile_list_armband_gain_sensitivity_kernel(
         place = lists.tile([P, S // 16], U16, name="place")
 
         sc_win = sb([P, T], U8, "sc_win")
-        wa_raw = sb([P, K_PASSES, H // 2], I32, "wa_raw")
         was_raw = sb([P, K_PASSES, H], U8, "was_raw")
         sc_got = sb([P, S], U8, "sc_got")
         v_plane = [sb([P, S], U8, f"v_plane{a}") for a in range(K_PASSES)]
         warm_in = sb([P, 1], F32, "warm_in", "table0")
         warm_out = sb([P, 1], F32, "warm_out", "table1")
 
+        gate = sb([P, 1], F32, "gate", "wa_raw")
+        nc.vector.memset(gate[:], 0.0)
         nc.vector.memset(sc_win[:].bitcast(I32), 0)
-        nc.vector.memset(warm_in[:], 0.0)
         nc.vector.memset(was_raw[:].rearrange("p a c -> p (a c)").bitcast(I32), 0)
+        nc.vector.tensor_copy(warm_in[:], gate[:])
         for a in range(K_PASSES):
             nc.vector.memset(v_plane[a][:].bitcast(I32), 0)
         nc.scalar.activation(warm_out[:], warm_in[:], ACT.Tanh)
 
         nc.sync.dma_start(pick[:], offs)
         nc.sync.dma_start(place[:], offs2)
-        nc.sync.dma_start(wa_raw[:], wa_words.bitcast(I32).rearrange("a p c -> p a c"))
         tab_rows = tab_scales.bitcast(I32)
         win32 = sc_win[:].bitcast(I32)
         for q in range(4):
             nc.sync.dma_start(win32[32 * q + 14 : 32 * q + 18, :], tab_rows[0, 4 * q : 4 * q + 4, :])
         nc.sync.dma_start(win32[3:P:8, :], tab_rows[1])
-        table = [sb([P, T], I32, "table", f"table{a}") for a in range(K_PASSES)]
-        for a in range(K_PASSES):
-            nc.sync.dma_start(table[a][:], tab_words[a].rearrange("p t i -> p (t i)").bitcast(I32))
+        wa_raw = sb([P, K_PASSES, H // 2], I32, "wa_raw")
+        nc.sync.dma_start(wa_raw[:], wa_words.bitcast(I32).rearrange("a p c -> p a c"))
         wa_rows = wa_scales.bitcast(I32).rearrange("a q c -> q a c")
         was32 = was_raw[:].bitcast(I32)
         for q in range(4):
-            nc.scalar.dma_start(was32[32 * q : 32 * q + 4, :, :], wa_rows[4 * q : 4 * q + 4, :, :])
+            nc.sync.dma_start(was32[32 * q : 32 * q + 4, :, :], wa_rows[4 * q : 4 * q + 4, :, :])
+        table = [sb([P, T], I32, "table", f"table{a}") for a in range(K_PASSES)]
+        for a in range(K_PASSES):
+            nc.sync.dma_start(table[a][:], tab_words[a].rearrange("p t i -> p (t i)").bitcast(I32))
 
         pages = {}
 
         def clear_page(i, tag):
             pages[i] = sb([P, T2], F32, "page", tag)
-            nc.vector.memset(pages[i][:], 0.0)
+            nc.vector.memset(pages[i][:].bitcast(I32), 0)
 
         clear_page(0, "page0")
-        clear_page(1, "page1")
 
         nc.vector.tensor_copy(sc_got[:], sc_win[:].indirect(pick[:]))
         got32 = sc_got[:].bitcast(I32)
@@ -104,20 +105,25 @@ def tile_list_armband_gain_sensitivity_kernel(
         nc.sync.dma_start(weight[:], wgo)
 
         v_words = {}
-        for a, lo, hi in ((0, 0, S), (1, 0, BLOCK), (1, BLOCK, S)):
-            got = sb([P, hi - lo], U32, f"v_words{a}_{lo}")
+
+        def gather_words(a, lo, hi, tag=None):
+            got = sb([P, hi - lo], U32, f"v_words{a}_{lo}", tag)
             nc.vector.tensor_copy(got[:], table[a][:].bitcast(U32).indirect(pick[:, lo // 16 : hi // 16]))
             for j in range(lo, hi, SUB):
                 v_words[a, j] = got[:, j - lo : j - lo + SUB]
 
+        gather_words(0, 0, S)
+        gather_words(1, 0, BLOCK)
+        gather_words(1, BLOCK, S)
+
         h_codes, h_plane = {}, {}
         units = []
 
-        def first_product(k):
+        def first_product(k, passes=range(H_PASSES)):
             lo = k * BLOCK
-            h_codes[k] = sb([P, H_PASSES, BLOCK], U32, f"h_codes{k}")
-            h_plane[k] = sb([P, H_PASSES, BLOCK], U8, f"h_plane{k}")
-            for b in range(H_PASSES):
+            for b in passes:
+                h_codes[k, b] = sb([P, BLOCK], U32, f"h_codes{k}_{b}")
+                h_plane[k, b] = sb([P, BLOCK], U8, f"h_plane{k}_{b}")
                 h_bf = sb([P, BLOCK, PACK], BF16, f"h_bf{k}_{b}")
                 for j in range(lo, lo + BLOCK, SUB):
                     acc = psum.tile([P, PACK, SUB], F32, name="acc", tag=f"bank{len(units) % FIRST_BANKS}")
@@ -134,10 +140,14 @@ def tile_list_armband_gain_sensitivity_kernel(
                                 start=(a == 0),
                                 stop=(a == K_PASSES - 1),
                             )
-                    nc.scalar.activation(h_bf[:, j - lo : j - lo + SUB, :], acc[:].rearrange("p t j -> p j t"), ACT.Relu)
+                    nc.scalar.activation(
+                        h_bf[:, j - lo : j - lo + SUB, :].rearrange("p (j e) t -> p j t e", e=2),
+                        acc[:].rearrange("p t (j e) -> p j t e", e=2),
+                        ACT.Relu,
+                    )
                 nc.vector.quantize_mx(
-                    out=h_codes[k][:, b, :].bitcast(FP8X4),
-                    scales=h_plane[k][:, b, :],
+                    out=h_codes[k, b][:].bitcast(FP8X4),
+                    scales=h_plane[k, b][:],
                     in_=h_bf[:].rearrange("p j t -> p (j t)"),
                 )
 
@@ -171,8 +181,8 @@ def tile_list_armband_gain_sensitivity_kernel(
                         out=neg_q[:, half, :],
                         lhsT=wb_codes[b, u][:, P * e : P * (e + 1)].bitcast(FP8X4),
                         lhsT_scale=wb_plane[b, u][:, P * e : P * (e + 1)],
-                        rhs=h_codes[k][:, b, :].bitcast(FP8X4),
-                        rhs_scale=h_plane[k][:, b, :],
+                        rhs=h_codes[k, b][:].bitcast(FP8X4),
+                        rhs_scale=h_plane[k, b][:],
                         start=(b == 0),
                         stop=(b == H_PASSES - 1),
                     )
@@ -204,14 +214,17 @@ def tile_list_armband_gain_sensitivity_kernel(
 
         low, high = (0, 1), (2, 3)
         first_product(0)
-        for b in range(H_PASSES):
+        quantise_wb(0, 0)
+        clear_page(1, "wb_bf0_0")
+        for b in range(1, H_PASSES):
             quantise_wb(b, 0)
         first = second_product((0,), low)
         for b in range(H_PASSES):
             quantise_wb(b, 1)
-        clear_page(2, "wb_bf1_0")
-        clear_page(3, "wb_bf2_0")
-        put(*slope(first))
+        clear_page(2, "wb_bf2_0")
+        step = slope(first)
+        clear_page(3, f"square{first}")
+        put(*step)
         first_product(1)
         put(*slope(second_product((0,), high)))
         first_product(2)

@@ -32,6 +32,7 @@ def tile_list_armband_gain_sensitivity_kernel(
     with ExitStack() as ctx:
         lists = ctx.enter_context(tc.tile_pool(name="lists", bufs=1))
         keep = ctx.enter_context(tc.tile_pool(name="keep", bufs=1))
+        head = ctx.enter_context(tc.tile_pool(name="head", bufs=1))
         psum = ctx.enter_context(tc.psum_pool(name="psum", bufs=1))
 
         def sb(shape, dtype, name, tag=None):
@@ -41,19 +42,29 @@ def tile_list_armband_gain_sensitivity_kernel(
         place = lists.tile([P, S // 16], U16, name="place")
 
         sc_win = sb([P, T], U8, "sc_win")
-        was_raw = sb([P, K_PASSES, H], U8, "was_raw")
+        was_raw = head.tile([P, K_PASSES, H], U8, name="was_raw", align_bytes=64, offset=4 * T2 - 64)
         sc_got = sb([P, S], U8, "sc_got")
         v_plane = [sb([P, S], U8, f"v_plane{a}") for a in range(K_PASSES)]
-        warm_in = sb([P, 1], F32, "warm_in", "table0")
+        warm_in = sb([P, 1], F32, "warm_in")
         warm_out = sb([P, 1], F32, "warm_out", "table1")
 
-        gate = sb([P, 1], F32, "gate", "wa_raw")
+        gate = sb([P, 1], F32, "gate", "table0")
+        gate_wa = sb([P, 1], F32, "gate_wa", "wa_raw")
+        relay = sb([P, 1], F32, "relay")
+
+        def clear_words(words):
+            odd = words.shape[1] // 2 + 1
+            nc.vector.memset(words[:, 0:odd], 0)
+            nc.vector.memset(words[:, odd:], 0)
+
+        nc.gpsimd.memset(sc_win[:].bitcast(I32), 0)
         nc.vector.memset(gate[:], 0.0)
-        nc.vector.memset(sc_win[:].bitcast(I32), 0)
-        nc.vector.memset(was_raw[:].rearrange("p a c -> p (a c)").bitcast(I32), 0)
-        nc.vector.tensor_copy(warm_in[:], gate[:])
+        nc.vector.memset(gate_wa[:], 0.0)
+        nc.vector.tensor_tensor(relay[:], gate[:], gate_wa[:], ALU.add)
+        clear_words(was_raw[:].rearrange("p a c -> p (a c)").bitcast(I32))
+        nc.vector.tensor_copy(warm_in[:], relay[:])
         for a in range(K_PASSES):
-            nc.vector.memset(v_plane[a][:].bitcast(I32), 0)
+            clear_words(v_plane[a][:].bitcast(I32))
         nc.scalar.activation(warm_out[:], warm_in[:], ACT.Tanh)
 
         nc.sync.dma_start(pick[:], offs)
@@ -65,21 +76,24 @@ def tile_list_armband_gain_sensitivity_kernel(
         nc.sync.dma_start(win32[3:P:8, :], tab_rows[1])
         wa_raw = sb([P, K_PASSES, H // 2], I32, "wa_raw")
         nc.sync.dma_start(wa_raw[:], wa_words.bitcast(I32).rearrange("a p c -> p a c"))
+        table = [sb([P, T], I32, "table", f"table{a}") for a in range(K_PASSES)]
+        table_rows = [tab_words[a].rearrange("p t i -> p (t i)").bitcast(I32) for a in range(K_PASSES)]
+        nc.sync.dma_start(table[0][:], table_rows[0])
         wa_rows = wa_scales.bitcast(I32).rearrange("a q c -> q a c")
         was32 = was_raw[:].bitcast(I32)
         for q in range(4):
             nc.sync.dma_start(was32[32 * q : 32 * q + 4, :, :], wa_rows[4 * q : 4 * q + 4, :, :])
-        table = [sb([P, T], I32, "table", f"table{a}") for a in range(K_PASSES)]
-        for a in range(K_PASSES):
-            nc.sync.dma_start(table[a][:], tab_words[a].rearrange("p t i -> p (t i)").bitcast(I32))
+        nc.sync.dma_start(table[1][:], table_rows[1])
 
         pages = {}
 
         def clear_page(i, tag):
             pages[i] = sb([P, T2], F32, "page", tag)
-            nc.vector.memset(pages[i][:].bitcast(I32), 0)
+            for lo in range(0, T2, T2 // 2):
+                nc.gpsimd.memset(pages[i][:, lo : lo + T2 // 2], 0.0)
 
         clear_page(0, "page0")
+        clear_page(1, "page1")
 
         nc.vector.tensor_copy(sc_got[:], sc_win[:].indirect(pick[:]))
         got32 = sc_got[:].bitcast(I32)
@@ -97,12 +111,20 @@ def tile_list_armband_gain_sensitivity_kernel(
 
         wb_rows = wb.rearrange("(b q t s) n -> b t q s n", b=H_PASSES, q=16, t=PACK)
         wb_raw = []
-        for b, tag in enumerate(("sc_win", "wa_raw", "was_raw")):
-            wb_raw.append(sb([P, PACK, N], F32, "wb_raw", tag))
+        wb_last_at = 4 * T2 + K_PASSES * H - 128
+        for b in range(H_PASSES):
+            if b < 2:
+                wb_raw.append(sb([P, PACK, N], F32, "wb_raw", ("sc_win", "wa_raw")[b]))
+            else:
+                wb_raw.append(head.tile([P, PACK, N], F32, name="wb_last", align_bytes=64, offset=wb_last_at))
             for t in range(PACK):
                 nc.sync.dma_start(wb_raw[b][:, t, :], wb_rows[b, t])
         weight = sb([P, S], F32, "weight", "sc_got")
         nc.sync.dma_start(weight[:], wgo)
+
+        pages[2] = head.tile([P, T2], F32, name="page2", align_bytes=64, offset=0)
+        for lo in range(0, T2, T2 // 2):
+            nc.gpsimd.memset(pages[2][:, lo : lo + T2 // 2], 0.0)
 
         v_words = {}
 
@@ -119,12 +141,12 @@ def tile_list_armband_gain_sensitivity_kernel(
         h_codes, h_plane = {}, {}
         units = []
 
-        def first_product(k, passes=range(H_PASSES)):
+        def first_product(k, passes=range(H_PASSES), behind=None):
             lo = k * BLOCK
             for b in passes:
                 h_codes[k, b] = sb([P, BLOCK], U32, f"h_codes{k}_{b}")
                 h_plane[k, b] = sb([P, BLOCK], U8, f"h_plane{k}_{b}")
-                h_bf = sb([P, BLOCK, PACK], BF16, f"h_bf{k}_{b}")
+                h_bf = sb([P, BLOCK, PACK], BF16, f"h_bf{k}_{b}", behind)
                 for j in range(lo, lo + BLOCK, SUB):
                     acc = psum.tile([P, PACK, SUB], F32, name="acc", tag=f"bank{len(units) % FIRST_BANKS}")
                     units.append(j)
@@ -153,14 +175,11 @@ def tile_list_armband_gain_sensitivity_kernel(
 
         wb_codes, wb_plane = {}, {}
 
-        def quantise_wb(b, u):
-            half = sb([P, 2, P, PACK], BF16, f"wb_bf{b}_{u}")
+        def quantise_wb(b, u, behind=None):
+            half = sb([P, 2, P, PACK], BF16, f"wb_bf{b}_{u}", behind)
             dst = half[:].rearrange("p e m t -> p m e t")
             src = wb_raw[b][:].rearrange("p t (m i) -> p m i t", i=PACK)[:, :, 2 * u : 2 * u + 2, :]
-            if u == 0:
-                nc.vector.tensor_scalar(dst, src, -1.0, None, ALU.mult)
-            else:
-                nc.scalar.activation(dst, src, ACT.Copy, scale=-1.0)
+            nc.vector.tensor_scalar(dst, src, -1.0, None, ALU.mult)
             wb_codes[b, u] = sb([P, 2 * P], U32, f"wb_codes{b}_{u}")
             wb_plane[b, u] = sb([P, 2 * P], U8, f"wb_plane{b}_{u}")
             nc.vector.quantize_mx(
@@ -173,7 +192,8 @@ def tile_list_armband_gain_sensitivity_kernel(
 
         def second_product(blocks, tiles):
             n = len(steps)
-            neg_q = psum.tile([P, 2, BLOCK], F32, name="neg_q", tag=f"bank{FIRST_BANKS + n % (8 - FIRST_BANKS)}")
+            width = len(blocks) * len(tiles) * BLOCK
+            neg_q = psum.tile([P, width // BLOCK, BLOCK], F32, name="neg_q", tag=f"bank{FIRST_BANKS + n % (8 - FIRST_BANKS)}")
             for half, (i, k) in enumerate((i, k) for i in tiles for k in blocks):
                 u, e = divmod(i, 2)
                 for b in range(H_PASSES):
@@ -187,16 +207,16 @@ def tile_list_armband_gain_sensitivity_kernel(
                         stop=(b == H_PASSES - 1),
                     )
             flat = neg_q[:].rearrange("p e j -> p (e j)")
-            drive = sb([P, 2 * BLOCK], F32, f"drive{n}")
+            drive = sb([P, width], F32, f"drive{n}")
             nc.scalar.activation(drive[:], flat, ACT.Tanh)
-            square = sb([P, 2 * BLOCK], F32, f"square{n}")
+            square = sb([P, width], F32, f"square{n}")
             nc.scalar.activation(square[:], drive[:], ACT.Square)
             steps.append((blocks, tiles, flat, square))
             return n
 
         def slope(n, tag=None):
             blocks, tiles, flat, square = steps[n]
-            y = sb([P, 2 * BLOCK], F32, f"y{n}", tag)
+            y = sb([P, flat.shape[1]], F32, f"y{n}", tag)
             nc.vector.scalar_tensor_tensor(y[:], square[:], 1.0, flat, ALU.subtract, ALU.mult)
             return blocks, tiles, y
 
@@ -214,19 +234,21 @@ def tile_list_armband_gain_sensitivity_kernel(
 
         low, high = (0, 1), (2, 3)
         first_product(0)
-        quantise_wb(0, 0)
-        clear_page(1, "wb_bf0_0")
-        for b in range(1, H_PASSES):
-            quantise_wb(b, 0)
-        first = second_product((0,), low)
         for b in range(H_PASSES):
+            quantise_wb(b, 0)
+        first = second_product((0,), (0,))
+        second = second_product((0,), (1,))
+        for b in range(H_PASSES - 1):
             quantise_wb(b, 1)
-        clear_page(2, "wb_bf2_0")
+        quantise_wb(H_PASSES - 1, 1, "wb_bf2_0")
+        later = second_product((0,), high)
         step = slope(first)
         clear_page(3, f"square{first}")
         put(*step)
-        first_product(1)
-        put(*slope(second_product((0,), high)))
+        put(*slope(second))
+        first_product(1, (0,), f"drive{second}")
+        first_product(1, (1, 2))
+        put(*slope(later, "h_bf1_2"))
         first_product(2)
         pair = [second_product((1,), low), second_product((1,), high)]
         for step in [slope(pair[0], f"drive{pair[1]}"), slope(pair[1])]:

@@ -23,6 +23,7 @@ H_PASSES = H // 512
 BLOCK = 256
 SUB = 128
 FIRST_BANKS = 4
+ON_VECTOR = 3
 
 
 def tile_list_armband_gain_sensitivity_kernel(
@@ -65,7 +66,7 @@ def tile_list_armband_gain_sensitivity_kernel(
         nc.vector.tensor_copy(warm_in[:], relay[:])
         for a in range(K_PASSES):
             clear_words(v_plane[a][:].bitcast(I32))
-        nc.scalar.activation(warm_out[:], warm_in[:], ACT.Tanh)
+        nc.scalar.activation(warm_out[:], warm_in[:], ACT.Silu)
 
         nc.sync.dma_start(pick[:], offs)
         nc.sync.dma_start(place[:], offs2)
@@ -136,7 +137,7 @@ def tile_list_armband_gain_sensitivity_kernel(
 
         gather_words(0, 0, S)
         gather_words(1, 0, BLOCK)
-        gather_words(1, BLOCK, S)
+        gather_words(1, BLOCK, 2 * BLOCK)
 
         h_codes, h_plane = {}, {}
         units = []
@@ -179,7 +180,7 @@ def tile_list_armband_gain_sensitivity_kernel(
             half = sb([P, 2, P, PACK], BF16, f"wb_bf{b}_{u}", behind)
             dst = half[:].rearrange("p e m t -> p m e t")
             src = wb_raw[b][:].rearrange("p t (m i) -> p m i t", i=PACK)[:, :, 2 * u : 2 * u + 2, :]
-            nc.vector.tensor_scalar(dst, src, -1.0, None, ALU.mult)
+            nc.vector.tensor_scalar(dst, src, 2.0, None, ALU.mult)
             wb_codes[b, u] = sb([P, 2 * P], U32, f"wb_codes{b}_{u}")
             wb_plane[b, u] = sb([P, 2 * P], U8, f"wb_plane{b}_{u}")
             nc.vector.quantize_mx(
@@ -207,28 +208,39 @@ def tile_list_armband_gain_sensitivity_kernel(
                         stop=(b == H_PASSES - 1),
                     )
             flat = neg_q[:].rearrange("p e j -> p (e j)")
+            gated = sb([P, width], F32, f"gated{n}")
+            nc.scalar.activation(gated[:], flat, ACT.Silu)
             drive = sb([P, width], F32, f"drive{n}")
-            nc.scalar.activation(drive[:], flat, ACT.Tanh)
-            square = sb([P, width], F32, f"square{n}")
-            nc.scalar.activation(square[:], drive[:], ACT.Square)
-            steps.append((blocks, tiles, flat, square))
+            nc.scalar.activation(drive[:], flat, ACT.Tanh, scale=0.5)
+            rest = sb([P, width], F32, f"square{n}")
+            nc.scalar.activation(rest[:], drive[:], ACT.Identity, scale=-1.0, bias=1.0)
+            steps.append((blocks, tiles, gated, rest))
             return n
 
         def slope(n, tag=None):
-            blocks, tiles, flat, square = steps[n]
-            y = sb([P, flat.shape[1]], F32, f"y{n}", tag)
-            nc.vector.scalar_tensor_tensor(y[:], square[:], 1.0, flat, ALU.subtract, ALU.mult)
-            return blocks, tiles, y
+            blocks, tiles, gated, rest = steps[n]
+            y = sb([P, gated.shape[1]], F32, f"y{n}", tag)
+            if n < ON_VECTOR:
+                nc.vector.tensor_tensor(y[:], gated[:], rest[:], ALU.mult)
+                return blocks, tiles, y, True
+            lo, hi = blocks[0] * BLOCK, (blocks[-1] + 1) * BLOCK
+            bare = sb([P, gated.shape[1]], F32, f"bare{n}")
+            for at in range(0, gated.shape[1], BLOCK):
+                cols = slice(at, at + BLOCK)
+                entry = lo + at % (hi - lo)
+                nc.gpsimd.tensor_tensor(bare[:, cols], gated[:, cols], rest[:, cols], ALU.mult)
+                nc.gpsimd.tensor_tensor(y[:, cols], bare[:, cols], weight[:, entry : entry + BLOCK], ALU.mult)
+            return blocks, tiles, y, False
 
-        def put(blocks, tiles, y):
+        def put(blocks, tiles, y, unweighted):
             lo, hi = blocks[0] * BLOCK, (blocks[-1] + 1) * BLOCK
             for n, i in enumerate(tiles):
-                nc.vector.tensor_tensor(
-                    pages[i][:].indirect(place[:, lo // 16 : hi // 16]),
-                    y[:, n * (hi - lo) : (n + 1) * (hi - lo)],
-                    weight[:, lo:hi],
-                    ALU.mult,
-                )
+                slots = pages[i][:].indirect(place[:, lo // 16 : hi // 16])
+                values = y[:, n * (hi - lo) : (n + 1) * (hi - lo)]
+                if unweighted:
+                    nc.vector.tensor_tensor(slots, values, weight[:, lo:hi], ALU.mult)
+                else:
+                    nc.vector.tensor_copy(slots, values)
                 if hi == S:
                     nc.sync.dma_start(out.rearrange("(p i) t -> i p t", i=PACK)[i], pages[i][:])
 
@@ -241,21 +253,19 @@ def tile_list_armband_gain_sensitivity_kernel(
         for b in range(H_PASSES - 1):
             quantise_wb(b, 1)
         quantise_wb(H_PASSES - 1, 1, "wb_bf2_0")
+        gather_words(1, 2 * BLOCK, S, "wb_bf2_0")
         later = second_product((0,), high)
+        first_product(1)
         step = slope(first)
         clear_page(3, f"square{first}")
         put(*step)
         put(*slope(second))
-        first_product(1, (0,), f"drive{second}")
-        first_product(1, (1, 2))
-        put(*slope(later, "h_bf1_2"))
+        put(*slope(later))
         first_product(2)
-        pair = [second_product((1,), low), second_product((1,), high)]
-        for step in [slope(pair[0], f"drive{pair[1]}"), slope(pair[1])]:
-            put(*step)
-        first_product(3)
-        put(*slope(second_product((2,), low)))
-        pair = [second_product((3,), low), second_product((2, 3), (2,))]
-        last = second_product((2, 3), (3,))
-        for step in [slope(pair[0], f"drive{pair[1]}"), slope(pair[1]), slope(last)]:
-            put(*step)
+        put(*slope(second_product((1,), low)))
+        first_product(3, (0, 1))
+        step = slope(second_product((1,), high))
+        first_product(3, (2,))
+        put(*step)
+        for blocks, tiles in (((2,), low), ((3,), low), ((2, 3), (2,)), ((2, 3), (3,))):
+            put(*slope(second_product(blocks, tiles)))

@@ -18,12 +18,18 @@ ALU = mybir.AluOpType
 
 P = 128
 PACK = 4
+GROUP = 16
+QUADS = 4
 K_PASSES = K // 512
 H_PASSES = H // 512
 BLOCK = 256
 SUB = 128
-FIRST_BANKS = 4
-ON_VECTOR = 3
+BANKS = 8
+FIRST_BANKS = 6
+ALIGN = 64
+SHIFT = 14
+MOVED = 112
+SPARE = 3
 
 
 def tile_list_armband_gain_sensitivity_kernel(
@@ -33,124 +39,126 @@ def tile_list_armband_gain_sensitivity_kernel(
     with ExitStack() as ctx:
         lists = ctx.enter_context(tc.tile_pool(name="lists", bufs=1))
         keep = ctx.enter_context(tc.tile_pool(name="keep", bufs=1))
-        head = ctx.enter_context(tc.tile_pool(name="head", bufs=1))
+        placed = ctx.enter_context(tc.tile_pool(name="placed", bufs=1))
         psum = ctx.enter_context(tc.psum_pool(name="psum", bufs=1))
 
-        def sb(shape, dtype, name, tag=None):
-            return keep.tile(shape, dtype, name=name, tag=tag or name, align_bytes=64)
+        def sb(shape, dtype, name, takes_over=None):
+            return keep.tile(shape, dtype, name=name, tag=takes_over or name, align_bytes=ALIGN)
 
-        pick = lists.tile([P, S // 16], U16, name="pick")
-        place = lists.tile([P, S // 16], U16, name="place")
+        pick = lists.tile([P, S // GROUP], U16, name="pick")
+        place = lists.tile([P, S // GROUP], U16, name="place")
 
-        sc_win = sb([P, T], U8, "sc_win")
-        was_raw = head.tile([P, K_PASSES, H], U8, name="was_raw", align_bytes=64, offset=4 * T2 - 64)
-        sc_got = sb([P, S], U8, "sc_got")
+        wa_scale_at = 4 * T2 - ALIGN
+        wb_last_at = wa_scale_at + K_PASSES * H - ALIGN
+
+        scale_window = sb([P, T], U8, "scale_window")
+        wa_scale_raw = placed.tile([P, K_PASSES, H], U8, name="wa_scale_raw", align_bytes=ALIGN, offset=wa_scale_at)
+        scale_got = sb([P, S], U8, "scale_got")
         v_plane = [sb([P, S], U8, f"v_plane{a}") for a in range(K_PASSES)]
-        warm_in = sb([P, 1], F32, "warm_in")
-        warm_out = sb([P, 1], F32, "warm_out", "table1")
 
-        gate = sb([P, 1], F32, "gate", "table0")
-        gate_wa = sb([P, 1], F32, "gate_wa", "wa_raw")
-        relay = sb([P, 1], F32, "relay")
+        zero_a = sb([P, 1], F32, "zero_a", "table0")
+        zero_b = sb([P, 1], F32, "zero_b", "wa_raw")
+        zero_sum = sb([P, 1], F32, "zero_sum")
+        silu_in = sb([P, 1], F32, "silu_in", "table1")
+        relu_bias = sb([P, 1], F32, "relu_bias")
 
         def clear_words(words):
             odd = words.shape[1] // 2 + 1
             nc.vector.memset(words[:, 0:odd], 0)
             nc.vector.memset(words[:, odd:], 0)
 
-        nc.gpsimd.memset(sc_win[:].bitcast(I32), 0)
-        nc.vector.memset(gate[:], 0.0)
-        nc.vector.memset(gate_wa[:], 0.0)
-        nc.vector.tensor_tensor(relay[:], gate[:], gate_wa[:], ALU.add)
-        clear_words(was_raw[:].rearrange("p a c -> p (a c)").bitcast(I32))
-        nc.vector.tensor_copy(warm_in[:], relay[:])
+        nc.gpsimd.memset(scale_window[:].bitcast(I32), 0)
+        nc.vector.memset(zero_a[:], 0.0)
+        nc.vector.memset(zero_b[:], 0.0)
+        nc.vector.tensor_tensor(zero_sum[:], zero_a[:], zero_b[:], ALU.add)
+        clear_words(wa_scale_raw[:].rearrange("p a c -> p (a c)").bitcast(I32))
+        nc.vector.tensor_copy(silu_in[:], zero_sum[:])
         for a in range(K_PASSES):
             clear_words(v_plane[a][:].bitcast(I32))
-        nc.scalar.activation(warm_out[:], warm_in[:], ACT.Silu)
+        nc.scalar.activation(relu_bias[:], silu_in[:], ACT.Silu)
 
         nc.sync.dma_start(pick[:], offs)
         nc.sync.dma_start(place[:], offs2)
-        tab_rows = tab_scales.bitcast(I32)
-        win32 = sc_win[:].bitcast(I32)
-        for q in range(4):
-            nc.sync.dma_start(win32[32 * q + 14 : 32 * q + 18, :], tab_rows[0, 4 * q : 4 * q + 4, :])
-        nc.sync.dma_start(win32[3:P:8, :], tab_rows[1])
+        tab_scale_rows = tab_scales.bitcast(I32)
+        window32 = scale_window[:].bitcast(I32)
+        for d in range(QUADS):
+            nc.sync.dma_start(window32[32 * d + SHIFT : 32 * d + SHIFT + 4, :], tab_scale_rows[0, 4 * d : 4 * d + 4, :])
+        nc.sync.dma_start(window32[SPARE:P:8, :], tab_scale_rows[1])
         wa_raw = sb([P, K_PASSES, H // 2], I32, "wa_raw")
         nc.sync.dma_start(wa_raw[:], wa_words.bitcast(I32).rearrange("a p c -> p a c"))
-        table = [sb([P, T], I32, "table", f"table{a}") for a in range(K_PASSES)]
+        table = [sb([P, T], I32, f"table{a}") for a in range(K_PASSES)]
         table_rows = [tab_words[a].rearrange("p t i -> p (t i)").bitcast(I32) for a in range(K_PASSES)]
         nc.sync.dma_start(table[0][:], table_rows[0])
-        wa_rows = wa_scales.bitcast(I32).rearrange("a q c -> q a c")
-        was32 = was_raw[:].bitcast(I32)
-        for q in range(4):
-            nc.sync.dma_start(was32[32 * q : 32 * q + 4, :, :], wa_rows[4 * q : 4 * q + 4, :, :])
+        wa_scale_rows = wa_scales.bitcast(I32).rearrange("a q c -> q a c")
+        wa_scale32 = wa_scale_raw[:].bitcast(I32)
+        for d in range(QUADS):
+            nc.sync.dma_start(wa_scale32[32 * d : 32 * d + 4, :, :], wa_scale_rows[4 * d : 4 * d + 4, :, :])
         nc.sync.dma_start(table[1][:], table_rows[1])
 
         pages = {}
 
-        def clear_page(i, tag):
-            pages[i] = sb([P, T2], F32, "page", tag)
+        def clear_page(i, page):
+            pages[i] = page
             for lo in range(0, T2, T2 // 2):
-                nc.gpsimd.memset(pages[i][:, lo : lo + T2 // 2], 0.0)
+                nc.gpsimd.memset(page[:, lo : lo + T2 // 2], 0.0)
 
-        clear_page(0, "page0")
-        clear_page(1, "page1")
+        clear_page(0, sb([P, T2], F32, "page0"))
+        clear_page(1, sb([P, T2], F32, "page1"))
 
-        nc.vector.tensor_copy(sc_got[:], sc_win[:].indirect(pick[:]))
-        got32 = sc_got[:].bitcast(I32)
-        for r in range(4):
-            nc.sync.dma_start(v_plane[1][:].bitcast(I32)[r:P:32, :], got32[8 * r + 3 : P : 32, :])
-        nc.sync.dma_start(v_plane[0][:].bitcast(I32)[0:112, :], got32[14:126, :])
+        nc.vector.tensor_copy(scale_got[:], scale_window[:].indirect(pick[:]))
+        got32 = scale_got[:].bitcast(I32)
+        nc.sync.dma_start(v_plane[0][:].bitcast(I32)[0:MOVED, :], got32[SHIFT : SHIFT + MOVED, :])
+        for row in range(4):
+            nc.sync.dma_start(v_plane[1][:].bitcast(I32)[row:P:32, :], got32[8 * row + SPARE : P : 32, :])
 
         wa_codes = sb([P, K_PASSES, 2 * H], U8, "wa_codes")
         wa_plane = sb([P, K_PASSES, H], U8, "wa_plane")
-        for dst, src in ((wa_codes, wa_raw[:]), (wa_plane, was32)):
+        for dealt, raw in ((wa_codes, wa_raw[:]), (wa_plane, wa_scale32)):
             nc.vector.tensor_copy(
-                dst[:].bitcast(I32).rearrange("p a (b t q w) -> p (a b) t q w", b=H_PASSES, t=PACK, q=16),
-                src.rearrange("p a (b q t w) -> p (a b) t q w", b=H_PASSES, t=PACK, q=16),
+                dealt[:].bitcast(I32).rearrange("p a (b t q w) -> p (a b) t q w", b=H_PASSES, t=PACK, q=16),
+                raw.rearrange("p a (b q t w) -> p (a b) t q w", b=H_PASSES, t=PACK, q=16),
             )
 
         wb_rows = wb.rearrange("(b q t s) n -> b t q s n", b=H_PASSES, q=16, t=PACK)
         wb_raw = []
-        wb_last_at = 4 * T2 + K_PASSES * H - 128
-        for b in range(H_PASSES):
-            if b < 2:
-                wb_raw.append(sb([P, PACK, N], F32, "wb_raw", ("sc_win", "wa_raw")[b]))
-            else:
-                wb_raw.append(head.tile([P, PACK, N], F32, name="wb_last", align_bytes=64, offset=wb_last_at))
+
+        def load_wb(rows):
             for t in range(PACK):
-                nc.sync.dma_start(wb_raw[b][:, t, :], wb_rows[b, t])
-        weight = sb([P, S], F32, "weight", "sc_got")
+                nc.sync.dma_start(rows[:, t, :], wb_rows[len(wb_raw), t])
+            wb_raw.append(rows)
+
+        load_wb(sb([P, PACK, N], F32, "wb_raw0", "scale_window"))
+        load_wb(sb([P, PACK, N], F32, "wb_raw1", "wa_raw"))
+        load_wb(placed.tile([P, PACK, N], F32, name="wb_raw2", align_bytes=ALIGN, offset=wb_last_at))
+        weight = sb([P, S], F32, "weight", "scale_got")
         nc.sync.dma_start(weight[:], wgo)
 
-        pages[2] = head.tile([P, T2], F32, name="page2", align_bytes=64, offset=0)
-        for lo in range(0, T2, T2 // 2):
-            nc.gpsimd.memset(pages[2][:, lo : lo + T2 // 2], 0.0)
+        clear_page(2, placed.tile([P, T2], F32, name="page2", align_bytes=ALIGN, offset=0))
 
         v_words = {}
 
-        def gather_words(a, lo, hi, tag=None):
-            got = sb([P, hi - lo], U32, f"v_words{a}_{lo}", tag)
-            nc.vector.tensor_copy(got[:], table[a][:].bitcast(U32).indirect(pick[:, lo // 16 : hi // 16]))
+        def gather_words(a, lo, hi, takes_over=None):
+            got = sb([P, hi - lo], U32, f"v_words{a}_{lo}", takes_over)
+            nc.vector.tensor_copy(got[:], table[a][:].bitcast(U32).indirect(pick[:, lo // GROUP : hi // GROUP]))
             for j in range(lo, hi, SUB):
                 v_words[a, j] = got[:, j - lo : j - lo + SUB]
 
         gather_words(0, 0, S)
-        gather_words(1, 0, BLOCK)
-        gather_words(1, BLOCK, 2 * BLOCK)
+        for block in (0, 1, 3):
+            gather_words(1, block * BLOCK, (block + 1) * BLOCK)
 
         h_codes, h_plane = {}, {}
-        units = []
+        filled = []
 
-        def first_product(k, passes=range(H_PASSES), behind=None):
-            lo = k * BLOCK
-            for b in passes:
-                h_codes[k, b] = sb([P, BLOCK], U32, f"h_codes{k}_{b}")
-                h_plane[k, b] = sb([P, BLOCK], U8, f"h_plane{k}_{b}")
-                h_bf = sb([P, BLOCK, PACK], BF16, f"h_bf{k}_{b}", behind)
+        def first_product(block):
+            lo = block * BLOCK
+            for b in range(H_PASSES):
+                h_codes[block, b] = sb([P, BLOCK], U32, f"h_codes{block}_{b}")
+                h_plane[block, b] = sb([P, BLOCK], U8, f"h_plane{block}_{b}")
+                h_bf = sb([P, BLOCK, PACK], BF16, f"h_bf{block}_{b}")
                 for j in range(lo, lo + BLOCK, SUB):
-                    acc = psum.tile([P, PACK, SUB], F32, name="acc", tag=f"bank{len(units) % FIRST_BANKS}")
-                    units.append(j)
+                    acc = psum.tile([P, PACK, SUB], F32, name="acc", tag=f"bank{len(filled) % FIRST_BANKS}")
+                    filled.append(j)
                     for t in range(PACK):
                         col = 512 * b + P * t
                         for a in range(K_PASSES):
@@ -167,105 +175,116 @@ def tile_list_armband_gain_sensitivity_kernel(
                         h_bf[:, j - lo : j - lo + SUB, :].rearrange("p (j e) t -> p j t e", e=2),
                         acc[:].rearrange("p t (j e) -> p j t e", e=2),
                         ACT.Relu,
+                        bias=relu_bias[:],
                     )
                 nc.vector.quantize_mx(
-                    out=h_codes[k, b][:].bitcast(FP8X4),
-                    scales=h_plane[k, b][:],
+                    out=h_codes[block, b][:].bitcast(FP8X4),
+                    scales=h_plane[block, b][:],
                     in_=h_bf[:].rearrange("p j t -> p (j t)"),
                 )
 
         wb_codes, wb_plane = {}, {}
 
-        def quantise_wb(b, u, behind=None):
-            half = sb([P, 2, P, PACK], BF16, f"wb_bf{b}_{u}", behind)
-            dst = half[:].rearrange("p e m t -> p m e t")
-            src = wb_raw[b][:].rearrange("p t (m i) -> p m i t", i=PACK)[:, :, 2 * u : 2 * u + 2, :]
-            nc.vector.tensor_scalar(dst, src, 2.0, None, ALU.mult)
+        def quantise_wb(b, u, takes_over=None):
+            rounded = sb([P, 2, P, PACK], BF16, f"wb_bf{b}_{u}", takes_over)
+            nc.vector.tensor_copy(
+                rounded[:].rearrange("p e m t -> p m e t"),
+                wb_raw[b][:].rearrange("p t (m i) -> p m i t", i=PACK)[:, :, 2 * u : 2 * u + 2, :],
+            )
             wb_codes[b, u] = sb([P, 2 * P], U32, f"wb_codes{b}_{u}")
             wb_plane[b, u] = sb([P, 2 * P], U8, f"wb_plane{b}_{u}")
             nc.vector.quantize_mx(
                 out=wb_codes[b, u][:].bitcast(FP8X4),
                 scales=wb_plane[b, u][:],
-                in_=half[:].rearrange("p e m t -> p (e m t)"),
+                in_=rounded[:].rearrange("p e m t -> p (e m t)"),
             )
 
         steps = []
 
-        def second_product(blocks, tiles):
+        def second_product(blocks, step_pages):
             n = len(steps)
-            width = len(blocks) * len(tiles) * BLOCK
-            neg_q = psum.tile([P, width // BLOCK, BLOCK], F32, name="neg_q", tag=f"bank{FIRST_BANKS + n % (8 - FIRST_BANKS)}")
-            for half, (i, k) in enumerate((i, k) for i in tiles for k in blocks):
+            parts = [(i, block) for i in step_pages for block in blocks]
+            bank = FIRST_BANKS + n % (BANKS - FIRST_BANKS)
+            q = psum.tile([P, len(parts), BLOCK], F32, name="q", tag=f"bank{bank}")
+            for part, (i, block) in enumerate(parts):
                 u, e = divmod(i, 2)
                 for b in range(H_PASSES):
                     nc.tensor.matmul_mx(
-                        out=neg_q[:, half, :],
+                        out=q[:, part, :],
                         lhsT=wb_codes[b, u][:, P * e : P * (e + 1)].bitcast(FP8X4),
                         lhsT_scale=wb_plane[b, u][:, P * e : P * (e + 1)],
-                        rhs=h_codes[k, b][:].bitcast(FP8X4),
-                        rhs_scale=h_plane[k, b][:],
+                        rhs=h_codes[block, b][:].bitcast(FP8X4),
+                        rhs_scale=h_plane[block, b][:],
                         start=(b == 0),
                         stop=(b == H_PASSES - 1),
                     )
-            flat = neg_q[:].rearrange("p e j -> p (e j)")
+            q_flat = q[:].rearrange("p e j -> p (e j)")
+            width = len(parts) * BLOCK
             gated = sb([P, width], F32, f"gated{n}")
-            nc.scalar.activation(gated[:], flat, ACT.Silu)
+            nc.scalar.activation(gated[:], q_flat, ACT.Silu, scale=2.0)
             drive = sb([P, width], F32, f"drive{n}")
-            nc.scalar.activation(drive[:], flat, ACT.Tanh, scale=0.5)
-            rest = sb([P, width], F32, f"square{n}")
+            nc.scalar.activation(drive[:], q_flat, ACT.Tanh)
+            rest = sb([P, width], F32, f"rest{n}")
             nc.scalar.activation(rest[:], drive[:], ACT.Identity, scale=-1.0, bias=1.0)
-            steps.append((blocks, tiles, gated, rest))
+            steps.append((blocks, step_pages, gated, rest))
             return n
 
-        def slope(n, tag=None):
-            blocks, tiles, gated, rest = steps[n]
-            y = sb([P, gated.shape[1]], F32, f"y{n}", tag)
-            if n < ON_VECTOR:
-                nc.vector.tensor_tensor(y[:], gated[:], rest[:], ALU.mult)
-                return blocks, tiles, y, True
+        def slope_on_vector(n):
+            blocks, step_pages, gated, rest = steps[n]
+            y = sb([P, gated.shape[1]], F32, f"y{n}")
+            nc.vector.tensor_tensor(y[:], gated[:], rest[:], ALU.mult)
+            return blocks, step_pages, y, False
+
+        def slope_on_gpsimd(n, weighted):
+            blocks, step_pages, gated, rest = steps[n]
             lo, hi = blocks[0] * BLOCK, (blocks[-1] + 1) * BLOCK
-            bare = sb([P, gated.shape[1]], F32, f"bare{n}")
+            values = sb([P, gated.shape[1]], F32, f"values{n}")
+            y = sb([P, gated.shape[1]], F32, f"y{n}") if weighted else values
             for at in range(0, gated.shape[1], BLOCK):
                 cols = slice(at, at + BLOCK)
                 entry = lo + at % (hi - lo)
-                nc.gpsimd.tensor_tensor(bare[:, cols], gated[:, cols], rest[:, cols], ALU.mult)
-                nc.gpsimd.tensor_tensor(y[:, cols], bare[:, cols], weight[:, entry : entry + BLOCK], ALU.mult)
-            return blocks, tiles, y, False
+                nc.gpsimd.tensor_tensor(y[:, cols], gated[:, cols], rest[:, cols], ALU.mult)
+                if weighted:
+                    nc.gpsimd.tensor_tensor(values[:, cols], y[:, cols], weight[:, entry : entry + BLOCK], ALU.mult)
+            return blocks, step_pages, values, weighted
 
-        def put(blocks, tiles, y, unweighted):
+        out_pages = out.rearrange("(p i) t -> i p t", i=PACK)
+
+        def put(blocks, step_pages, values, weighted):
             lo, hi = blocks[0] * BLOCK, (blocks[-1] + 1) * BLOCK
-            for n, i in enumerate(tiles):
-                slots = pages[i][:].indirect(place[:, lo // 16 : hi // 16])
-                values = y[:, n * (hi - lo) : (n + 1) * (hi - lo)]
-                if unweighted:
-                    nc.vector.tensor_tensor(slots, values, weight[:, lo:hi], ALU.mult)
+            for part, i in enumerate(step_pages):
+                slots = pages[i][:].indirect(place[:, lo // GROUP : hi // GROUP])
+                page_values = values[:, part * (hi - lo) : (part + 1) * (hi - lo)]
+                if weighted:
+                    nc.vector.tensor_copy(slots, page_values)
                 else:
-                    nc.vector.tensor_copy(slots, values)
+                    nc.vector.tensor_tensor(slots, page_values, weight[:, lo:hi], ALU.mult)
                 if hi == S:
-                    nc.sync.dma_start(out.rearrange("(p i) t -> i p t", i=PACK)[i], pages[i][:])
+                    nc.sync.dma_start(out_pages[i], pages[i][:])
 
         low, high = (0, 1), (2, 3)
+        last_pass = H_PASSES - 1
+        last_low = f"wb_bf{last_pass}_0"
+
         first_product(0)
         for b in range(H_PASSES):
             quantise_wb(b, 0)
-        first = second_product((0,), (0,))
-        second = second_product((0,), (1,))
-        for b in range(H_PASSES - 1):
+        opening = [second_product((0,), (i,)) for i in low]
+        for b in range(last_pass):
             quantise_wb(b, 1)
-        quantise_wb(H_PASSES - 1, 1, "wb_bf2_0")
-        gather_words(1, 2 * BLOCK, S, "wb_bf2_0")
-        later = second_product((0,), high)
+        quantise_wb(last_pass, 1, last_low)
+        gather_words(1, 2 * BLOCK, 3 * BLOCK, last_low)
+        opening.append(second_product((0,), high))
         first_product(1)
-        step = slope(first)
-        clear_page(3, f"square{first}")
-        put(*step)
-        put(*slope(second))
-        put(*slope(later))
+        first_values = slope_on_vector(opening[0])
+        clear_page(3, sb([P, T2], F32, "page3", f"rest{opening[0]}"))
+        put(*first_values)
+        for n in opening[1:]:
+            put(*slope_on_vector(n))
+
         first_product(2)
-        put(*slope(second_product((1,), low)))
-        first_product(3, (0, 1))
-        step = slope(second_product((1,), high))
-        first_product(3, (2,))
-        put(*step)
-        for blocks, tiles in (((2,), low), ((3,), low), ((2, 3), (2,)), ((2, 3), (3,))):
-            put(*slope(second_product(blocks, tiles)))
+        put(*slope_on_gpsimd(second_product((1,), low), True))
+        first_product(3)
+        for blocks, step_pages in (((1,), high), ((2,), low), ((3,), low), ((2, 3), (2,))):
+            put(*slope_on_gpsimd(second_product(blocks, step_pages), True))
+        put(*slope_on_gpsimd(second_product((2, 3), (3,)), False))

@@ -40,9 +40,13 @@ def tile_list_armband_gain_sensitivity_kernel(
         lists = ctx.enter_context(tc.tile_pool(name="lists", bufs=1))
         keep = ctx.enter_context(tc.tile_pool(name="keep", bufs=1))
         placed = ctx.enter_context(tc.tile_pool(name="placed", bufs=1))
+        held = ctx.enter_context(tc.tile_pool(name="held", bufs=1))
+        spots = {"wb_bf2_0": 0, "h_codes1": 2 * 2 * P * PACK - ALIGN}
         psum = ctx.enter_context(tc.psum_pool(name="psum", bufs=1))
 
         def sb(shape, dtype, name, takes_over=None):
+            if name in spots:
+                return held.tile(shape, dtype, name=name, align_bytes=ALIGN, offset=spots[name])
             return keep.tile(shape, dtype, name=name, tag=takes_over or name, align_bytes=ALIGN)
 
         pick = lists.tile([P, S // GROUP], U16, name="pick")
@@ -54,13 +58,14 @@ def tile_list_armband_gain_sensitivity_kernel(
         scale_window = sb([P, T], U8, "scale_window")
         wa_scale_raw = placed.tile([P, K_PASSES, H], U8, name="wa_scale_raw", align_bytes=ALIGN, offset=wa_scale_at)
         scale_got = sb([P, S], U8, "scale_got")
-        v_plane = [sb([P, S], U8, f"v_plane{a}") for a in range(K_PASSES)]
+        half = S // 2
+        v_plane = [sb([P, half], U8, "v_plane0"), sb([P, S], U8, "v_plane1")]
 
         zero_a = sb([P, 1], F32, "zero_a", "table0")
         zero_b = sb([P, 1], F32, "zero_b", "wa_raw")
         zero_sum = sb([P, 1], F32, "zero_sum")
         silu_in = sb([P, 1], F32, "silu_in", "table1")
-        relu_bias = sb([P, 1], F32, "relu_bias")
+        zero_bias = sb([P, 1], F32, "zero_bias")
 
         def clear_words(words):
             odd = words.shape[1] // 2 + 1
@@ -73,9 +78,7 @@ def tile_list_armband_gain_sensitivity_kernel(
         nc.vector.tensor_tensor(zero_sum[:], zero_a[:], zero_b[:], ALU.add)
         clear_words(wa_scale_raw[:].rearrange("p a c -> p (a c)").bitcast(I32))
         nc.vector.tensor_copy(silu_in[:], zero_sum[:])
-        for a in range(K_PASSES):
-            clear_words(v_plane[a][:].bitcast(I32))
-        nc.scalar.activation(relu_bias[:], silu_in[:], ACT.Silu)
+        nc.scalar.activation(zero_bias[:], silu_in[:], ACT.Silu)
 
         nc.sync.dma_start(pick[:], offs)
         nc.sync.dma_start(place[:], offs2)
@@ -85,39 +88,14 @@ def tile_list_armband_gain_sensitivity_kernel(
             nc.sync.dma_start(window32[32 * d + SHIFT : 32 * d + SHIFT + 4, :], tab_scale_rows[0, 4 * d : 4 * d + 4, :])
         nc.sync.dma_start(window32[SPARE:P:8, :], tab_scale_rows[1])
         wa_raw = sb([P, K_PASSES, H // 2], I32, "wa_raw")
-        nc.sync.dma_start(wa_raw[:], wa_words.bitcast(I32).rearrange("a p c -> p a c"))
-        table = [sb([P, T], I32, f"table{a}") for a in range(K_PASSES)]
         table_rows = [tab_words[a].rearrange("p t i -> p (t i)").bitcast(I32) for a in range(K_PASSES)]
+        table = [sb([P, T], I32, "table0")]
         nc.sync.dma_start(table[0][:], table_rows[0])
+        nc.sync.dma_start(wa_raw[:], wa_words.bitcast(I32).rearrange("a p c -> p a c"))
         wa_scale_rows = wa_scales.bitcast(I32).rearrange("a q c -> q a c")
         wa_scale32 = wa_scale_raw[:].bitcast(I32)
         for d in range(QUADS):
             nc.sync.dma_start(wa_scale32[32 * d : 32 * d + 4, :, :], wa_scale_rows[4 * d : 4 * d + 4, :, :])
-        nc.sync.dma_start(table[1][:], table_rows[1])
-
-        pages = {}
-
-        def clear_page(i, page):
-            pages[i] = page
-            for lo in range(0, T2, T2 // 2):
-                nc.gpsimd.memset(page[:, lo : lo + T2 // 2], 0.0)
-
-        clear_page(0, sb([P, T2], F32, "page0"))
-        clear_page(1, sb([P, T2], F32, "page1"))
-
-        nc.vector.tensor_copy(scale_got[:], scale_window[:].indirect(pick[:]))
-        got32 = scale_got[:].bitcast(I32)
-        nc.sync.dma_start(v_plane[0][:].bitcast(I32)[0:MOVED, :], got32[SHIFT : SHIFT + MOVED, :])
-        for row in range(4):
-            nc.sync.dma_start(v_plane[1][:].bitcast(I32)[row:P:32, :], got32[8 * row + SPARE : P : 32, :])
-
-        wa_codes = sb([P, K_PASSES, 2 * H], U8, "wa_codes")
-        wa_plane = sb([P, K_PASSES, H], U8, "wa_plane")
-        for dealt, raw in ((wa_codes, wa_raw[:]), (wa_plane, wa_scale32)):
-            nc.vector.tensor_copy(
-                dealt[:].bitcast(I32).rearrange("p a (b t q w) -> p (a b) t q w", b=H_PASSES, t=PACK, q=16),
-                raw.rearrange("p a (b q t w) -> p (a b) t q w", b=H_PASSES, t=PACK, q=16),
-            )
 
         wb_rows = wb.rearrange("(b q t s) n -> b t q s n", b=H_PASSES, q=16, t=PACK)
         wb_raw = []
@@ -127,13 +105,25 @@ def tile_list_armband_gain_sensitivity_kernel(
                 nc.sync.dma_start(rows[:, t, :], wb_rows[len(wb_raw), t])
             wb_raw.append(rows)
 
-        load_wb(sb([P, PACK, N], F32, "wb_raw0", "scale_window"))
-        load_wb(sb([P, PACK, N], F32, "wb_raw1", "wa_raw"))
-        load_wb(placed.tile([P, PACK, N], F32, name="wb_raw2", align_bytes=ALIGN, offset=wb_last_at))
-        weight = sb([P, S], F32, "weight", "scale_got")
-        nc.sync.dma_start(weight[:], wgo)
+        table.append(sb([P, T], I32, "table1"))
+        nc.sync.dma_start(table[1][:], table_rows[1])
 
-        clear_page(2, placed.tile([P, T2], F32, name="page2", align_bytes=ALIGN, offset=0))
+        pages = {}
+
+        def clear_page(i, page):
+            pages[i] = page
+            for lo in range(0, T2, T2 // 2):
+                nc.gpsimd.memset(page[:, lo : lo + T2 // 2], 0.0)
+
+        for i in range(PACK - 1):
+            clear_page(i, sb([P, T2], F32, f"page{i}"))
+
+        nc.vector.tensor_copy(scale_got[:], scale_window[:].indirect(pick[:]))
+        got32 = scale_got[:].bitcast(I32)
+        nc.sync.dma_start(v_plane[0][:].bitcast(I32)[0:MOVED, :], got32[SHIFT : SHIFT + MOVED, 0 : half // 4])
+        for row in range(4):
+            nc.sync.dma_start(v_plane[1][:].bitcast(I32)[row:P:32, :], got32[8 * row + SPARE : P : 32, :])
+        load_wb(sb([P, PACK, N], F32, "wb_raw0", "scale_window"))
 
         v_words = {}
 
@@ -144,147 +134,181 @@ def tile_list_armband_gain_sensitivity_kernel(
                 v_words[a, j] = got[:, j - lo : j - lo + SUB]
 
         gather_words(0, 0, S)
-        for block in (0, 1, 3):
-            gather_words(1, block * BLOCK, (block + 1) * BLOCK)
 
-        h_codes, h_plane = {}, {}
+        wa_codes = sb([P, K_PASSES, 2 * H], U8, "wa_codes")
+        wa_plane = sb([P, K_PASSES, H], U8, "wa_plane")
+        for dealt, raw in ((wa_codes, wa_raw[:]), (wa_plane, wa_scale32)):
+            nc.vector.tensor_copy(
+                dealt[:].bitcast(I32).rearrange("p a (b t q w) -> p (a b) t q w", b=H_PASSES, t=PACK, q=16),
+                raw.rearrange("p a (b q t w) -> p (a b) t q w", b=H_PASSES, t=PACK, q=16),
+            )
+
+        load_wb(sb([P, PACK, N], F32, "wb_raw1", "wa_raw"))
+        load_wb(placed.tile([P, PACK, N], F32, name="wb_raw2", align_bytes=ALIGN, offset=wb_last_at))
+
+        clear_page(PACK - 1, placed.tile([P, T2], F32, name="page3", align_bytes=ALIGN, offset=0))
+
+        gather_words(1, 0, BLOCK)
+        gather_words(1, BLOCK, S)
+        weight = sb([P, S], F32, "weight", "table1")
+        nc.sync.dma_start(weight[:], wgo)
+
+        v_scale = {(1, j): v_plane[1][:, j : j + SUB] for j in range(0, S, SUB)}
+        for j in range(0, half, SUB):
+            v_scale[0, j] = v_plane[0][:, j : j + SUB]
+
+        def move_late_scales():
+            late = sb([P, half], U8, "v_plane_late", "scale_window")
+            nc.sync.dma_start(late[:].bitcast(I32)[0:MOVED, :], got32[SHIFT : SHIFT + MOVED, half // 4 :])
+            for j in range(half, S, SUB):
+                v_scale[0, j] = late[:, j - half : j - half + SUB]
+
+        h_codes, h_plane, block_codes = {}, {}, {}
         filled = []
 
-        def first_product(block):
+        def next_bank():
+            filled.append(len(filled) % BANKS)
+            return f"bank{filled[-1]}"
+
+        def first_matmuls(acc, b, j, table_passes, whole_bank):
+            for t, a in whole_bank:
+                if a in table_passes:
+                    col = 512 * b + P * t
+                    nc.tensor.matmul_mx(
+                        out=acc[:, t, :],
+                        lhsT=wa_codes[:, a, 2 * col : 2 * (col + P)].bitcast(FP4X4),
+                        lhsT_scale=wa_plane[:, a, col : col + P],
+                        rhs=v_words[a, j].bitcast(FP8X4),
+                        rhs_scale=v_scale[a, j],
+                        start=(a == 0),
+                        stop=(a == K_PASSES - 1),
+                    )
+
+        def first_product(block, passes, early=False, behind=None):
             lo = block * BLOCK
-            for b in range(H_PASSES):
-                h_codes[block, b] = sb([P, BLOCK], U32, f"h_codes{block}_{b}")
+            whole_bank = [(t, a) for t in range(PACK) for a in range(K_PASSES)]
+            accs = {}
+            if early:
+                for b in passes:
+                    for j in range(lo, lo + BLOCK, SUB):
+                        accs[b, j] = psum.tile([P, PACK, SUB], F32, name="acc", tag=next_bank())
+                        first_matmuls(accs[b, j], b, j, (0,), whole_bank)
+            for b in passes:
+                if b == 0:
+                    block_codes[block] = sb([P, H_PASSES * BLOCK], U32, f"h_codes{block}", behind)
+                h_codes[block, b] = block_codes[block][:, b * BLOCK : (b + 1) * BLOCK]
                 h_plane[block, b] = sb([P, BLOCK], U8, f"h_plane{block}_{b}")
                 h_bf = sb([P, BLOCK, PACK], BF16, f"h_bf{block}_{b}")
                 for j in range(lo, lo + BLOCK, SUB):
-                    acc = psum.tile([P, PACK, SUB], F32, name="acc", tag=f"bank{len(filled) % FIRST_BANKS}")
-                    filled.append(j)
-                    for t in range(PACK):
-                        col = 512 * b + P * t
-                        for a in range(K_PASSES):
-                            nc.tensor.matmul_mx(
-                                out=acc[:, t, :],
-                                lhsT=wa_codes[:, a, 2 * col : 2 * (col + P)].bitcast(FP4X4),
-                                lhsT_scale=wa_plane[:, a, col : col + P],
-                                rhs=v_words[a, j].bitcast(FP8X4),
-                                rhs_scale=v_plane[a][:, j : j + SUB],
-                                start=(a == 0),
-                                stop=(a == K_PASSES - 1),
-                            )
+                    if early:
+                        acc = accs[b, j]
+                        first_matmuls(acc, b, j, (1,), whole_bank)
+                    else:
+                        acc = psum.tile([P, PACK, SUB], F32, name="acc", tag=next_bank())
+                        first_matmuls(acc, b, j, (0, 1), whole_bank)
                     nc.scalar.activation(
                         h_bf[:, j - lo : j - lo + SUB, :].rearrange("p (j e) t -> p j t e", e=2),
                         acc[:].rearrange("p t (j e) -> p j t e", e=2),
                         ACT.Relu,
-                        bias=relu_bias[:],
+                        bias=zero_bias[:] if (b, j) == (0, 0) else 0.0,
                     )
                 nc.vector.quantize_mx(
-                    out=h_codes[block, b][:].bitcast(FP8X4),
+                    out=h_codes[block, b].bitcast(FP8X4),
                     scales=h_plane[block, b][:],
                     in_=h_bf[:].rearrange("p j t -> p (j t)"),
                 )
 
         wb_codes, wb_plane = {}, {}
 
-        def quantise_wb(b, u, takes_over=None):
-            rounded = sb([P, 2, P, PACK], BF16, f"wb_bf{b}_{u}", takes_over)
+        def quantise_wb(b, first_page, count):
+            rounded = sb([P, count, P, PACK], BF16, f"wb_bf{b}_{first_page}")
             nc.vector.tensor_copy(
-                rounded[:].rearrange("p e m t -> p m e t"),
-                wb_raw[b][:].rearrange("p t (m i) -> p m i t", i=PACK)[:, :, 2 * u : 2 * u + 2, :],
+                rounded[:].rearrange("p i m t -> p m i t"),
+                wb_raw[b][:].rearrange("p t (m i) -> p m i t", i=PACK)[:, :, first_page : first_page + count, :],
             )
-            wb_codes[b, u] = sb([P, 2 * P], U32, f"wb_codes{b}_{u}")
-            wb_plane[b, u] = sb([P, 2 * P], U8, f"wb_plane{b}_{u}")
+            codes = sb([P, count * P], U32, f"wb_codes{b}_{first_page}")
+            plane = sb([P, count * P], U8, f"wb_plane{b}_{first_page}")
             nc.vector.quantize_mx(
-                out=wb_codes[b, u][:].bitcast(FP8X4),
-                scales=wb_plane[b, u][:],
-                in_=rounded[:].rearrange("p e m t -> p (e m t)"),
+                out=codes[:].bitcast(FP8X4),
+                scales=plane[:],
+                in_=rounded[:].rearrange("p i m t -> p (i m t)"),
             )
+            for e in range(count):
+                wb_codes[b, first_page + e] = codes[:, P * e : P * (e + 1)]
+                wb_plane[b, first_page + e] = plane[:, P * e : P * (e + 1)]
 
         steps = []
+        out_pages = out.rearrange("(p i) t -> i p t", i=PACK)
 
-        def second_product(blocks, step_pages):
+        def second_product(blocks, step_pages, fused=False):
             n = len(steps)
+            steps.append(n)
             parts = [(i, block) for i in step_pages for block in blocks]
-            bank = FIRST_BANKS + n % (BANKS - FIRST_BANKS)
-            q = psum.tile([P, len(parts), BLOCK], F32, name="q", tag=f"bank{bank}")
+            q = psum.tile([P, len(parts), BLOCK], F32, name="q", tag=next_bank())
             for part, (i, block) in enumerate(parts):
-                u, e = divmod(i, 2)
                 for b in range(H_PASSES):
                     nc.tensor.matmul_mx(
                         out=q[:, part, :],
-                        lhsT=wb_codes[b, u][:, P * e : P * (e + 1)].bitcast(FP8X4),
-                        lhsT_scale=wb_plane[b, u][:, P * e : P * (e + 1)],
-                        rhs=h_codes[block, b][:].bitcast(FP8X4),
+                        lhsT=wb_codes[b, i].bitcast(FP8X4),
+                        lhsT_scale=wb_plane[b, i],
+                        rhs=h_codes[block, b].bitcast(FP8X4),
                         rhs_scale=h_plane[block, b][:],
                         start=(b == 0),
                         stop=(b == H_PASSES - 1),
                     )
             q_flat = q[:].rearrange("p e j -> p (e j)")
             width = len(parts) * BLOCK
+            lo, hi = blocks[0] * BLOCK, (blocks[-1] + 1) * BLOCK
+            drive = sb([P, width], F32, f"drive{n}", f"drive{n % 2}")
+            nc.scalar.activation(drive[:], q_flat, ACT.Tanh)
             gated = sb([P, width], F32, f"gated{n}")
             nc.scalar.activation(gated[:], q_flat, ACT.Silu, scale=2.0)
-            drive = sb([P, width], F32, f"drive{n}")
-            nc.scalar.activation(drive[:], q_flat, ACT.Tanh)
             rest = sb([P, width], F32, f"rest{n}")
             nc.scalar.activation(rest[:], drive[:], ACT.Identity, scale=-1.0, bias=1.0)
-            steps.append((blocks, step_pages, gated, rest))
-            return n
-
-        def slope_on_vector(n):
-            blocks, step_pages, gated, rest = steps[n]
-            y = sb([P, gated.shape[1]], F32, f"y{n}")
-            nc.vector.tensor_tensor(y[:], gated[:], rest[:], ALU.mult)
-            return blocks, step_pages, y, False
-
-        def slope_on_gpsimd(n, weighted):
-            blocks, step_pages, gated, rest = steps[n]
-            lo, hi = blocks[0] * BLOCK, (blocks[-1] + 1) * BLOCK
-            values = sb([P, gated.shape[1]], F32, f"values{n}")
-            y = sb([P, gated.shape[1]], F32, f"y{n}") if weighted else values
-            for at in range(0, gated.shape[1], BLOCK):
-                cols = slice(at, at + BLOCK)
-                entry = lo + at % (hi - lo)
-                nc.gpsimd.tensor_tensor(y[:, cols], gated[:, cols], rest[:, cols], ALU.mult)
-                if weighted:
-                    nc.gpsimd.tensor_tensor(values[:, cols], y[:, cols], weight[:, entry : entry + BLOCK], ALU.mult)
-            return blocks, step_pages, values, weighted
-
-        out_pages = out.rearrange("(p i) t -> i p t", i=PACK)
-
-        def put(blocks, step_pages, values, weighted):
-            lo, hi = blocks[0] * BLOCK, (blocks[-1] + 1) * BLOCK
+            values = sb([P, width], F32, f"values{n}")
+            weighted = gated if fused else sb([P, width], F32, f"weighted{n}")
+            if not fused:
+                by_page = [P, len(step_pages), hi - lo]
+                nc.gpsimd.tensor_tensor(
+                    weighted[:].rearrange("p (e j) -> p e j", e=len(step_pages)),
+                    gated[:].rearrange("p (e j) -> p e j", e=len(step_pages)),
+                    weight[:, lo:hi].unsqueeze(1).to_broadcast(by_page),
+                    ALU.mult,
+                )
+            for at in range(0, width, hi - lo):
+                cols = slice(at, at + hi - lo)
+                nc.gpsimd.tensor_tensor(values[:, cols], weighted[:, cols], rest[:, cols], ALU.mult)
             for part, i in enumerate(step_pages):
                 slots = pages[i][:].indirect(place[:, lo // GROUP : hi // GROUP])
                 page_values = values[:, part * (hi - lo) : (part + 1) * (hi - lo)]
-                if weighted:
-                    nc.vector.tensor_copy(slots, page_values)
-                else:
+                if fused:
                     nc.vector.tensor_tensor(slots, page_values, weight[:, lo:hi], ALU.mult)
+                else:
+                    nc.vector.tensor_copy(slots, page_values)
                 if hi == S:
                     nc.sync.dma_start(out_pages[i], pages[i][:])
 
         low, high = (0, 1), (2, 3)
-        last_pass = H_PASSES - 1
-        last_low = f"wb_bf{last_pass}_0"
+        every_pass = range(H_PASSES)
 
-        first_product(0)
-        for b in range(H_PASSES):
-            quantise_wb(b, 0)
-        opening = [second_product((0,), (i,)) for i in low]
-        for b in range(last_pass):
-            quantise_wb(b, 1)
-        quantise_wb(last_pass, 1, last_low)
-        gather_words(1, 2 * BLOCK, 3 * BLOCK, last_low)
-        opening.append(second_product((0,), high))
-        first_product(1)
-        first_values = slope_on_vector(opening[0])
-        clear_page(3, sb([P, T2], F32, "page3", f"rest{opening[0]}"))
-        put(*first_values)
-        for n in opening[1:]:
-            put(*slope_on_vector(n))
-
-        first_product(2)
-        put(*slope_on_gpsimd(second_product((1,), low), True))
-        first_product(3)
-        for blocks, step_pages in (((1,), high), ((2,), low), ((3,), low), ((2, 3), (2,))):
-            put(*slope_on_gpsimd(second_product(blocks, step_pages), True))
-        put(*slope_on_gpsimd(second_product((2, 3), (3,)), False))
+        first_product(0, every_pass)
+        quantise_wb(0, 0, PACK)
+        move_late_scales()
+        quantise_wb(1, 0, PACK)
+        quantise_wb(2, 0, 2)
+        second_product((0,), (0,))
+        second_product((0,), (1,))
+        quantise_wb(2, 2, 2)
+        first_product(1, every_pass)
+        second_product((0,), (2,))
+        second_product((0,), (3,))
+        first_product(2, (0,))
+        second_product((1,), low)
+        first_product(2, (1, 2))
+        second_product((1,), high)
+        first_product(3, every_pass)
+        second_product((2,), low)
+        second_product((2,), (2,))
+        second_product((3,), (0,))
+        second_product((3,), (1, 2))
+        second_product((2, 3), (3,), fused=True)

@@ -150,8 +150,9 @@ def tile_list_armband_gain_sensitivity_kernel(
 
         gather_words(1, 0, BLOCK)
         gather_words(1, BLOCK, S)
-        weight = sb([P, S], F32, "weight", "table1")
-        nc.sync.dma_start(weight[:], wgo)
+        weight = sb([P, S // BLOCK, 2, BLOCK], F32, "weight", "table1")
+        for e in range(2):
+            nc.sync.dma_start(weight[:, :, e, :], wgo.rearrange("p (k j) -> p k j", j=BLOCK))
 
         v_scale = {(1, j): v_plane[1][:, j : j + SUB] for j in range(0, S, SUB)}
         for j in range(0, half, SUB):
@@ -167,7 +168,7 @@ def tile_list_armband_gain_sensitivity_kernel(
         filled = []
 
         def next_bank():
-            filled.append(len(filled) % BANKS)
+            filled.append(len(filled) % FIRST_BANKS)
             return f"bank{filled[-1]}"
 
         def first_matmuls(acc, b, j, table_passes, whole_bank):
@@ -244,7 +245,7 @@ def tile_list_armband_gain_sensitivity_kernel(
             n = len(steps)
             steps.append(n)
             parts = [(i, block) for i in step_pages for block in blocks]
-            q = psum.tile([P, len(parts), BLOCK], F32, name="q", tag=next_bank())
+            q = psum.tile([P, len(parts), BLOCK], F32, name="q", tag=f"bank{FIRST_BANKS + n % (BANKS - FIRST_BANKS)}")
             for part, (i, block) in enumerate(parts):
                 for b in range(H_PASSES):
                     nc.tensor.matmul_mx(
@@ -258,7 +259,6 @@ def tile_list_armband_gain_sensitivity_kernel(
                     )
             q_flat = q[:].rearrange("p e j -> p (e j)")
             width = len(parts) * BLOCK
-            lo, hi = blocks[0] * BLOCK, (blocks[-1] + 1) * BLOCK
             drive = sb([P, width], F32, f"drive{n}", f"drive{n % 2}")
             nc.scalar.activation(drive[:], q_flat, ACT.Tanh)
             gated = sb([P, width], F32, f"gated{n}")
@@ -267,25 +267,22 @@ def tile_list_armband_gain_sensitivity_kernel(
             nc.scalar.activation(rest[:], drive[:], ACT.Identity, scale=-1.0, bias=1.0)
             values = sb([P, width], F32, f"values{n}")
             weighted = gated if fused else sb([P, width], F32, f"weighted{n}")
-            if not fused:
-                by_page = [P, len(step_pages), hi - lo]
-                nc.gpsimd.tensor_tensor(
-                    weighted[:].rearrange("p (e j) -> p e j", e=len(step_pages)),
-                    gated[:].rearrange("p (e j) -> p e j", e=len(step_pages)),
-                    weight[:, lo:hi].unsqueeze(1).to_broadcast(by_page),
-                    ALU.mult,
-                )
-            for at in range(0, width, hi - lo):
-                cols = slice(at, at + hi - lo)
+            if len(blocks) > 1 and not fused:
+                for part, block in enumerate(blocks):
+                    cols = slice(part * BLOCK, (part + 1) * BLOCK)
+                    nc.gpsimd.tensor_tensor(weighted[:, cols], gated[:, cols], weight[:, block, 0, :], ALU.mult)
+            elif not fused:
+                twice = weight[:, blocks[0]].rearrange("p e j -> p (e j)")
+                nc.gpsimd.tensor_tensor(weighted[:], gated[:], twice[:, 0:width], ALU.mult)
+            for part, (i, block) in enumerate(parts):
+                cols = slice(part * BLOCK, (part + 1) * BLOCK)
                 nc.gpsimd.tensor_tensor(values[:, cols], weighted[:, cols], rest[:, cols], ALU.mult)
-            for part, i in enumerate(step_pages):
-                slots = pages[i][:].indirect(place[:, lo // GROUP : hi // GROUP])
-                page_values = values[:, part * (hi - lo) : (part + 1) * (hi - lo)]
+                slots = pages[i][:].indirect(place[:, block * BLOCK // GROUP : (block + 1) * BLOCK // GROUP])
                 if fused:
-                    nc.vector.tensor_tensor(slots, page_values, weight[:, lo:hi], ALU.mult)
+                    nc.vector.tensor_tensor(slots, values[:, cols], weight[:, block, 0, :], ALU.mult)
                 else:
-                    nc.vector.tensor_copy(slots, page_values)
-                if hi == S:
+                    nc.vector.tensor_copy(slots, values[:, cols])
+                if block == S // BLOCK - 1:
                     nc.sync.dma_start(out_pages[i], pages[i][:])
 
         low, high = (0, 1), (2, 3)
@@ -299,16 +296,13 @@ def tile_list_armband_gain_sensitivity_kernel(
         second_product((0,), (0,))
         second_product((0,), (1,))
         quantise_wb(2, 2, 2)
+        second_product((0,), high)
         first_product(1, every_pass)
-        second_product((0,), (2,))
-        second_product((0,), (3,))
-        first_product(2, (0,))
+        first_product(2, every_pass)
         second_product((1,), low)
-        first_product(2, (1, 2))
-        second_product((1,), high)
         first_product(3, every_pass)
+        second_product((1,), high)
         second_product((2,), low)
-        second_product((2,), (2,))
-        second_product((3,), (0,))
-        second_product((3,), (1, 2))
+        second_product((3,), low)
+        second_product((2, 3), (2,))
         second_product((2, 3), (3,), fused=True)

@@ -150,9 +150,8 @@ def tile_list_armband_gain_sensitivity_kernel(
 
         gather_words(1, 0, BLOCK)
         gather_words(1, BLOCK, S)
-        weight = sb([P, S // BLOCK, 2, BLOCK], F32, "weight", "table1")
-        for e in range(2):
-            nc.sync.dma_start(weight[:, :, e, :], wgo.rearrange("p (k j) -> p k j", j=BLOCK))
+        weight = sb([P, S], F32, "weight", "table1")
+        nc.sync.dma_start(weight[:], wgo)
 
         v_scale = {(1, j): v_plane[1][:, j : j + SUB] for j in range(0, S, SUB)}
         for j in range(0, half, SUB):
@@ -223,9 +222,10 @@ def tile_list_armband_gain_sensitivity_kernel(
 
         def quantise_wb(b, first_page, count):
             rounded = sb([P, count, P, PACK], BF16, f"wb_bf{b}_{first_page}")
-            nc.vector.tensor_copy(
+            nc.vector.tensor_scalar_mul(
                 rounded[:].rearrange("p i m t -> p m i t"),
                 wb_raw[b][:].rearrange("p t (m i) -> p m i t", i=PACK)[:, :, first_page : first_page + count, :],
+                -1.0,
             )
             codes = sb([P, count * P], U32, f"wb_codes{b}_{first_page}")
             plane = sb([P, count * P], U8, f"wb_plane{b}_{first_page}")
@@ -238,10 +238,10 @@ def tile_list_armband_gain_sensitivity_kernel(
                 wb_codes[b, first_page + e] = codes[:, P * e : P * (e + 1)]
                 wb_plane[b, first_page + e] = plane[:, P * e : P * (e + 1)]
 
-        steps = []
+        steps, done = [], []
         out_pages = out.rearrange("(p i) t -> i p t", i=PACK)
 
-        def second_product(blocks, step_pages, fused=False):
+        def second_product(blocks, step_pages, on_vector=1, fused=False):
             n = len(steps)
             steps.append(n)
             parts = [(i, block) for i in step_pages for block in blocks]
@@ -257,33 +257,50 @@ def tile_list_armband_gain_sensitivity_kernel(
                         start=(b == 0),
                         stop=(b == H_PASSES - 1),
                     )
-            q_flat = q[:].rearrange("p e j -> p (e j)")
-            width = len(parts) * BLOCK
-            drive = sb([P, width], F32, f"drive{n}", f"drive{n % 2}")
-            nc.scalar.activation(drive[:], q_flat, ACT.Tanh)
-            gated = sb([P, width], F32, f"gated{n}")
-            nc.scalar.activation(gated[:], q_flat, ACT.Silu, scale=2.0)
-            rest = sb([P, width], F32, f"rest{n}")
-            nc.scalar.activation(rest[:], drive[:], ACT.Identity, scale=-1.0, bias=1.0)
-            values = sb([P, width], F32, f"values{n}")
-            weighted = gated if fused else sb([P, width], F32, f"weighted{n}")
-            if len(blocks) > 1 and not fused:
-                for part, block in enumerate(blocks):
-                    cols = slice(part * BLOCK, (part + 1) * BLOCK)
-                    nc.gpsimd.tensor_tensor(weighted[:, cols], gated[:, cols], weight[:, block, 0, :], ALU.mult)
-            elif not fused:
-                twice = weight[:, blocks[0]].rearrange("p e j -> p (e j)")
-                nc.gpsimd.tensor_tensor(weighted[:], gated[:], twice[:, 0:width], ALU.mult)
-            for part, (i, block) in enumerate(parts):
-                cols = slice(part * BLOCK, (part + 1) * BLOCK)
-                nc.gpsimd.tensor_tensor(values[:, cols], weighted[:, cols], rest[:, cols], ALU.mult)
-                slots = pages[i][:].indirect(place[:, block * BLOCK // GROUP : (block + 1) * BLOCK // GROUP])
-                if fused:
-                    nc.vector.tensor_tensor(slots, values[:, cols], weight[:, block, 0, :], ALU.mult)
+            drive = sb([P, len(parts), BLOCK], F32, f"drive{n}", f"drive{n % 2}")
+            nc.scalar.activation(drive[:], q[:], ACT.Tanh)
+            slope = sb([P, on_vector, BLOCK], F32, f"slope{n}") if on_vector else None
+            others = len(parts) - on_vector
+            if others:
+                gated = sb([P, others, BLOCK], F32, f"gated{n}")
+                nc.scalar.activation(gated[:], q[:, on_vector:], ACT.Silu, scale=-2.0)
+                rest = sb([P, others, BLOCK], F32, f"rest{n}")
+                nc.scalar.activation(rest[:], drive[:, on_vector:], ACT.Identity, bias=1.0)
+            if on_vector:
+                square = sb([P, on_vector, BLOCK], F32, f"square{n}")
+                nc.scalar.activation(square[:], drive[:, 0:on_vector], ACT.Square)
+                nc.vector.scalar_tensor_tensor(
+                    slope[:].rearrange("p e j -> p (e j)"),
+                    square[:].rearrange("p e j -> p (e j)"),
+                    1.0,
+                    q[:, 0:on_vector].rearrange("p e j -> p (e j)"),
+                    ALU.subtract,
+                    ALU.mult,
+                )
+            values = sb([P, len(parts), BLOCK], F32, f"values{n}")
+            for part in reversed(range(len(parts))):
+                i, block = parts[part]
+                entries = weight[:, block * BLOCK : (block + 1) * BLOCK]
+                if part < on_vector:
+                    nc.gpsimd.tensor_tensor(values[:, part], slope[:, part], entries, ALU.mult)
+                elif fused:
+                    nc.gpsimd.tensor_tensor(values[:, part], gated[:, part - on_vector], rest[:, part - on_vector], ALU.mult)
                 else:
-                    nc.vector.tensor_copy(slots, values[:, cols])
-                if block == S // BLOCK - 1:
+                    weighted = sb([P, BLOCK], F32, f"weighted{n}_{part}")
+                    nc.gpsimd.tensor_tensor(weighted[:], gated[:, part - on_vector], entries, ALU.mult)
+                    nc.gpsimd.tensor_tensor(values[:, part], weighted[:], rest[:, part - on_vector], ALU.mult)
+                if fused:
+                    continue
+                slots = pages[i][:].indirect(place[:, block * BLOCK // GROUP : (block + 1) * BLOCK // GROUP])
+                nc.vector.tensor_copy(slots, values[:, part])
+                done.append(i)
+                if len([k for k in done if k == i]) == S // BLOCK:
                     nc.sync.dma_start(out_pages[i], pages[i][:])
+            if fused:
+                lo, i = blocks[0] * BLOCK, step_pages[0]
+                slots = pages[i][:].indirect(place[:, lo // GROUP :])
+                nc.vector.tensor_tensor(slots, values[:].rearrange("p e j -> p (e j)"), weight[:, lo:], ALU.mult)
+                nc.sync.dma_start(out_pages[i], pages[i][:])
 
         low, high = (0, 1), (2, 3)
         every_pass = range(H_PASSES)
@@ -294,7 +311,7 @@ def tile_list_armband_gain_sensitivity_kernel(
         quantise_wb(1, 0, PACK)
         quantise_wb(2, 0, 2)
         second_product((0,), (0,))
-        second_product((0,), (1,))
+        second_product((0,), (1,), 0)
         quantise_wb(2, 2, 2)
         second_product((0,), high)
         first_product(1, every_pass)
@@ -305,4 +322,4 @@ def tile_list_armband_gain_sensitivity_kernel(
         second_product((2,), low)
         second_product((3,), low)
         second_product((2, 3), (2,))
-        second_product((2, 3), (3,), fused=True)
+        second_product((2, 3), (3,), 0, fused=True)

@@ -115,8 +115,10 @@ def tile_list_armband_gain_sensitivity_kernel(
             for lo in range(0, T2, T2 // 2):
                 nc.gpsimd.memset(page[:, lo : lo + T2 // 2], 0.0)
 
-        for i in range(PACK - 1):
+        for i in range(2):
             clear_page(i, sb([P, T2], F32, f"page{i}"))
+        pages[2] = sb([P, T2], F32, "page2")
+        clear_words(pages[2][:])
 
         nc.vector.tensor_copy(scale_got[:], scale_window[:].indirect(pick[:]))
         got32 = scale_got[:].bitcast(I32)
@@ -306,20 +308,22 @@ def tile_list_armband_gain_sensitivity_kernel(
         every_pass = range(H_PASSES)
 
         first_product(0, every_pass)
-        quantise_wb(0, 0, PACK)
+        quantise_wb(0, 0, 2)
+        quantise_wb(0, 2, 2)
         move_late_scales()
-        quantise_wb(1, 0, PACK)
+        quantise_wb(1, 0, 2)
         quantise_wb(2, 0, 2)
         second_product((0,), (0,))
         second_product((0,), (1,), 0)
+        quantise_wb(1, 2, 2)
         quantise_wb(2, 2, 2)
-        second_product((0,), high)
+        second_product((0,), high, 0)
         first_product(1, every_pass)
         first_product(2, every_pass)
         second_product((1,), low)
         first_product(3, every_pass)
-        second_product((1,), high)
+        second_product((1,), high, 0)
         second_product((2,), low)
-        second_product((3,), low)
-        second_product((2, 3), (2,))
+        second_product((3,), low, 0)
+        second_product((2, 3), (2,), 0)
         second_product((2, 3), (3,), 0, fused=True)

@@ -41,7 +41,17 @@ def tile_list_armband_gain_sensitivity_kernel(
         keep = ctx.enter_context(tc.tile_pool(name="keep", bufs=1))
         placed = ctx.enter_context(tc.tile_pool(name="placed", bufs=1))
         held = ctx.enter_context(tc.tile_pool(name="held", bufs=1))
-        spots = {"wb_bf2_0": 0, "h_codes1": 2 * 2 * P * PACK - ALIGN}
+        h_bytes = 2 * BLOCK * PACK
+        low_end = 2 * h_bytes + H_PASSES * 4 * BLOCK
+        spots = {
+            "wb_bf2_0": 0,
+            "h_codes1": h_bytes - ALIGN,
+            "h_bf2_2": low_end,
+            "slope2": low_end + h_bytes - ALIGN,
+            "bridge": low_end + 2 * h_bytes,
+            "h_bf3_2": low_end + 2 * h_bytes + 4 * BLOCK - ALIGN,
+            "weighted3_0": low_end + 3 * h_bytes + 4 * BLOCK - 2 * ALIGN,
+        }
         psum = ctx.enter_context(tc.psum_pool(name="psum", bufs=1))
 
         def sb(shape, dtype, name, takes_over=None):
@@ -160,10 +170,12 @@ def tile_list_armband_gain_sensitivity_kernel(
             v_scale[0, j] = v_plane[0][:, j : j + SUB]
 
         def move_late_scales():
-            late = sb([P, half], U8, "v_plane_late", "scale_window")
+            late = placed.tile([P, half], U8, name="v_plane_late", align_bytes=ALIGN, offset=wa_scale_at + 1024)
             nc.sync.dma_start(late[:].bitcast(I32)[0:MOVED, :], got32[SHIFT : SHIFT + MOVED, half // 4 :])
             for j in range(half, S, SUB):
                 v_scale[0, j] = late[:, j - half : j - half + SUB]
+
+        move_late_scales()
 
         h_codes, h_plane, block_codes = {}, {}, {}
         filled = []
@@ -240,14 +252,14 @@ def tile_list_armband_gain_sensitivity_kernel(
                 wb_codes[b, first_page + e] = codes[:, P * e : P * (e + 1)]
                 wb_plane[b, first_page + e] = plane[:, P * e : P * (e + 1)]
 
-        steps, done = [], []
         out_pages = out.rearrange("(p i) t -> i p t", i=PACK)
+        steps = []
 
-        def second_product(blocks, step_pages, on_vector=1, fused=False):
+        def second_product(blocks, step_pages, bank):
             n = len(steps)
             steps.append(n)
             parts = [(i, block) for i in step_pages for block in blocks]
-            q = psum.tile([P, len(parts), BLOCK], F32, name="q", tag=f"bank{FIRST_BANKS + n % (BANKS - FIRST_BANKS)}")
+            q = psum.tile([P, len(parts), BLOCK], F32, name="q", tag=f"bank{bank}")
             for part, (i, block) in enumerate(parts):
                 for b in range(H_PASSES):
                     nc.tensor.matmul_mx(
@@ -259,49 +271,43 @@ def tile_list_armband_gain_sensitivity_kernel(
                         start=(b == 0),
                         stop=(b == H_PASSES - 1),
                     )
-            drive = sb([P, len(parts), BLOCK], F32, f"drive{n}", f"drive{n % 2}")
-            nc.scalar.activation(drive[:], q[:], ACT.Tanh)
-            slope = sb([P, on_vector, BLOCK], F32, f"slope{n}") if on_vector else None
-            others = len(parts) - on_vector
-            if others:
-                gated = sb([P, others, BLOCK], F32, f"gated{n}")
-                nc.scalar.activation(gated[:], q[:, on_vector:], ACT.Silu, scale=-2.0)
-                rest = sb([P, others, BLOCK], F32, f"rest{n}")
-                nc.scalar.activation(rest[:], drive[:, on_vector:], ACT.Identity, bias=1.0)
-            if on_vector:
-                square = sb([P, on_vector, BLOCK], F32, f"square{n}")
-                nc.scalar.activation(square[:], drive[:, 0:on_vector], ACT.Square)
-                nc.vector.scalar_tensor_tensor(
-                    slope[:].rearrange("p e j -> p (e j)"),
-                    square[:].rearrange("p e j -> p (e j)"),
-                    1.0,
-                    q[:, 0:on_vector].rearrange("p e j -> p (e j)"),
-                    ALU.subtract,
-                    ALU.mult,
-                )
-            values = sb([P, len(parts), BLOCK], F32, f"values{n}")
-            for part in reversed(range(len(parts))):
-                i, block = parts[part]
-                entries = weight[:, block * BLOCK : (block + 1) * BLOCK]
-                if part < on_vector:
-                    nc.gpsimd.tensor_tensor(values[:, part], slope[:, part], entries, ALU.mult)
-                elif fused:
-                    nc.gpsimd.tensor_tensor(values[:, part], gated[:, part - on_vector], rest[:, part - on_vector], ALU.mult)
-                else:
-                    weighted = sb([P, BLOCK], F32, f"weighted{n}_{part}")
-                    nc.gpsimd.tensor_tensor(weighted[:], gated[:, part - on_vector], entries, ALU.mult)
-                    nc.gpsimd.tensor_tensor(values[:, part], weighted[:], rest[:, part - on_vector], ALU.mult)
-                if fused:
-                    continue
-                slots = pages[i][:].indirect(place[:, block * BLOCK // GROUP : (block + 1) * BLOCK // GROUP])
-                nc.vector.tensor_copy(slots, values[:, part])
-                done.append(i)
-                if len([k for k in done if k == i]) == S // BLOCK:
-                    nc.sync.dma_start(out_pages[i], pages[i][:])
-            if fused:
-                lo, i = blocks[0] * BLOCK, step_pages[0]
-                slots = pages[i][:].indirect(place[:, lo // GROUP :])
-                nc.vector.tensor_tensor(slots, values[:].rearrange("p e j -> p (e j)"), weight[:, lo:], ALU.mult)
+            q_flat = q[:].rearrange("p e j -> p (e j)")
+            drive = sb([P, len(parts) * BLOCK], F32, f"drive{n}", f"drive{n % 2}")
+            nc.scalar.activation(drive[:], q_flat, ACT.Tanh)
+            return n, parts, q_flat, drive
+
+        def slope_on_vector(n, parts, q_flat, drive):
+            square = sb([P, len(parts) * BLOCK], F32, f"square{n}")
+            nc.scalar.activation(square[:], drive[:], ACT.Square)
+            slope = sb([P, len(parts) * BLOCK], F32, f"slope{n}")
+            nc.vector.scalar_tensor_tensor(slope[:], square[:], 1.0, q_flat, ALU.subtract, ALU.mult)
+            return slope
+
+        def values_on_gpsimd(n, parts, q_flat, drive, weighted=True):
+            width = len(parts) * BLOCK
+            gated = sb([P, width], F32, f"gated{n}")
+            nc.scalar.activation(gated[:], q_flat, ACT.Silu, scale=-2.0)
+            rest = sb([P, width], F32, f"rest{n}")
+            nc.scalar.activation(rest[:], drive[:], ACT.Identity, bias=1.0)
+            values = sb([P, width], F32, f"values{n}")
+            for part, (i, block) in enumerate(parts):
+                cols = slice(part * BLOCK, (part + 1) * BLOCK)
+                factor = gated[:, cols]
+                if weighted:
+                    product = sb([P, BLOCK], F32, f"weighted{n}_{part}")
+                    nc.gpsimd.tensor_tensor(product[:], factor, weight[:, block * BLOCK : (block + 1) * BLOCK], ALU.mult)
+                    factor = product[:]
+                nc.gpsimd.tensor_tensor(values[:, cols], factor, rest[:, cols], ALU.mult)
+            return values
+
+        def put(i, lo, values, weighted):
+            hi = lo + values.shape[1]
+            slots = pages[i][:].indirect(place[:, lo // GROUP : hi // GROUP])
+            if weighted:
+                nc.vector.tensor_copy(slots, values)
+            else:
+                nc.vector.tensor_tensor(slots, values, weight[:, lo:hi], ALU.mult)
+            if hi == S:
                 nc.sync.dma_start(out_pages[i], pages[i][:])
 
         low, high = (0, 1), (2, 3)
@@ -310,20 +316,31 @@ def tile_list_armband_gain_sensitivity_kernel(
         first_product(0, every_pass)
         quantise_wb(0, 0, 2)
         quantise_wb(0, 2, 2)
-        move_late_scales()
         quantise_wb(1, 0, 2)
         quantise_wb(2, 0, 2)
-        second_product((0,), (0,))
-        second_product((0,), (1,), 0)
+        opening = [slope_on_vector(*second_product((0,), (i,), FIRST_BANKS + i)) for i in low]
         quantise_wb(1, 2, 2)
         quantise_wb(2, 2, 2)
-        second_product((0,), high, 0)
         first_product(1, every_pass)
+        for i in low:
+            put(i, 0, opening[i][:], False)
+        high_step = second_product((0,), high, FIRST_BANKS)
         first_product(2, every_pass)
-        second_product((1,), low)
+        slope = slope_on_vector(*high_step)
+        put(2, 0, slope[:, 0:BLOCK], False)
         first_product(3, every_pass)
-        second_product((1,), high, 0)
-        second_product((2,), low)
-        second_product((3,), low, 0)
-        second_product((2, 3), (2,), 0)
-        second_product((2, 3), (3,), 0, fused=True)
+        bridge = sb([P, BLOCK], F32, "bridge")
+        nc.vector.tensor_tensor(bridge[:], slope[:, BLOCK:], weight[:, 0:BLOCK], ALU.mult)
+        put(3, 0, bridge[:], True)
+
+        for blocks, step_pages, bank in (
+            ((1,), low, filled[-3]),
+            ((1,), high, filled[-2]),
+            ((2,), low, filled[-1]),
+            ((3,), low, FIRST_BANKS + 1),
+        ):
+            values = values_on_gpsimd(*second_product(blocks, step_pages, bank))
+            for part, i in enumerate(step_pages):
+                put(i, blocks[0] * BLOCK, values[:, part * BLOCK : (part + 1) * BLOCK], True)
+        put(2, 2 * BLOCK, values_on_gpsimd(*second_product((2, 3), (2,), FIRST_BANKS))[:], True)
+        put(3, 2 * BLOCK, values_on_gpsimd(*second_product((2, 3), (3,), 0), weighted=False)[:], False)

@@ -46,11 +46,11 @@ def tile_list_armband_gain_sensitivity_kernel(
         spots = {
             "wb_bf2_0": 0,
             "h_codes1": h_bytes - ALIGN,
-            "h_bf2_2": low_end,
-            "slope2": low_end + h_bytes - ALIGN,
-            "bridge": low_end + 2 * h_bytes,
-            "h_bf3_2": low_end + 2 * h_bytes + 4 * BLOCK - ALIGN,
-            "weighted3_0": low_end + 3 * h_bytes + 4 * BLOCK - 2 * ALIGN,
+            "square2": low_end,
+            "h_codes2": low_end + h_bytes - ALIGN,
+            "bridge": 2 * low_end,
+            "h_bf3_2": 2 * low_end + 4 * BLOCK - ALIGN,
+            "weighted4_0": 2 * low_end + h_bytes + 4 * BLOCK - 2 * ALIGN,
         }
         psum = ctx.enter_context(tc.psum_pool(name="psum", bufs=1))
 
@@ -144,8 +144,21 @@ def tile_list_armband_gain_sensitivity_kernel(
             nc.vector.tensor_copy(got[:], table[a][:].bitcast(U32).indirect(pick[:, lo // GROUP : hi // GROUP]))
             for j in range(lo, hi, SUB):
                 v_words[a, j] = got[:, j - lo : j - lo + SUB]
+            return got
 
-        gather_words(0, 0, S)
+        v_first = gather_words(0, 0, S)
+
+        warm = psum.tile([P, 512], F32, name="warm", tag=f"bank{BANKS - 1}")
+        for repeat in range(3):
+            nc.tensor.matmul_mx(
+                out=warm[:],
+                lhsT=v_first[:, 0:P].bitcast(FP8X4),
+                lhsT_scale=scale_got[:, 0:P],
+                rhs=v_first[:, 0:512].bitcast(FP8X4),
+                rhs_scale=scale_got[:, 0:512],
+                start=True,
+                stop=True,
+            )
 
         wa_codes = sb([P, K_PASSES, 2 * H], U8, "wa_codes")
         wa_plane = sb([P, K_PASSES, H], U8, "wa_plane")
@@ -283,21 +296,24 @@ def tile_list_armband_gain_sensitivity_kernel(
             nc.vector.scalar_tensor_tensor(slope[:], square[:], 1.0, q_flat, ALU.subtract, ALU.mult)
             return slope
 
-        def values_on_gpsimd(n, parts, q_flat, drive, weighted=True):
+        def values_on_gpsimd(n, parts, q_flat, drive, piece=BLOCK, weighted=True):
             width = len(parts) * BLOCK
             gated = sb([P, width], F32, f"gated{n}")
             nc.scalar.activation(gated[:], q_flat, ACT.Silu, scale=-2.0)
             rest = sb([P, width], F32, f"rest{n}")
             nc.scalar.activation(rest[:], drive[:], ACT.Identity, bias=1.0)
             values = sb([P, width], F32, f"values{n}")
-            for part, (i, block) in enumerate(parts):
-                cols = slice(part * BLOCK, (part + 1) * BLOCK)
-                factor = gated[:, cols]
+            lo = parts[0][1] * BLOCK
+            run = width if parts[0][0] == parts[-1][0] else BLOCK
+            for at in range(0, width, run):
+                factor = gated[:, at : at + run]
                 if weighted:
-                    product = sb([P, BLOCK], F32, f"weighted{n}_{part}")
-                    nc.gpsimd.tensor_tensor(product[:], factor, weight[:, block * BLOCK : (block + 1) * BLOCK], ALU.mult)
+                    product = sb([P, run], F32, f"weighted{n}_{at}")
+                    nc.gpsimd.tensor_tensor(product[:], factor, weight[:, lo : lo + run], ALU.mult)
                     factor = product[:]
-                nc.gpsimd.tensor_tensor(values[:, cols], factor, rest[:, cols], ALU.mult)
+                for part in range(0, run, piece):
+                    cols = slice(at + part, at + part + piece)
+                    nc.gpsimd.tensor_tensor(values[:, cols], factor[:, part : part + piece], rest[:, cols], ALU.mult)
             return values
 
         def put(i, lo, values, weighted):
@@ -324,23 +340,25 @@ def tile_list_armband_gain_sensitivity_kernel(
         first_product(1, every_pass)
         for i in low:
             put(i, 0, opening[i][:], False)
-        high_step = second_product((0,), high, FIRST_BANKS)
+        slope = slope_on_vector(*second_product((0,), high, FIRST_BANKS))
+        for part, i in enumerate(high):
+            put(i, 0, slope[:, part * BLOCK : (part + 1) * BLOCK], False)
         first_product(2, every_pass)
-        slope = slope_on_vector(*high_step)
-        put(2, 0, slope[:, 0:BLOCK], False)
-        first_product(3, every_pass)
+        first_product(3, (0, 1))
+        bridge_slope = slope_on_vector(*second_product((1,), (0,), filled[-3]))
+        first_product(3, (2,))
         bridge = sb([P, BLOCK], F32, "bridge")
-        nc.vector.tensor_tensor(bridge[:], slope[:, BLOCK:], weight[:, 0:BLOCK], ALU.mult)
-        put(3, 0, bridge[:], True)
+        nc.vector.tensor_tensor(bridge[:], bridge_slope[:], weight[:, BLOCK : 2 * BLOCK], ALU.mult)
+        put(0, BLOCK, bridge[:], True)
 
-        for blocks, step_pages, bank in (
-            ((1,), low, filled[-3]),
-            ((1,), high, filled[-2]),
-            ((2,), low, filled[-1]),
-            ((3,), low, FIRST_BANKS + 1),
-        ):
-            values = values_on_gpsimd(*second_product(blocks, step_pages, bank))
-            for part, i in enumerate(step_pages):
-                put(i, blocks[0] * BLOCK, values[:, part * BLOCK : (part + 1) * BLOCK], True)
-        put(2, 2 * BLOCK, values_on_gpsimd(*second_product((2, 3), (2,), FIRST_BANKS))[:], True)
-        put(3, 2 * BLOCK, values_on_gpsimd(*second_product((2, 3), (3,), 0), weighted=False)[:], False)
+        put(1, BLOCK, values_on_gpsimd(*second_product((1,), (1,), filled[-3]))[:], True)
+        values = values_on_gpsimd(*second_product((1,), high, filled[-2]))
+        for part, i in enumerate(high):
+            put(i, BLOCK, values[:, part * BLOCK : (part + 1) * BLOCK], True)
+        values = values_on_gpsimd(*second_product((2, 3), (0,), filled[-1]))
+        for part in range(2):
+            put(0, (2 + part) * BLOCK, values[:, part * BLOCK : (part + 1) * BLOCK], True)
+        for i, bank in ((1, FIRST_BANKS + 1), (2, FIRST_BANKS)):
+            put(i, 2 * BLOCK, values_on_gpsimd(*second_product((2, 3), (i,), bank), 2 * BLOCK)[:], True)
+        last = second_product((2, 3), (3,), filled[-4])
+        put(3, 2 * BLOCK, values_on_gpsimd(*last, 2 * BLOCK, weighted=False)[:], False)

@@ -62,7 +62,7 @@ def tile_list_armband_gain_sensitivity_kernel(
         pick = lists.tile([P, S // GROUP], U16, name="pick")
         place = lists.tile([P, S // GROUP], U16, name="place")
 
-        wa_scale_at = 4 * T2 - ALIGN
+        wa_scale_at = 0
         wb_last_at = wa_scale_at + K_PASSES * H - ALIGN
 
         scale_window = sb([P, T], U8, "scale_window")
@@ -72,9 +72,10 @@ def tile_list_armband_gain_sensitivity_kernel(
         v_plane = [sb([P, half], U8, "v_plane0"), sb([P, S], U8, "v_plane1")]
 
         zero_a = sb([P, 1], F32, "zero_a", "table0")
-        zero_b = sb([P, 1], F32, "zero_b", "wa_raw")
+        zero_b = sb([P, 1], F32, "zero_b")
         zero_sum = sb([P, 1], F32, "zero_sum")
-        silu_in = sb([P, 1], F32, "silu_in", "table1")
+        silu_in = sb([P, 1], F32, "silu_in", "wa_raw")
+        bias_in = sb([P, 1], F32, "bias_in", "table1")
         zero_bias = sb([P, 1], F32, "zero_bias")
 
         def clear_words(words):
@@ -88,7 +89,8 @@ def tile_list_armband_gain_sensitivity_kernel(
         nc.vector.tensor_tensor(zero_sum[:], zero_a[:], zero_b[:], ALU.add)
         clear_words(wa_scale_raw[:].rearrange("p a c -> p (a c)").bitcast(I32))
         nc.vector.tensor_copy(silu_in[:], zero_sum[:])
-        nc.scalar.activation(zero_bias[:], silu_in[:], ACT.Silu)
+        nc.vector.tensor_copy(bias_in[:], silu_in[:])
+        nc.scalar.activation(zero_bias[:], bias_in[:], ACT.Silu)
 
         nc.sync.dma_start(pick[:], offs)
         nc.sync.dma_start(place[:], offs2)
@@ -101,11 +103,11 @@ def tile_list_armband_gain_sensitivity_kernel(
         table_rows = [tab_words[a].rearrange("p t i -> p (t i)").bitcast(I32) for a in range(K_PASSES)]
         table = [sb([P, T], I32, "table0")]
         nc.sync.dma_start(table[0][:], table_rows[0])
-        nc.sync.dma_start(wa_raw[:], wa_words.bitcast(I32).rearrange("a p c -> p a c"))
         wa_scale_rows = wa_scales.bitcast(I32).rearrange("a q c -> q a c")
         wa_scale32 = wa_scale_raw[:].bitcast(I32)
         for d in range(QUADS):
             nc.sync.dma_start(wa_scale32[32 * d : 32 * d + 4, :, :], wa_scale_rows[4 * d : 4 * d + 4, :, :])
+        nc.sync.dma_start(wa_raw[:], wa_words.bitcast(I32).rearrange("a p c -> p a c"))
 
         wb_rows = wb.rearrange("(b q t s) n -> b t q s n", b=H_PASSES, q=16, t=PACK)
         wb_raw = []
@@ -125,7 +127,7 @@ def tile_list_armband_gain_sensitivity_kernel(
             for lo in range(0, T2, T2 // 2):
                 nc.gpsimd.memset(page[:, lo : lo + T2 // 2], 0.0)
 
-        for i in range(2):
+        for i in (0, 1, 3):
             clear_page(i, sb([P, T2], F32, f"page{i}"))
         pages[2] = sb([P, T2], F32, "page2")
         clear_words(pages[2][:])
@@ -162,8 +164,8 @@ def tile_list_armband_gain_sensitivity_kernel(
 
         wa_codes = sb([P, K_PASSES, 2 * H], U8, "wa_codes")
         wa_plane = sb([P, K_PASSES, H], U8, "wa_plane")
-        for dealt, raw in ((wa_codes, wa_raw[:]), (wa_plane, wa_scale32)):
-            nc.vector.tensor_copy(
+        for engine, dealt, raw in ((nc.gpsimd, wa_codes, wa_raw[:]), (nc.vector, wa_plane, wa_scale32)):
+            engine.tensor_copy(
                 dealt[:].bitcast(I32).rearrange("p a (b t q w) -> p (a b) t q w", b=H_PASSES, t=PACK, q=16),
                 raw.rearrange("p a (b q t w) -> p (a b) t q w", b=H_PASSES, t=PACK, q=16),
             )
@@ -171,7 +173,6 @@ def tile_list_armband_gain_sensitivity_kernel(
         load_wb(sb([P, PACK, N], F32, "wb_raw1", "wa_raw"))
         load_wb(placed.tile([P, PACK, N], F32, name="wb_raw2", align_bytes=ALIGN, offset=wb_last_at))
 
-        clear_page(PACK - 1, placed.tile([P, T2], F32, name="page3", align_bytes=ALIGN, offset=0))
 
         gather_words(1, 0, BLOCK)
         gather_words(1, BLOCK, S)
@@ -190,7 +191,7 @@ def tile_list_armband_gain_sensitivity_kernel(
 
         move_late_scales()
 
-        h_codes, h_plane, block_codes = {}, {}, {}
+        h_codes, h_plane, block_codes, block_plane = {}, {}, {}, {}
         filled = []
 
         def next_bank():
@@ -224,8 +225,12 @@ def tile_list_armband_gain_sensitivity_kernel(
                 if b == 0:
                     block_codes[block] = sb([P, H_PASSES * BLOCK], U32, f"h_codes{block}", behind)
                 h_codes[block, b] = block_codes[block][:, b * BLOCK : (b + 1) * BLOCK]
-                h_plane[block, b] = sb([P, BLOCK], U8, f"h_plane{block}_{b}")
-                h_bf = sb([P, BLOCK, PACK], BF16, f"h_bf{block}_{b}")
+                if b == 0:
+                    block_plane[block] = sb([P, H_PASSES * BLOCK], U8, f"h_plane{block}")
+                h_plane[block, b] = block_plane[block][:, b * BLOCK : (b + 1) * BLOCK]
+                if b != 1:
+                    rounded = sb([P, (2 - b // 2) * BLOCK, PACK], BF16, f"h_bf{block}_{b}")
+                h_bf = rounded[:, b % 2 * BLOCK : (b % 2 + 1) * BLOCK, :]
                 for j in range(lo, lo + BLOCK, SUB):
                     if early:
                         acc = accs[b, j]
@@ -239,21 +244,26 @@ def tile_list_armband_gain_sensitivity_kernel(
                         ACT.Relu,
                         bias=zero_bias[:] if (b, j) == (0, 0) else 0.0,
                     )
-                nc.vector.quantize_mx(
-                    out=h_codes[block, b].bitcast(FP8X4),
-                    scales=h_plane[block, b][:],
-                    in_=h_bf[:].rearrange("p j t -> p (j t)"),
-                )
+                if b != 0:
+                    cols = slice(b // 2 * 2 * BLOCK, (b + 1) * BLOCK)
+                    nc.vector.quantize_mx(
+                        out=block_codes[block][:, cols].bitcast(FP8X4),
+                        scales=block_plane[block][:, cols],
+                        in_=rounded[:].rearrange("p j t -> p (j t)"),
+                    )
 
         wb_codes, wb_plane = {}, {}
 
-        def quantise_wb(b, first_page, count):
+        def quantise_wb(*halves):
+            b, first_page = halves[0]
+            count = 2 * len(halves)
             rounded = sb([P, count, P, PACK], BF16, f"wb_bf{b}_{first_page}")
-            nc.vector.tensor_scalar_mul(
-                rounded[:].rearrange("p i m t -> p m i t"),
-                wb_raw[b][:].rearrange("p t (m i) -> p m i t", i=PACK)[:, :, first_page : first_page + count, :],
-                -1.0,
-            )
+            for e, (c, page) in enumerate(halves):
+                nc.vector.tensor_scalar_mul(
+                    rounded[:, 2 * e : 2 * e + 2, :, :].rearrange("p i m t -> p m i t"),
+                    wb_raw[c][:].rearrange("p t (m i) -> p m i t", i=PACK)[:, :, page : page + 2, :],
+                    -1.0,
+                )
             codes = sb([P, count * P], U32, f"wb_codes{b}_{first_page}")
             plane = sb([P, count * P], U8, f"wb_plane{b}_{first_page}")
             nc.vector.quantize_mx(
@@ -262,8 +272,9 @@ def tile_list_armband_gain_sensitivity_kernel(
                 in_=rounded[:].rearrange("p i m t -> p (i m t)"),
             )
             for e in range(count):
-                wb_codes[b, first_page + e] = codes[:, P * e : P * (e + 1)]
-                wb_plane[b, first_page + e] = plane[:, P * e : P * (e + 1)]
+                c, page = halves[e // 2]
+                wb_codes[c, page + e % 2] = codes[:, P * e : P * (e + 1)]
+                wb_plane[c, page + e % 2] = plane[:, P * e : P * (e + 1)]
 
         out_pages = out.rearrange("(p i) t -> i p t", i=PACK)
         steps = []
@@ -280,7 +291,7 @@ def tile_list_armband_gain_sensitivity_kernel(
                         lhsT=wb_codes[b, i].bitcast(FP8X4),
                         lhsT_scale=wb_plane[b, i],
                         rhs=h_codes[block, b].bitcast(FP8X4),
-                        rhs_scale=h_plane[block, b][:],
+                        rhs_scale=h_plane[block, b],
                         start=(b == 0),
                         stop=(b == H_PASSES - 1),
                     )
@@ -330,13 +341,11 @@ def tile_list_armband_gain_sensitivity_kernel(
         every_pass = range(H_PASSES)
 
         first_product(0, every_pass)
-        quantise_wb(0, 0, 2)
-        quantise_wb(0, 2, 2)
-        quantise_wb(1, 0, 2)
-        quantise_wb(2, 0, 2)
+        quantise_wb((0, 0), (0, 2))
+        quantise_wb((1, 0))
+        quantise_wb((2, 0))
         opening = [slope_on_vector(*second_product((0,), (i,), FIRST_BANKS + i)) for i in low]
-        quantise_wb(1, 2, 2)
-        quantise_wb(2, 2, 2)
+        quantise_wb((1, 2), (2, 2))
         first_product(1, every_pass)
         for i in low:
             put(i, 0, opening[i][:], False)
@@ -355,10 +364,7 @@ def tile_list_armband_gain_sensitivity_kernel(
         values = values_on_gpsimd(*second_product((1,), high, filled[-2]))
         for part, i in enumerate(high):
             put(i, BLOCK, values[:, part * BLOCK : (part + 1) * BLOCK], True)
-        values = values_on_gpsimd(*second_product((2, 3), (0,), filled[-1]))
-        for part in range(2):
-            put(0, (2 + part) * BLOCK, values[:, part * BLOCK : (part + 1) * BLOCK], True)
-        for i, bank in ((1, FIRST_BANKS + 1), (2, FIRST_BANKS)):
+        for i, bank in ((0, filled[-1]), (1, FIRST_BANKS + 1), (2, FIRST_BANKS)):
             put(i, 2 * BLOCK, values_on_gpsimd(*second_product((2, 3), (i,), bank), 2 * BLOCK)[:], True)
         last = second_product((2, 3), (3,), filled[-4])
         put(3, 2 * BLOCK, values_on_gpsimd(*last, 2 * BLOCK, weighted=False)[:], False)

@@ -41,6 +41,7 @@ def tile_list_armband_gain_sensitivity_kernel(
         keep = ctx.enter_context(tc.tile_pool(name="keep", bufs=1))
         placed = ctx.enter_context(tc.tile_pool(name="placed", bufs=1))
         held = ctx.enter_context(tc.tile_pool(name="held", bufs=1))
+        staged = ctx.enter_context(tc.tile_pool(name="staged", bufs=1))
         h_bytes = 2 * BLOCK * PACK
         low_end = 2 * h_bytes + H_PASSES * 4 * BLOCK
         spots = {
@@ -62,19 +63,17 @@ def tile_list_armband_gain_sensitivity_kernel(
         pick = lists.tile([P, S // GROUP], U16, name="pick")
         place = lists.tile([P, S // GROUP], U16, name="place")
 
-        wa_scale_at = 0
-        wb_last_at = wa_scale_at + K_PASSES * H - ALIGN
-
-        scale_window = sb([P, T], U8, "scale_window")
-        wa_scale_raw = placed.tile([P, K_PASSES, H], U8, name="wa_scale_raw", align_bytes=ALIGN, offset=wa_scale_at)
+        window_at = 4 * T - ALIGN
+        scale_window = staged.tile([P, T], U8, name="scale_window", align_bytes=ALIGN, offset=window_at)
+        wa_at = 4 * T - ALIGN
+        wa_raw = placed.tile([P, K_PASSES, H // 2], I32, name="wa_raw", align_bytes=ALIGN, offset=wa_at)
+        wa_scale_raw = sb([P, K_PASSES, H], U8, "wa_scale_raw")
         scale_got = sb([P, S], U8, "scale_got")
         half = S // 2
         v_plane = [sb([P, half], U8, "v_plane0"), sb([P, S], U8, "v_plane1")]
 
         zero_a = sb([P, 1], F32, "zero_a", "table0")
-        zero_b = sb([P, 1], F32, "zero_b")
-        zero_sum = sb([P, 1], F32, "zero_sum")
-        silu_in = sb([P, 1], F32, "silu_in", "wa_raw")
+        silu_in = placed.tile([P, 1], F32, name="silu_in", align_bytes=ALIGN, offset=wa_at + ALIGN)
         bias_in = sb([P, 1], F32, "bias_in", "table1")
         zero_bias = sb([P, 1], F32, "zero_bias")
 
@@ -85,10 +84,10 @@ def tile_list_armband_gain_sensitivity_kernel(
 
         nc.gpsimd.memset(scale_window[:].bitcast(I32), 0)
         nc.vector.memset(zero_a[:], 0.0)
-        nc.vector.memset(zero_b[:], 0.0)
-        nc.vector.tensor_tensor(zero_sum[:], zero_a[:], zero_b[:], ALU.add)
+        zero_b = sb([P, 1], F32, "zero_b")
+        nc.vector.tensor_copy(zero_b[:], zero_a[:])
         clear_words(wa_scale_raw[:].rearrange("p a c -> p (a c)").bitcast(I32))
-        nc.vector.tensor_copy(silu_in[:], zero_sum[:])
+        nc.vector.tensor_copy(silu_in[:], zero_b[:])
         nc.vector.tensor_copy(bias_in[:], silu_in[:])
         nc.scalar.activation(zero_bias[:], bias_in[:], ACT.Silu)
 
@@ -99,7 +98,6 @@ def tile_list_armband_gain_sensitivity_kernel(
         for d in range(QUADS):
             nc.sync.dma_start(window32[32 * d + SHIFT : 32 * d + SHIFT + 4, :], tab_scale_rows[0, 4 * d : 4 * d + 4, :])
         nc.sync.dma_start(window32[SPARE:P:8, :], tab_scale_rows[1])
-        wa_raw = sb([P, K_PASSES, H // 2], I32, "wa_raw")
         table_rows = [tab_words[a].rearrange("p t i -> p (t i)").bitcast(I32) for a in range(K_PASSES)]
         table = [sb([P, T], I32, "table0")]
         nc.sync.dma_start(table[0][:], table_rows[0])
@@ -109,12 +107,11 @@ def tile_list_armband_gain_sensitivity_kernel(
             nc.sync.dma_start(wa_scale32[32 * d : 32 * d + 4, :, :], wa_scale_rows[4 * d : 4 * d + 4, :, :])
         nc.sync.dma_start(wa_raw[:], wa_words.bitcast(I32).rearrange("a p c -> p a c"))
 
-        wb_rows = wb.rearrange("(b q t s) n -> b t q s n", b=H_PASSES, q=16, t=PACK)
+        wb_rows = wb.rearrange("(b p t) n -> b p t n", b=H_PASSES, t=PACK)
         wb_raw = []
 
         def load_wb(rows):
-            for t in range(PACK):
-                nc.sync.dma_start(rows[:, t, :], wb_rows[len(wb_raw), t])
+            nc.sync.dma_start(rows[:], wb_rows[len(wb_raw)])
             wb_raw.append(rows)
 
         table.append(sb([P, T], I32, "table1"))
@@ -122,13 +119,13 @@ def tile_list_armband_gain_sensitivity_kernel(
 
         pages = {}
 
-        def clear_page(i, page):
+        def clear_page(i, pieces, page):
             pages[i] = page
-            for lo in range(0, T2, T2 // 2):
-                nc.gpsimd.memset(page[:, lo : lo + T2 // 2], 0.0)
+            for lo in range(0, T2, T2 // pieces):
+                nc.gpsimd.memset(pages[i][:, lo : lo + T2 // pieces], 0.0)
 
-        for i in (0, 1, 3):
-            clear_page(i, sb([P, T2], F32, f"page{i}"))
+        for i in range(2):
+            clear_page(i, 2, sb([P, T2], F32, f"page{i}"))
         pages[2] = sb([P, T2], F32, "page2")
         clear_words(pages[2][:])
 
@@ -137,43 +134,37 @@ def tile_list_armband_gain_sensitivity_kernel(
         nc.sync.dma_start(v_plane[0][:].bitcast(I32)[0:MOVED, :], got32[SHIFT : SHIFT + MOVED, 0 : half // 4])
         for row in range(4):
             nc.sync.dma_start(v_plane[1][:].bitcast(I32)[row:P:32, :], got32[8 * row + SPARE : P : 32, :])
-        load_wb(sb([P, PACK, N], F32, "wb_raw0", "scale_window"))
+        load_wb(staged.tile([P, PACK, N], F32, name="wb_raw0", align_bytes=ALIGN, offset=0))
+
+        wa_codes = sb([P, K_PASSES, 2 * H], U8, "wa_codes")
+        nc.vector.tensor_copy(
+            wa_codes[:].bitcast(U16).rearrange("p a (b t g m) -> p (a b) g t m", b=H_PASSES, t=PACK, m=8),
+            wa_raw[:].bitcast(U16).rearrange("p a (b g m t) -> p (a b) g t m", b=H_PASSES, t=PACK, m=8),
+        )
+        wa_plane = []
+        for b in range(H_PASSES):
+            if b < H_PASSES - 1:
+                wa_plane.append(sb([P, K_PASSES, 512], U8, f"wa_plane{b}"))
+            else:
+                at = wa_at + 1024
+                wa_plane.append(placed.tile([P, K_PASSES, 512], U8, name="wa_plane2", align_bytes=ALIGN, offset=at))
+            nc.gpsimd.tensor_copy(
+                wa_plane[b][:].rearrange("p a (t g m) -> p a g t m", t=PACK, m=16),
+                wa_scale_raw[:, :, 512 * b : 512 * (b + 1)].rearrange("p a (g m t) -> p a g t m", t=PACK, m=16),
+            )
+        clear_page(3, 4, placed.tile([P, T2], F32, name="page3", align_bytes=ALIGN, offset=0))
+        load_wb(staged.tile([P, PACK, N], F32, name="wb_raw1", align_bytes=ALIGN, offset=window_at + T - ALIGN))
 
         v_words = {}
 
-        def gather_words(a, lo, hi, takes_over=None):
-            got = sb([P, hi - lo], U32, f"v_words{a}_{lo}", takes_over)
+        def gather_words(a, lo, hi):
+            got = sb([P, hi - lo], U32, f"v_words{a}_{lo}")
             nc.vector.tensor_copy(got[:], table[a][:].bitcast(U32).indirect(pick[:, lo // GROUP : hi // GROUP]))
             for j in range(lo, hi, SUB):
                 v_words[a, j] = got[:, j - lo : j - lo + SUB]
-            return got
 
-        v_first = gather_words(0, 0, S)
-
-        warm = psum.tile([P, 512], F32, name="warm", tag=f"bank{BANKS - 1}")
-        for repeat in range(3):
-            nc.tensor.matmul_mx(
-                out=warm[:],
-                lhsT=v_first[:, 0:P].bitcast(FP8X4),
-                lhsT_scale=scale_got[:, 0:P],
-                rhs=v_first[:, 0:512].bitcast(FP8X4),
-                rhs_scale=scale_got[:, 0:512],
-                start=True,
-                stop=True,
-            )
-
-        wa_codes = sb([P, K_PASSES, 2 * H], U8, "wa_codes")
-        wa_plane = sb([P, K_PASSES, H], U8, "wa_plane")
-        for engine, dealt, raw in ((nc.gpsimd, wa_codes, wa_raw[:]), (nc.vector, wa_plane, wa_scale32)):
-            engine.tensor_copy(
-                dealt[:].bitcast(I32).rearrange("p a (b t q w) -> p (a b) t q w", b=H_PASSES, t=PACK, q=16),
-                raw.rearrange("p a (b q t w) -> p (a b) t q w", b=H_PASSES, t=PACK, q=16),
-            )
-
-        load_wb(sb([P, PACK, N], F32, "wb_raw1", "wa_raw"))
-        load_wb(placed.tile([P, PACK, N], F32, name="wb_raw2", align_bytes=ALIGN, offset=wb_last_at))
-
-
+        gather_words(0, 0, S)
+        load_wb(sb([P, PACK, N], F32, "wb_raw2", "table0"))
         gather_words(1, 0, BLOCK)
         gather_words(1, BLOCK, S)
         weight = sb([P, S], F32, "weight", "table1")
@@ -182,14 +173,10 @@ def tile_list_armband_gain_sensitivity_kernel(
         v_scale = {(1, j): v_plane[1][:, j : j + SUB] for j in range(0, S, SUB)}
         for j in range(0, half, SUB):
             v_scale[0, j] = v_plane[0][:, j : j + SUB]
-
-        def move_late_scales():
-            late = placed.tile([P, half], U8, name="v_plane_late", align_bytes=ALIGN, offset=wa_scale_at + 1024)
-            nc.sync.dma_start(late[:].bitcast(I32)[0:MOVED, :], got32[SHIFT : SHIFT + MOVED, half // 4 :])
-            for j in range(half, S, SUB):
-                v_scale[0, j] = late[:, j - half : j - half + SUB]
-
-        move_late_scales()
+        late = sb([P, half], U8, "v_plane_late", "wa_scale_raw")
+        nc.sync.dma_start(late[:].bitcast(I32)[0:MOVED, :], got32[SHIFT : SHIFT + MOVED, half // 4 :])
+        for j in range(half, S, SUB):
+            v_scale[0, j] = late[:, j - half : j - half + SUB]
 
         h_codes, h_plane, block_codes, block_plane = {}, {}, {}, {}
         filled = []
@@ -205,7 +192,7 @@ def tile_list_armband_gain_sensitivity_kernel(
                     nc.tensor.matmul_mx(
                         out=acc[:, t, :],
                         lhsT=wa_codes[:, a, 2 * col : 2 * (col + P)].bitcast(FP4X4),
-                        lhsT_scale=wa_plane[:, a, col : col + P],
+                        lhsT_scale=wa_plane[b][:, a, P * t : P * (t + 1)],
                         rhs=v_words[a, j].bitcast(FP8X4),
                         rhs_scale=v_scale[a, j],
                         start=(a == 0),
@@ -354,16 +341,15 @@ def tile_list_armband_gain_sensitivity_kernel(
             put(i, 0, slope[:, part * BLOCK : (part + 1) * BLOCK], False)
         first_product(2, every_pass)
         first_product(3, (0, 1))
-        bridge_slope = slope_on_vector(*second_product((1,), (0,), filled[-3]))
+        bridge_slope = slope_on_vector(*second_product((1,), low, filled[-3]))
+        put(0, BLOCK, bridge_slope[:, 0:BLOCK], False)
         first_product(3, (2,))
         bridge = sb([P, BLOCK], F32, "bridge")
-        nc.vector.tensor_tensor(bridge[:], bridge_slope[:], weight[:, BLOCK : 2 * BLOCK], ALU.mult)
-        put(0, BLOCK, bridge[:], True)
+        nc.vector.tensor_tensor(bridge[:], bridge_slope[:, BLOCK:], weight[:, BLOCK : 2 * BLOCK], ALU.mult)
+        put(1, BLOCK, bridge[:], True)
 
-        put(1, BLOCK, values_on_gpsimd(*second_product((1,), (1,), filled[-3]))[:], True)
-        values = values_on_gpsimd(*second_product((1,), high, filled[-2]))
-        for part, i in enumerate(high):
-            put(i, BLOCK, values[:, part * BLOCK : (part + 1) * BLOCK], True)
+        for i, bank in ((2, filled[-3]), (3, filled[-2])):
+            put(i, BLOCK, values_on_gpsimd(*second_product((1,), (i,), bank))[:], True)
         for i, bank in ((0, filled[-1]), (1, FIRST_BANKS + 1), (2, FIRST_BANKS)):
             put(i, 2 * BLOCK, values_on_gpsimd(*second_product((2, 3), (i,), bank), 2 * BLOCK)[:], True)
         last = second_product((2, 3), (3,), filled[-4])

@@ -42,17 +42,20 @@ def tile_list_armband_gain_sensitivity_kernel(
         placed = ctx.enter_context(tc.tile_pool(name="placed", bufs=1))
         held = ctx.enter_context(tc.tile_pool(name="held", bufs=1))
         staged = ctx.enter_context(tc.tile_pool(name="staged", bufs=1))
-        h_bytes = 2 * BLOCK * PACK
-        low_end = 2 * h_bytes + H_PASSES * 4 * BLOCK
-        spots = {
-            "wb_bf2_0": 0,
-            "h_codes1": h_bytes - ALIGN,
-            "square2": low_end,
-            "h_codes2": low_end + h_bytes - ALIGN,
-            "bridge": 2 * low_end,
-            "h_bf3_2": 2 * low_end + 4 * BLOCK - ALIGN,
-            "weighted4_0": 2 * low_end + h_bytes + 4 * BLOCK - 2 * ALIGN,
-        }
+        spots = {}
+        end = 0
+        for chain in (
+            (("v_plane_late", S // 2), ("wb_bf1_0", 4 * P * PACK), ("h_codes0", 12 * BLOCK)),
+            (("wb_bf2_0", 4 * P * PACK), ("h_codes1", 12 * BLOCK)),
+            (("square0", 4 * BLOCK), ("h_bf1_2", 8 * BLOCK)),
+            (("square1", 4 * BLOCK), ("h_bf2_0", 16 * BLOCK)),
+            (("square2", 8 * BLOCK), ("h_codes2", 12 * BLOCK)),
+            (("bridge", 4 * BLOCK), ("h_bf3_2", 8 * BLOCK), ("weighted4_0", 4 * BLOCK)),
+        ):
+            for name, size in chain:
+                spots[name] = end
+                end = end + size - ALIGN
+            end = end + ALIGN
         psum = ctx.enter_context(tc.psum_pool(name="psum", bufs=1))
 
         def sb(shape, dtype, name, takes_over=None):
@@ -136,11 +139,13 @@ def tile_list_armband_gain_sensitivity_kernel(
             nc.sync.dma_start(v_plane[1][:].bitcast(I32)[row:P:32, :], got32[8 * row + SPARE : P : 32, :])
         load_wb(staged.tile([P, PACK, N], F32, name="wb_raw0", align_bytes=ALIGN, offset=0))
 
-        wa_codes = sb([P, K_PASSES, 2 * H], U8, "wa_codes")
-        nc.vector.tensor_copy(
-            wa_codes[:].bitcast(U16).rearrange("p a (b t g m) -> p (a b) g t m", b=H_PASSES, t=PACK, m=8),
-            wa_raw[:].bitcast(U16).rearrange("p a (b g m t) -> p (a b) g t m", b=H_PASSES, t=PACK, m=8),
-        )
+        wa_codes = []
+        for a in range(K_PASSES):
+            wa_codes.append(sb([P, 2 * H], U8, f"wa_codes{a}"))
+            nc.vector.tensor_copy(
+                wa_codes[a][:].bitcast(U16).rearrange("p (b t g m) -> p g b t m", b=H_PASSES, t=PACK, m=8),
+                wa_raw[:, a, :].bitcast(U16).rearrange("p (b g m t) -> p g b t m", b=H_PASSES, t=PACK, m=8),
+            )
         wa_plane = []
         for b in range(H_PASSES):
             if b < H_PASSES - 1:
@@ -173,10 +178,12 @@ def tile_list_armband_gain_sensitivity_kernel(
         v_scale = {(1, j): v_plane[1][:, j : j + SUB] for j in range(0, S, SUB)}
         for j in range(0, half, SUB):
             v_scale[0, j] = v_plane[0][:, j : j + SUB]
-        late = sb([P, half], U8, "v_plane_late", "wa_scale_raw")
-        nc.sync.dma_start(late[:].bitcast(I32)[0:MOVED, :], got32[SHIFT : SHIFT + MOVED, half // 4 :])
-        for j in range(half, S, SUB):
-            v_scale[0, j] = late[:, j - half : j - half + SUB]
+
+        def move_late_scales():
+            late = sb([P, half], U8, "v_plane_late")
+            nc.sync.dma_start(late[:].bitcast(I32)[0:MOVED, :], got32[SHIFT : SHIFT + MOVED, half // 4 :])
+            for j in range(half, S, SUB):
+                v_scale[0, j] = late[:, j - half : j - half + SUB]
 
         h_codes, h_plane, block_codes, block_plane = {}, {}, {}, {}
         filled = []
@@ -185,32 +192,41 @@ def tile_list_armband_gain_sensitivity_kernel(
             filled.append(len(filled) % FIRST_BANKS)
             return f"bank{filled[-1]}"
 
-        def first_matmuls(acc, b, j, table_passes, whole_bank):
-            for t, a in whole_bank:
-                if a in table_passes:
-                    col = 512 * b + P * t
-                    nc.tensor.matmul_mx(
-                        out=acc[:, t, :],
-                        lhsT=wa_codes[:, a, 2 * col : 2 * (col + P)].bitcast(FP4X4),
-                        lhsT_scale=wa_plane[b][:, a, P * t : P * (t + 1)],
-                        rhs=v_words[a, j].bitcast(FP8X4),
-                        rhs_scale=v_scale[a, j],
-                        start=(a == 0),
-                        stop=(a == K_PASSES - 1),
-                    )
+        def first_matmul(acc, b, j, t, a, start, stop):
+            col = 512 * b + P * t
+            nc.tensor.matmul_mx(
+                out=acc[:, t, :],
+                lhsT=wa_codes[a][:, 2 * col : 2 * (col + P)].bitcast(FP4X4),
+                lhsT_scale=wa_plane[b][:, a, P * t : P * (t + 1)],
+                rhs=v_words[a, j].bitcast(FP8X4),
+                rhs_scale=v_scale[a, j],
+                start=start,
+                stop=stop,
+            )
 
-        def first_product(block, passes, early=False, behind=None):
+        waiting = []
+
+        def quantise_h():
+            for block, b, rounded in waiting:
+                cols = slice(b // 2 * 2 * BLOCK, (b + 1) * BLOCK)
+                nc.vector.quantize_mx(
+                    out=block_codes[block][:, cols].bitcast(FP8X4),
+                    scales=block_plane[block][:, cols],
+                    in_=rounded[:].rearrange("p j t -> p (j t)"),
+                )
+            waiting.clear()
+
+        def first_product(block, passes, early=()):
             lo = block * BLOCK
-            whole_bank = [(t, a) for t in range(PACK) for a in range(K_PASSES)]
             accs = {}
-            if early:
-                for b in passes:
-                    for j in range(lo, lo + BLOCK, SUB):
-                        accs[b, j] = psum.tile([P, PACK, SUB], F32, name="acc", tag=next_bank())
-                        first_matmuls(accs[b, j], b, j, (0,), whole_bank)
+            for b in early:
+                for j in range(lo, lo + BLOCK, SUB):
+                    accs[b, j] = psum.tile([P, PACK, SUB], F32, name="acc", tag=next_bank())
+                    for t in range(PACK):
+                        first_matmul(accs[b, j], b, j, t, 0, t == 0, False)
             for b in passes:
                 if b == 0:
-                    block_codes[block] = sb([P, H_PASSES * BLOCK], U32, f"h_codes{block}", behind)
+                    block_codes[block] = sb([P, H_PASSES * BLOCK], U32, f"h_codes{block}")
                 h_codes[block, b] = block_codes[block][:, b * BLOCK : (b + 1) * BLOCK]
                 if b == 0:
                     block_plane[block] = sb([P, H_PASSES * BLOCK], U8, f"h_plane{block}")
@@ -219,12 +235,15 @@ def tile_list_armband_gain_sensitivity_kernel(
                     rounded = sb([P, (2 - b // 2) * BLOCK, PACK], BF16, f"h_bf{block}_{b}")
                 h_bf = rounded[:, b % 2 * BLOCK : (b % 2 + 1) * BLOCK, :]
                 for j in range(lo, lo + BLOCK, SUB):
-                    if early:
+                    if b in early:
                         acc = accs[b, j]
-                        first_matmuls(acc, b, j, (1,), whole_bank)
+                        for t in range(PACK):
+                            first_matmul(acc, b, j, t, 1, False, t == PACK - 1)
                     else:
                         acc = psum.tile([P, PACK, SUB], F32, name="acc", tag=next_bank())
-                        first_matmuls(acc, b, j, (0, 1), whole_bank)
+                        for t in range(PACK):
+                            first_matmul(acc, b, j, t, 1, True, False)
+                            first_matmul(acc, b, j, t, 0, False, True)
                     nc.scalar.activation(
                         h_bf[:, j - lo : j - lo + SUB, :].rearrange("p (j e) t -> p j t e", e=2),
                         acc[:].rearrange("p t (j e) -> p j t e", e=2),
@@ -232,12 +251,9 @@ def tile_list_armband_gain_sensitivity_kernel(
                         bias=zero_bias[:] if (b, j) == (0, 0) else 0.0,
                     )
                 if b != 0:
-                    cols = slice(b // 2 * 2 * BLOCK, (b + 1) * BLOCK)
-                    nc.vector.quantize_mx(
-                        out=block_codes[block][:, cols].bitcast(FP8X4),
-                        scales=block_plane[block][:, cols],
-                        in_=rounded[:].rearrange("p j t -> p (j t)"),
-                    )
+                    waiting.append((block, b, rounded))
+                if block != 0:
+                    quantise_h()
 
         wb_codes, wb_plane = {}, {}
 
@@ -327,9 +343,11 @@ def tile_list_armband_gain_sensitivity_kernel(
         low, high = (0, 1), (2, 3)
         every_pass = range(H_PASSES)
 
-        first_product(0, every_pass)
+        first_product(0, every_pass, early=(0,))
         quantise_wb((0, 0), (0, 2))
         quantise_wb((1, 0))
+        move_late_scales()
+        quantise_h()
         quantise_wb((2, 0))
         opening = [slope_on_vector(*second_product((0,), (i,), FIRST_BANKS + i)) for i in low]
         quantise_wb((1, 2), (2, 2))

@@ -45,10 +45,9 @@ def tile_list_armband_gain_sensitivity_kernel(
         spots = {}
         end = 0
         for chain in (
-            (("v_plane_late", S // 2), ("wb_bf1_0", 4 * P * PACK), ("h_codes0", 12 * BLOCK)),
+            (("wb_bf1_0", 4 * P * PACK), ("h_codes0", 12 * BLOCK)),
             (("wb_bf2_0", 4 * P * PACK), ("h_codes1", 12 * BLOCK)),
-            (("square0", 4 * BLOCK), ("h_bf1_2", 8 * BLOCK)),
-            (("square1", 4 * BLOCK), ("h_bf2_0", 16 * BLOCK)),
+            (("square0", 4 * BLOCK), ("page3", 4 * T2)),
             (("square2", 8 * BLOCK), ("h_codes2", 12 * BLOCK)),
             (("bridge", 4 * BLOCK), ("h_bf3_2", 8 * BLOCK), ("weighted4_0", 4 * BLOCK)),
         ):
@@ -68,8 +67,9 @@ def tile_list_armband_gain_sensitivity_kernel(
 
         window_at = 4 * T - ALIGN
         scale_window = staged.tile([P, T], U8, name="scale_window", align_bytes=ALIGN, offset=window_at)
-        wa_at = 4 * T - ALIGN
-        wa_raw = placed.tile([P, K_PASSES, H // 2], I32, name="wa_raw", align_bytes=ALIGN, offset=wa_at)
+        wa_at = 0
+        wa_first = placed.tile([P, K_PASSES, 256], I32, name="wa_first", align_bytes=ALIGN, offset=wa_at + ALIGN)
+        wa_rows = wa_words.bitcast(I32).rearrange("a p c -> p a c")
         wa_scale_raw = sb([P, K_PASSES, H], U8, "wa_scale_raw")
         scale_got = sb([P, S], U8, "scale_got")
         half = S // 2
@@ -108,7 +108,7 @@ def tile_list_armband_gain_sensitivity_kernel(
         wa_scale32 = wa_scale_raw[:].bitcast(I32)
         for d in range(QUADS):
             nc.sync.dma_start(wa_scale32[32 * d : 32 * d + 4, :, :], wa_scale_rows[4 * d : 4 * d + 4, :, :])
-        nc.sync.dma_start(wa_raw[:], wa_words.bitcast(I32).rearrange("a p c -> p a c"))
+        nc.sync.dma_start(wa_first[:], wa_rows[:, :, 0:256])
 
         wb_rows = wb.rearrange("(b p t) n -> b p t n", b=H_PASSES, t=PACK)
         wb_raw = []
@@ -137,41 +137,47 @@ def tile_list_armband_gain_sensitivity_kernel(
         nc.sync.dma_start(v_plane[0][:].bitcast(I32)[0:MOVED, :], got32[SHIFT : SHIFT + MOVED, 0 : half // 4])
         for row in range(4):
             nc.sync.dma_start(v_plane[1][:].bitcast(I32)[row:P:32, :], got32[8 * row + SPARE : P : 32, :])
+        rest_at = window_at + T - ALIGN
+        wa_rest = staged.tile([P, K_PASSES, 512], I32, name="wa_rest", align_bytes=ALIGN, offset=rest_at)
+        nc.sync.dma_start(wa_rest[:], wa_rows[:, :, 256:])
         load_wb(staged.tile([P, PACK, N], F32, name="wb_raw0", align_bytes=ALIGN, offset=0))
 
         wa_codes = []
-        for a in range(K_PASSES):
-            wa_codes.append(sb([P, 2 * H], U8, f"wa_codes{a}"))
+        for b, raw in enumerate((wa_first[:], wa_rest[:, :, 0:256], wa_rest[:, :, 256:])):
+            wa_codes.append(sb([P, K_PASSES, 1024], U8, f"wa_codes{b}"))
             nc.vector.tensor_copy(
-                wa_codes[a][:].bitcast(U16).rearrange("p (b t g m) -> p g b t m", b=H_PASSES, t=PACK, m=8),
-                wa_raw[:, a, :].bitcast(U16).rearrange("p (b g m t) -> p g b t m", b=H_PASSES, t=PACK, m=8),
+                wa_codes[b][:].bitcast(U16).rearrange("p a (t g m) -> p a g t m", t=PACK, m=8),
+                raw.bitcast(U16).rearrange("p a (g m t) -> p a g t m", t=PACK, m=8),
             )
         wa_plane = []
         for b in range(H_PASSES):
-            if b < H_PASSES - 1:
-                wa_plane.append(sb([P, K_PASSES, 512], U8, f"wa_plane{b}"))
+            if b == 0:
+                wa_plane.append(sb([P, K_PASSES, 512], U8, "wa_plane0"))
             else:
-                at = wa_at + 1024
-                wa_plane.append(placed.tile([P, K_PASSES, 512], U8, name="wa_plane2", align_bytes=ALIGN, offset=at))
+                at = wa_at + 1024 * (b - 1)
+                wa_plane.append(placed.tile([P, K_PASSES, 512], U8, name=f"wa_plane{b}", align_bytes=ALIGN, offset=at))
             nc.gpsimd.tensor_copy(
                 wa_plane[b][:].rearrange("p a (t g m) -> p a g t m", t=PACK, m=16),
                 wa_scale_raw[:, :, 512 * b : 512 * (b + 1)].rearrange("p a (g m t) -> p a g t m", t=PACK, m=16),
             )
-        clear_page(3, 4, placed.tile([P, T2], F32, name="page3", align_bytes=ALIGN, offset=0))
-        load_wb(staged.tile([P, PACK, N], F32, name="wb_raw1", align_bytes=ALIGN, offset=window_at + T - ALIGN))
 
         v_words = {}
 
-        def gather_words(a, lo, hi):
-            got = sb([P, hi - lo], U32, f"v_words{a}_{lo}")
+        def gather_words(a, lo, hi, at=None):
+            if at is None:
+                got = sb([P, hi - lo], U32, f"v_words{a}_{lo}")
+            else:
+                got = staged.tile([P, hi - lo], U32, name="v_words_rest", align_bytes=ALIGN, offset=at)
             nc.vector.tensor_copy(got[:], table[a][:].bitcast(U32).indirect(pick[:, lo // GROUP : hi // GROUP]))
             for j in range(lo, hi, SUB):
                 v_words[a, j] = got[:, j - lo : j - lo + SUB]
 
         gather_words(0, 0, S)
-        load_wb(sb([P, PACK, N], F32, "wb_raw2", "table0"))
+        load_wb(sb([P, PACK, N], F32, "wb_raw1", "table0"))
+        load_wb(placed.tile([P, PACK, N], F32, name="wb_raw2", align_bytes=ALIGN, offset=2048))
         gather_words(1, 0, BLOCK)
-        gather_words(1, BLOCK, S)
+        gather_words(1, BLOCK, half)
+        gather_words(1, half, S, rest_at)
         weight = sb([P, S], F32, "weight", "table1")
         nc.sync.dma_start(weight[:], wgo)
 
@@ -180,7 +186,7 @@ def tile_list_armband_gain_sensitivity_kernel(
             v_scale[0, j] = v_plane[0][:, j : j + SUB]
 
         def move_late_scales():
-            late = sb([P, half], U8, "v_plane_late")
+            late = sb([P, half], U8, "v_plane_late", "wa_scale_raw")
             nc.sync.dma_start(late[:].bitcast(I32)[0:MOVED, :], got32[SHIFT : SHIFT + MOVED, half // 4 :])
             for j in range(half, S, SUB):
                 v_scale[0, j] = late[:, j - half : j - half + SUB]
@@ -193,10 +199,9 @@ def tile_list_armband_gain_sensitivity_kernel(
             return f"bank{filled[-1]}"
 
         def first_matmul(acc, b, j, t, a, start, stop):
-            col = 512 * b + P * t
             nc.tensor.matmul_mx(
                 out=acc[:, t, :],
-                lhsT=wa_codes[a][:, 2 * col : 2 * (col + P)].bitcast(FP4X4),
+                lhsT=wa_codes[b][:, a, 2 * P * t : 2 * P * (t + 1)].bitcast(FP4X4),
                 lhsT_scale=wa_plane[b][:, a, P * t : P * (t + 1)],
                 rhs=v_words[a, j].bitcast(FP8X4),
                 rhs_scale=v_scale[a, j],
@@ -350,6 +355,7 @@ def tile_list_armband_gain_sensitivity_kernel(
         quantise_h()
         quantise_wb((2, 0))
         opening = [slope_on_vector(*second_product((0,), (i,), FIRST_BANKS + i)) for i in low]
+        clear_page(3, 4, sb([P, T2], F32, "page3"))
         quantise_wb((1, 2), (2, 2))
         first_product(1, every_pass)
         for i in low:

@@ -22,14 +22,16 @@ GROUP = 16
 QUADS = 4
 K_PASSES = K // 512
 H_PASSES = H // 512
-BLOCK = 256
+BATCH = 256
+HALF = S // 2
 SUB = 128
-BANKS = 8
 FIRST_BANKS = 6
 ALIGN = 64
 SHIFT = 14
 MOVED = 112
 SPARE = 3
+WA_PASS = 256
+VECTOR_CLEARS = 1280
 
 
 def tile_list_armband_gain_sensitivity_kernel(
@@ -45,11 +47,11 @@ def tile_list_armband_gain_sensitivity_kernel(
         spots = {}
         end = 0
         for chain in (
-            (("wb_bf1_0", 4 * P * PACK), ("h_codes0", 12 * BLOCK)),
-            (("wb_bf2_0", 4 * P * PACK), ("h_codes1", 12 * BLOCK)),
-            (("square0", 4 * BLOCK), ("page3", 4 * T2)),
-            (("square2", 8 * BLOCK), ("h_codes2", 12 * BLOCK)),
-            (("bridge", 4 * BLOCK), ("h_bf3_2", 8 * BLOCK), ("weighted4_0", 4 * BLOCK)),
+            (("wb_bf1_0", 4 * P * PACK), ("h_codes0", 12 * BATCH)),
+            (("wb_bf2_0", 4 * P * PACK), ("h_codes1", 12 * BATCH)),
+            (("square0", 4 * BATCH), ("page3", 4 * T2)),
+            (("square2", 8 * BATCH), ("h_codes2", 12 * BATCH)),
+            (("bridge", 4 * BATCH), ("h_bf3_2", 8 * BATCH), ("weighted4_0", 4 * BATCH)),
         ):
             for name, size in chain:
                 spots[name] = end
@@ -65,18 +67,17 @@ def tile_list_armband_gain_sensitivity_kernel(
         pick = lists.tile([P, S // GROUP], U16, name="pick")
         place = lists.tile([P, S // GROUP], U16, name="place")
 
-        window_at = 4 * T - ALIGN
+        window_at = 4 * PACK * N - ALIGN
+        rest_at = window_at + T - ALIGN
         scale_window = staged.tile([P, T], U8, name="scale_window", align_bytes=ALIGN, offset=window_at)
-        wa_at = 0
-        wa_first = placed.tile([P, K_PASSES, 256], I32, name="wa_first", align_bytes=ALIGN, offset=wa_at + ALIGN)
+        wa_first = placed.tile([P, K_PASSES, WA_PASS], I32, name="wa_first", align_bytes=ALIGN, offset=ALIGN)
         wa_rows = wa_words.bitcast(I32).rearrange("a p c -> p a c")
         wa_scale_raw = sb([P, K_PASSES, H], U8, "wa_scale_raw")
         scale_got = sb([P, S], U8, "scale_got")
-        half = S // 2
-        v_plane = [sb([P, half], U8, "v_plane0"), sb([P, S], U8, "v_plane1")]
+        v_plane = [sb([P, HALF], U8, "v_plane0"), sb([P, S], U8, "v_plane1")]
 
         zero_a = sb([P, 1], F32, "zero_a", "table0")
-        silu_in = placed.tile([P, 1], F32, name="silu_in", align_bytes=ALIGN, offset=wa_at + ALIGN)
+        silu_in = placed.tile([P, 1], F32, name="silu_in", align_bytes=ALIGN, offset=ALIGN)
         bias_in = sb([P, 1], F32, "bias_in", "table1")
         zero_bias = sb([P, 1], F32, "zero_bias")
 
@@ -108,7 +109,7 @@ def tile_list_armband_gain_sensitivity_kernel(
         wa_scale32 = wa_scale_raw[:].bitcast(I32)
         for d in range(QUADS):
             nc.sync.dma_start(wa_scale32[32 * d : 32 * d + 4, :, :], wa_scale_rows[4 * d : 4 * d + 4, :, :])
-        nc.sync.dma_start(wa_first[:], wa_rows[:, :, 0:256])
+        nc.sync.dma_start(wa_first[:], wa_rows[:, :, 0:WA_PASS])
 
         wb_rows = wb.rearrange("(b p t) n -> b p t n", b=H_PASSES, t=PACK)
         wb_raw = []
@@ -130,20 +131,20 @@ def tile_list_armband_gain_sensitivity_kernel(
         for i in range(2):
             clear_page(i, 2, sb([P, T2], F32, f"page{i}"))
         pages[2] = sb([P, T2], F32, "page2")
-        clear_words(pages[2][:])
+        clear_words(pages[2][:, 0:VECTOR_CLEARS])
+        nc.gpsimd.memset(pages[2][:, VECTOR_CLEARS:], 0.0)
 
         nc.vector.tensor_copy(scale_got[:], scale_window[:].indirect(pick[:]))
         got32 = scale_got[:].bitcast(I32)
-        nc.sync.dma_start(v_plane[0][:].bitcast(I32)[0:MOVED, :], got32[SHIFT : SHIFT + MOVED, 0 : half // 4])
+        nc.sync.dma_start(v_plane[0][:].bitcast(I32)[0:MOVED, :], got32[SHIFT : SHIFT + MOVED, 0 : HALF // 4])
         for row in range(4):
             nc.sync.dma_start(v_plane[1][:].bitcast(I32)[row:P:32, :], got32[8 * row + SPARE : P : 32, :])
-        rest_at = window_at + T - ALIGN
-        wa_rest = staged.tile([P, K_PASSES, 512], I32, name="wa_rest", align_bytes=ALIGN, offset=rest_at)
-        nc.sync.dma_start(wa_rest[:], wa_rows[:, :, 256:])
+        wa_rest = staged.tile([P, K_PASSES, 2 * WA_PASS], I32, name="wa_rest", align_bytes=ALIGN, offset=rest_at)
+        nc.sync.dma_start(wa_rest[:], wa_rows[:, :, WA_PASS:])
         load_wb(staged.tile([P, PACK, N], F32, name="wb_raw0", align_bytes=ALIGN, offset=0))
 
         wa_codes = []
-        for b, raw in enumerate((wa_first[:], wa_rest[:, :, 0:256], wa_rest[:, :, 256:])):
+        for b, raw in enumerate((wa_first[:], wa_rest[:, :, 0:WA_PASS], wa_rest[:, :, WA_PASS:])):
             wa_codes.append(sb([P, K_PASSES, 1024], U8, f"wa_codes{b}"))
             nc.vector.tensor_copy(
                 wa_codes[b][:].bitcast(U16).rearrange("p a (t g m) -> p a g t m", t=PACK, m=8),
@@ -151,11 +152,10 @@ def tile_list_armband_gain_sensitivity_kernel(
             )
         wa_plane = []
         for b in range(H_PASSES):
-            if b == 0:
-                wa_plane.append(sb([P, K_PASSES, 512], U8, "wa_plane0"))
+            if b < H_PASSES - 1:
+                wa_plane.append(sb([P, K_PASSES, 512], U8, f"wa_plane{b}"))
             else:
-                at = wa_at + 1024 * (b - 1)
-                wa_plane.append(placed.tile([P, K_PASSES, 512], U8, name=f"wa_plane{b}", align_bytes=ALIGN, offset=at))
+                wa_plane.append(placed.tile([P, K_PASSES, 512], U8, name="wa_plane2", align_bytes=ALIGN, offset=0))
             nc.gpsimd.tensor_copy(
                 wa_plane[b][:].rearrange("p a (t g m) -> p a g t m", t=PACK, m=16),
                 wa_scale_raw[:, :, 512 * b : 512 * (b + 1)].rearrange("p a (g m t) -> p a g t m", t=PACK, m=16),
@@ -174,24 +174,24 @@ def tile_list_armband_gain_sensitivity_kernel(
 
         gather_words(0, 0, S)
         load_wb(sb([P, PACK, N], F32, "wb_raw1", "table0"))
-        load_wb(placed.tile([P, PACK, N], F32, name="wb_raw2", align_bytes=ALIGN, offset=2048))
-        gather_words(1, 0, BLOCK)
-        gather_words(1, BLOCK, half)
-        gather_words(1, half, S, rest_at)
+        load_wb(placed.tile([P, PACK, N], F32, name="wb_raw2", align_bytes=ALIGN, offset=8 * WA_PASS))
+        gather_words(1, 0, BATCH)
+        gather_words(1, BATCH, HALF)
+        gather_words(1, HALF, S, rest_at)
         weight = sb([P, S], F32, "weight", "table1")
         nc.sync.dma_start(weight[:], wgo)
 
         v_scale = {(1, j): v_plane[1][:, j : j + SUB] for j in range(0, S, SUB)}
-        for j in range(0, half, SUB):
+        for j in range(0, HALF, SUB):
             v_scale[0, j] = v_plane[0][:, j : j + SUB]
 
         def move_late_scales():
-            late = sb([P, half], U8, "v_plane_late", "wa_scale_raw")
-            nc.sync.dma_start(late[:].bitcast(I32)[0:MOVED, :], got32[SHIFT : SHIFT + MOVED, half // 4 :])
-            for j in range(half, S, SUB):
-                v_scale[0, j] = late[:, j - half : j - half + SUB]
+            late = sb([P, HALF], U8, "v_plane_late", "wa_scale_raw")
+            nc.sync.dma_start(late[:].bitcast(I32)[0:MOVED, :], got32[SHIFT : SHIFT + MOVED, HALF // 4 :])
+            for j in range(HALF, S, SUB):
+                v_scale[0, j] = late[:, j - HALF : j - HALF + SUB]
 
-        h_codes, h_plane, block_codes, block_plane = {}, {}, {}, {}
+        h_codes, h_plane, batch_codes, batch_plane = {}, {}, {}, {}
         filled = []
 
         def next_bank():
@@ -212,34 +212,34 @@ def tile_list_armband_gain_sensitivity_kernel(
         waiting = []
 
         def quantise_h():
-            for block, b, rounded in waiting:
-                cols = slice(b // 2 * 2 * BLOCK, (b + 1) * BLOCK)
+            for batch, b, rounded in waiting:
+                cols = slice(b // 2 * 2 * BATCH, (b + 1) * BATCH)
                 nc.vector.quantize_mx(
-                    out=block_codes[block][:, cols].bitcast(FP8X4),
-                    scales=block_plane[block][:, cols],
+                    out=batch_codes[batch][:, cols].bitcast(FP8X4),
+                    scales=batch_plane[batch][:, cols],
                     in_=rounded[:].rearrange("p j t -> p (j t)"),
                 )
             waiting.clear()
 
-        def first_product(block, passes, early=()):
-            lo = block * BLOCK
+        def first_product(batch, passes, early=()):
+            lo = batch * BATCH
             accs = {}
             for b in early:
-                for j in range(lo, lo + BLOCK, SUB):
+                for j in range(lo, lo + BATCH, SUB):
                     accs[b, j] = psum.tile([P, PACK, SUB], F32, name="acc", tag=next_bank())
                     for t in range(PACK):
                         first_matmul(accs[b, j], b, j, t, 0, t == 0, False)
             for b in passes:
                 if b == 0:
-                    block_codes[block] = sb([P, H_PASSES * BLOCK], U32, f"h_codes{block}")
-                h_codes[block, b] = block_codes[block][:, b * BLOCK : (b + 1) * BLOCK]
+                    batch_codes[batch] = sb([P, H_PASSES * BATCH], U32, f"h_codes{batch}")
+                h_codes[batch, b] = batch_codes[batch][:, b * BATCH : (b + 1) * BATCH]
                 if b == 0:
-                    block_plane[block] = sb([P, H_PASSES * BLOCK], U8, f"h_plane{block}")
-                h_plane[block, b] = block_plane[block][:, b * BLOCK : (b + 1) * BLOCK]
+                    batch_plane[batch] = sb([P, H_PASSES * BATCH], U8, f"h_plane{batch}")
+                h_plane[batch, b] = batch_plane[batch][:, b * BATCH : (b + 1) * BATCH]
                 if b != 1:
-                    rounded = sb([P, (2 - b // 2) * BLOCK, PACK], BF16, f"h_bf{block}_{b}")
-                h_bf = rounded[:, b % 2 * BLOCK : (b % 2 + 1) * BLOCK, :]
-                for j in range(lo, lo + BLOCK, SUB):
+                    rounded = sb([P, (2 - b // 2) * BATCH, PACK], BF16, f"h_bf{batch}_{b}")
+                h_bf = rounded[:, b % 2 * BATCH : (b % 2 + 1) * BATCH, :]
+                for j in range(lo, lo + BATCH, SUB):
                     if b in early:
                         acc = accs[b, j]
                         for t in range(PACK):
@@ -256,8 +256,8 @@ def tile_list_armband_gain_sensitivity_kernel(
                         bias=zero_bias[:] if (b, j) == (0, 0) else 0.0,
                     )
                 if b != 0:
-                    waiting.append((block, b, rounded))
-                if block != 0:
+                    waiting.append((batch, b, rounded))
+                if batch != 0:
                     quantise_h()
 
         wb_codes, wb_plane = {}, {}
@@ -287,52 +287,50 @@ def tile_list_armband_gain_sensitivity_kernel(
         out_pages = out.rearrange("(p i) t -> i p t", i=PACK)
         steps = []
 
-        def second_product(blocks, step_pages, bank):
+        def second_product(batches, step_pages, bank):
             n = len(steps)
             steps.append(n)
-            parts = [(i, block) for i in step_pages for block in blocks]
-            q = psum.tile([P, len(parts), BLOCK], F32, name="q", tag=f"bank{bank}")
-            for part, (i, block) in enumerate(parts):
+            parts = [(i, batch) for i in step_pages for batch in batches]
+            u = psum.tile([P, len(parts), BATCH], F32, name="q", tag=f"bank{bank}")
+            for part, (i, batch) in enumerate(parts):
                 for b in range(H_PASSES):
                     nc.tensor.matmul_mx(
-                        out=q[:, part, :],
+                        out=u[:, part, :],
                         lhsT=wb_codes[b, i].bitcast(FP8X4),
                         lhsT_scale=wb_plane[b, i],
-                        rhs=h_codes[block, b].bitcast(FP8X4),
-                        rhs_scale=h_plane[block, b],
+                        rhs=h_codes[batch, b].bitcast(FP8X4),
+                        rhs_scale=h_plane[batch, b],
                         start=(b == 0),
                         stop=(b == H_PASSES - 1),
                     )
-            q_flat = q[:].rearrange("p e j -> p (e j)")
-            drive = sb([P, len(parts) * BLOCK], F32, f"drive{n}", f"drive{n % 2}")
-            nc.scalar.activation(drive[:], q_flat, ACT.Tanh)
-            return n, parts, q_flat, drive
+            u_flat = u[:].rearrange("p e j -> p (e j)")
+            drive = sb([P, len(parts) * BATCH], F32, f"drive{n}", f"drive{n % 2}")
+            nc.scalar.activation(drive[:], u_flat, ACT.Tanh)
+            return n, parts, u_flat, drive
 
-        def slope_on_vector(n, parts, q_flat, drive):
-            square = sb([P, len(parts) * BLOCK], F32, f"square{n}")
+        def slope_on_vector(n, parts, u_flat, drive):
+            square = sb([P, len(parts) * BATCH], F32, f"square{n}")
             nc.scalar.activation(square[:], drive[:], ACT.Square)
-            slope = sb([P, len(parts) * BLOCK], F32, f"slope{n}")
-            nc.vector.scalar_tensor_tensor(slope[:], square[:], 1.0, q_flat, ALU.subtract, ALU.mult)
+            slope = sb([P, len(parts) * BATCH], F32, f"slope{n}")
+            nc.vector.scalar_tensor_tensor(slope[:], square[:], 1.0, u_flat, ALU.subtract, ALU.mult)
             return slope
 
-        def values_on_gpsimd(n, parts, q_flat, drive, piece=BLOCK, weighted=True):
-            width = len(parts) * BLOCK
+        def values_on_gpsimd(n, parts, u_flat, drive, weighted=True):
+            width = len(parts) * BATCH
             gated = sb([P, width], F32, f"gated{n}")
-            nc.scalar.activation(gated[:], q_flat, ACT.Silu, scale=-2.0)
+            nc.scalar.activation(gated[:], u_flat, ACT.Silu, scale=-2.0)
             rest = sb([P, width], F32, f"rest{n}")
             nc.scalar.activation(rest[:], drive[:], ACT.Identity, bias=1.0)
             values = sb([P, width], F32, f"values{n}")
-            lo = parts[0][1] * BLOCK
-            run = width if parts[0][0] == parts[-1][0] else BLOCK
+            lo = parts[0][1] * BATCH
+            run = width if parts[0][0] == parts[-1][0] else BATCH
             for at in range(0, width, run):
                 factor = gated[:, at : at + run]
                 if weighted:
                     product = sb([P, run], F32, f"weighted{n}_{at}")
                     nc.gpsimd.tensor_tensor(product[:], factor, weight[:, lo : lo + run], ALU.mult)
                     factor = product[:]
-                for part in range(0, run, piece):
-                    cols = slice(at + part, at + part + piece)
-                    nc.gpsimd.tensor_tensor(values[:, cols], factor[:, part : part + piece], rest[:, cols], ALU.mult)
+                nc.gpsimd.tensor_tensor(values[:, at : at + run], factor, rest[:, at : at + run], ALU.mult)
             return values
 
         def put(i, lo, values, weighted):
@@ -362,19 +360,22 @@ def tile_list_armband_gain_sensitivity_kernel(
             put(i, 0, opening[i][:], False)
         slope = slope_on_vector(*second_product((0,), high, FIRST_BANKS))
         for part, i in enumerate(high):
-            put(i, 0, slope[:, part * BLOCK : (part + 1) * BLOCK], False)
+            put(i, 0, slope[:, part * BATCH : (part + 1) * BATCH], False)
         first_product(2, every_pass)
         first_product(3, (0, 1))
         bridge_slope = slope_on_vector(*second_product((1,), low, filled[-3]))
-        put(0, BLOCK, bridge_slope[:, 0:BLOCK], False)
+        put(0, BATCH, bridge_slope[:, 0:BATCH], False)
         first_product(3, (2,))
-        bridge = sb([P, BLOCK], F32, "bridge")
-        nc.vector.tensor_tensor(bridge[:], bridge_slope[:, BLOCK:], weight[:, BLOCK : 2 * BLOCK], ALU.mult)
-        put(1, BLOCK, bridge[:], True)
+        bridge = sb([P, BATCH], F32, "bridge")
+        nc.vector.tensor_tensor(bridge[:], bridge_slope[:, BATCH:], weight[:, BATCH : 2 * BATCH], ALU.mult)
+        put(1, BATCH, bridge[:], True)
 
         for i, bank in ((2, filled[-3]), (3, filled[-2])):
-            put(i, BLOCK, values_on_gpsimd(*second_product((1,), (i,), bank))[:], True)
-        for i, bank in ((0, filled[-1]), (1, FIRST_BANKS + 1), (2, FIRST_BANKS)):
-            put(i, 2 * BLOCK, values_on_gpsimd(*second_product((2, 3), (i,), bank), 2 * BLOCK)[:], True)
+            put(i, BATCH, values_on_gpsimd(*second_product((1,), (i,), bank))[:], True)
+        for batch, bank in ((2, FIRST_BANKS + 1), (3, filled[-1])):
+            values = values_on_gpsimd(*second_product((batch,), low, bank))
+            for i in low:
+                put(i, batch * BATCH, values[:, i * BATCH : (i + 1) * BATCH], True)
+        put(2, 2 * BATCH, values_on_gpsimd(*second_product((2, 3), (2,), FIRST_BANKS))[:], True)
         last = second_product((2, 3), (3,), filled[-4])
-        put(3, 2 * BLOCK, values_on_gpsimd(*last, 2 * BLOCK, weighted=False)[:], False)
+        put(3, 2 * BATCH, values_on_gpsimd(*last, weighted=False)[:], False)

@@ -268,8 +268,8 @@ def tile_list_armband_gain_sensitivity_kernel(
             rounded = sb([P, count, P, PACK], BF16, f"wb_bf{b}_{first_page}")
             for e, (c, page) in enumerate(halves):
                 nc.vector.tensor_scalar_mul(
-                    rounded[:, 2 * e : 2 * e + 2, :, :].rearrange("p i m t -> p m i t"),
-                    wb_raw[c][:].rearrange("p t (m i) -> p m i t", i=PACK)[:, :, page : page + 2, :],
+                    rounded[:, 2 * e : 2 * e + 2, :, :].rearrange("p i m t -> p m t i"),
+                    wb_raw[c][:].rearrange("p t (m i) -> p m t i", i=PACK)[:, :, :, page : page + 2],
                     -1.0,
                 )
             codes = sb([P, count * P], U32, f"wb_codes{b}_{first_page}")

@@ -23,14 +23,13 @@ QUADS = 4
 K_PASSES = K // 512
 H_PASSES = H // 512
 BATCH = 256
-HALF = S // 2
 SUB = 128
 FIRST_BANKS = 6
 ALIGN = 64
 SHIFT = 14
 MOVED = 112
 SPARE = 3
-WA_PASS = 256
+EARLY = (0,)
 VECTOR_CLEARS = 1280
 
 
@@ -41,16 +40,13 @@ def tile_list_armband_gain_sensitivity_kernel(
     with ExitStack() as ctx:
         lists = ctx.enter_context(tc.tile_pool(name="lists", bufs=1))
         keep = ctx.enter_context(tc.tile_pool(name="keep", bufs=1))
-        placed = ctx.enter_context(tc.tile_pool(name="placed", bufs=1))
         held = ctx.enter_context(tc.tile_pool(name="held", bufs=1))
-        staged = ctx.enter_context(tc.tile_pool(name="staged", bufs=1))
         spots = {}
         end = 0
         for chain in (
-            (("wb_bf1_0", 4 * P * PACK), ("h_codes0", 12 * BATCH)),
             (("wb_bf2_0", 4 * P * PACK), ("h_codes1", 12 * BATCH)),
-            (("square0", 4 * BATCH), ("page3", 4 * T2)),
-            (("square2", 8 * BATCH), ("h_codes2", 12 * BATCH)),
+            (("wa_raw0", 2 * H), ("silu_in", ALIGN * 2), ("wa_raw1", 2 * H), ("wb_raw2", 4 * PACK * N)),
+            (("zero_mid", ALIGN * 2), ("table1", 4 * T)),
             (("bridge", 4 * BATCH), ("h_bf3_2", 8 * BATCH), ("weighted4_0", 4 * BATCH)),
         ):
             for name, size in chain:
@@ -66,186 +62,139 @@ def tile_list_armband_gain_sensitivity_kernel(
 
         pick = lists.tile([P, S // GROUP], U16, name="pick")
         place = lists.tile([P, S // GROUP], U16, name="place")
-
-        window_at = 4 * PACK * N - ALIGN
-        rest_at = window_at + T - ALIGN
-        scale_window = staged.tile([P, T], U8, name="scale_window", align_bytes=ALIGN, offset=window_at)
-        wa_first = placed.tile([P, K_PASSES, WA_PASS], I32, name="wa_first", align_bytes=ALIGN, offset=ALIGN)
-        wa_rows = wa_words.bitcast(I32).rearrange("a p c -> p a c")
+        scale_window = sb([P, T], U8, "scale_window")
         wa_scale_raw = sb([P, K_PASSES, H], U8, "wa_scale_raw")
         scale_got = sb([P, S], U8, "scale_got")
-        v_plane = [sb([P, HALF], U8, "v_plane0"), sb([P, S], U8, "v_plane1")]
-
-        zero_a = sb([P, 1], F32, "zero_a", "table0")
-        silu_in = placed.tile([P, 1], F32, name="silu_in", align_bytes=ALIGN, offset=ALIGN)
-        bias_in = sb([P, 1], F32, "bias_in", "table1")
+        zero = sb([P, 1], F32, "zero", "table0")
+        silu_in = sb([P, ALIGN // 2], F32, "silu_in")
+        zero_mid = sb([P, ALIGN // 2], F32, "zero_mid")
         zero_bias = sb([P, 1], F32, "zero_bias")
+        pages = {i: sb([P, T2], F32, f"page{i}") for i in range(PACK - 1)}
 
-        def clear_words(words):
+        def clear_on_vector(words):
             odd = words.shape[1] // 2 + 1
             nc.vector.memset(words[:, 0:odd], 0)
             nc.vector.memset(words[:, odd:], 0)
 
+        def clear_on_gpsimd(words, piece):
+            for lo in range(0, words.shape[1], piece):
+                nc.gpsimd.memset(words[:, lo : lo + piece], 0.0)
+
+        nc.gpsimd.memset(zero[:], 0.0)
         nc.gpsimd.memset(scale_window[:].bitcast(I32), 0)
-        nc.vector.memset(zero_a[:], 0.0)
-        zero_b = sb([P, 1], F32, "zero_b")
-        nc.vector.tensor_copy(zero_b[:], zero_a[:])
-        clear_words(wa_scale_raw[:].rearrange("p a c -> p (a c)").bitcast(I32))
-        nc.vector.tensor_copy(silu_in[:], zero_b[:])
-        nc.vector.tensor_copy(bias_in[:], silu_in[:])
-        nc.scalar.activation(zero_bias[:], bias_in[:], ACT.Silu)
+        nc.gpsimd.tensor_copy(silu_in[:, 0:1], zero[:])
+        clear_on_vector(wa_scale_raw[:].rearrange("p a c -> p (a c)").bitcast(I32))
+        clear_on_vector(pages[2][:, 0:VECTOR_CLEARS])
 
         nc.sync.dma_start(pick[:], offs)
         nc.sync.dma_start(place[:], offs2)
         tab_scale_rows = tab_scales.bitcast(I32)
         window32 = scale_window[:].bitcast(I32)
+        nc.sync.dma_start(window32[SPARE:P:8, :], tab_scale_rows[1])
         for d in range(QUADS):
             nc.sync.dma_start(window32[32 * d + SHIFT : 32 * d + SHIFT + 4, :], tab_scale_rows[0, 4 * d : 4 * d + 4, :])
-        nc.sync.dma_start(window32[SPARE:P:8, :], tab_scale_rows[1])
-        table_rows = [tab_words[a].rearrange("p t i -> p (t i)").bitcast(I32) for a in range(K_PASSES)]
-        table = [sb([P, T], I32, "table0")]
-        nc.sync.dma_start(table[0][:], table_rows[0])
-        wa_scale_rows = wa_scales.bitcast(I32).rearrange("a q c -> q a c")
+        nc.scalar.activation(zero_mid[:, 0:1], silu_in[:, 0:1], ACT.Silu)
+        nc.scalar.activation(zero_bias[:], zero_mid[:, 0:1], ACT.Tanh)
+        table = []
+
+        def load_table(a):
+            table.append(sb([P, T], I32, f"table{a}"))
+            nc.sync.dma_start(table[a][:], tab_words[a].rearrange("p t i -> p (t i)").bitcast(I32))
+
+        load_table(0)
+        wa_scale_rows = wa_scales.bitcast(I32).rearrange("a (d r) c -> r d a c", r=4)
         wa_scale32 = wa_scale_raw[:].bitcast(I32)
-        for d in range(QUADS):
-            nc.sync.dma_start(wa_scale32[32 * d : 32 * d + 4, :, :], wa_scale_rows[4 * d : 4 * d + 4, :, :])
-        nc.sync.dma_start(wa_first[:], wa_rows[:, :, 0:WA_PASS])
+        for row in range(4):
+            nc.sync.dma_start(wa_scale32[row:P:32, :, :], wa_scale_rows[row])
+        wa_raw = []
+        for a in range(K_PASSES):
+            wa_raw.append(sb([P, H // 2], I32, f"wa_raw{a}"))
+            nc.sync.dma_start(wa_raw[a][:], wa_words.bitcast(I32)[a])
+        load_table(1)
 
-        wb_rows = wb.rearrange("(b p t) n -> b p t n", b=H_PASSES, t=PACK)
-        wb_raw = []
-
-        def load_wb(rows):
-            nc.sync.dma_start(rows[:], wb_rows[len(wb_raw)])
-            wb_raw.append(rows)
-
-        table.append(sb([P, T], I32, "table1"))
-        nc.sync.dma_start(table[1][:], table_rows[1])
-
-        pages = {}
-
-        def clear_page(i, pieces, page):
-            pages[i] = page
-            for lo in range(0, T2, T2 // pieces):
-                nc.gpsimd.memset(pages[i][:, lo : lo + T2 // pieces], 0.0)
-
-        for i in range(2):
-            clear_page(i, 2, sb([P, T2], F32, f"page{i}"))
-        pages[2] = sb([P, T2], F32, "page2")
-        clear_words(pages[2][:, 0:VECTOR_CLEARS])
-        nc.gpsimd.memset(pages[2][:, VECTOR_CLEARS:], 0.0)
+        clear_on_gpsimd(pages[0][:], T2 // 2)
+        clear_on_gpsimd(pages[1][:], T2 // 2)
 
         nc.vector.tensor_copy(scale_got[:], scale_window[:].indirect(pick[:]))
         got32 = scale_got[:].bitcast(I32)
-        nc.sync.dma_start(v_plane[0][:].bitcast(I32)[0:MOVED, :], got32[SHIFT : SHIFT + MOVED, 0 : HALF // 4])
-        for row in range(4):
-            nc.sync.dma_start(v_plane[1][:].bitcast(I32)[row:P:32, :], got32[8 * row + SPARE : P : 32, :])
-        wa_rest = staged.tile([P, K_PASSES, 2 * WA_PASS], I32, name="wa_rest", align_bytes=ALIGN, offset=rest_at)
-        nc.sync.dma_start(wa_rest[:], wa_rows[:, :, WA_PASS:])
-        load_wb(staged.tile([P, PACK, N], F32, name="wb_raw0", align_bytes=ALIGN, offset=0))
+        v_plane = []
 
-        wa_codes = []
-        for b, raw in enumerate((wa_first[:], wa_rest[:, :, 0:WA_PASS], wa_rest[:, :, WA_PASS:])):
-            wa_codes.append(sb([P, K_PASSES, 1024], U8, f"wa_codes{b}"))
-            nc.vector.tensor_copy(
-                wa_codes[b][:].bitcast(U16).rearrange("p a (t g m) -> p a g t m", t=PACK, m=8),
-                raw.bitcast(U16).rearrange("p a (g m t) -> p a g t m", t=PACK, m=8),
-            )
-        wa_plane = []
-        for b in range(H_PASSES):
-            if b < H_PASSES - 1:
-                wa_plane.append(sb([P, K_PASSES, 512], U8, f"wa_plane{b}"))
-            else:
-                wa_plane.append(placed.tile([P, K_PASSES, 512], U8, name="wa_plane2", align_bytes=ALIGN, offset=0))
-            nc.gpsimd.tensor_copy(
-                wa_plane[b][:].rearrange("p a (t g m) -> p a g t m", t=PACK, m=16),
-                wa_scale_raw[:, :, 512 * b : 512 * (b + 1)].rearrange("p a (g m t) -> p a g t m", t=PACK, m=16),
-            )
+        def move_scales():
+            v_plane.extend((sb([P, S // 2], U8, "v_plane0"), sb([P, S], U8, "v_plane1")))
+            nc.sync.dma_start(v_plane[0][:].bitcast(I32)[0:MOVED, :], got32[SHIFT : SHIFT + MOVED, 0 : S // 8])
+            for row in range(4):
+                nc.sync.dma_start(v_plane[1][:].bitcast(I32)[row:P:32, :], got32[8 * row + SPARE : P : 32, :])
+
+        wa_codes, wa_plane = {}, {}
+        for a in range(K_PASSES):
+            if a == 1:
+                move_scales()
+            for b in range(H_PASSES):
+                wa_codes[a, b] = sb([P, 1024], U8, f"wa_codes{a}_{b}")
+                nc.scalar.copy(
+                    wa_codes[a, b][:].bitcast(U16).rearrange("p (t g m) -> p g t m", t=PACK, m=8),
+                    wa_raw[a][:, 256 * b : 256 * (b + 1)].bitcast(U16).rearrange("p (g m t) -> p g t m", t=PACK, m=8),
+                )
+                wa_plane[a, b] = sb([P, 512], U8, f"wa_plane{a}_{b}")
+                nc.gpsimd.tensor_copy(
+                    wa_plane[a, b][:].rearrange("p (t g m) -> p g t m", t=PACK, m=16),
+                    wa_scale_raw[:, a, 512 * b : 512 * (b + 1)].rearrange("p (g m t) -> p g t m", t=PACK, m=16),
+                )
+
+        clear_on_gpsimd(pages[2][:, VECTOR_CLEARS:], T2 - VECTOR_CLEARS)
 
         v_words = {}
 
-        def gather_words(a, lo, hi, at=None):
-            if at is None:
-                got = sb([P, hi - lo], U32, f"v_words{a}_{lo}")
-            else:
-                got = staged.tile([P, hi - lo], U32, name="v_words_rest", align_bytes=ALIGN, offset=at)
+        def gather_words(a, lo, hi):
+            got = sb([P, hi - lo], U32, f"v_words{a}_{lo}")
             nc.vector.tensor_copy(got[:], table[a][:].bitcast(U32).indirect(pick[:, lo // GROUP : hi // GROUP]))
             for j in range(lo, hi, SUB):
                 v_words[a, j] = got[:, j - lo : j - lo + SUB]
 
-        gather_words(0, 0, S)
-        load_wb(sb([P, PACK, N], F32, "wb_raw1", "table0"))
-        load_wb(placed.tile([P, PACK, N], F32, name="wb_raw2", align_bytes=ALIGN, offset=8 * WA_PASS))
+        gather_words(0, 0, BATCH)
+        gather_words(0, BATCH, S)
         gather_words(1, 0, BATCH)
-        gather_words(1, BATCH, HALF)
-        gather_words(1, HALF, S, rest_at)
-        weight = sb([P, S], F32, "weight", "table1")
-        nc.sync.dma_start(weight[:], wgo)
+        gather_words(1, BATCH, S)
 
-        v_scale = {(1, j): v_plane[1][:, j : j + SUB] for j in range(0, S, SUB)}
-        for j in range(0, HALF, SUB):
-            v_scale[0, j] = v_plane[0][:, j : j + SUB]
+        wb_rows = wb.rearrange("(b p t) n -> b p t n", b=H_PASSES, t=PACK)
+        wb_raw = []
+        for b, tenant in enumerate(("scale_window", "table0", None)):
+            wb_raw.append(sb([P, PACK, N], F32, f"wb_raw{b}", tenant))
+            nc.sync.dma_start(wb_raw[b][:], wb_rows[b])
 
-        def move_late_scales():
-            late = sb([P, HALF], U8, "v_plane_late", "wa_scale_raw")
-            nc.sync.dma_start(late[:].bitcast(I32)[0:MOVED, :], got32[SHIFT : SHIFT + MOVED, HALF // 4 :])
-            for j in range(HALF, S, SUB):
-                v_scale[0, j] = late[:, j - HALF : j - HALF + SUB]
+        h_codes, h_plane, h_rounded = {}, {}, {}
 
-        h_codes, h_plane, batch_codes, batch_plane = {}, {}, {}, {}
-        filled = []
-
-        def next_bank():
-            filled.append(len(filled) % FIRST_BANKS)
-            return f"bank{filled[-1]}"
 
         def first_matmul(acc, b, j, t, a, start, stop):
             nc.tensor.matmul_mx(
                 out=acc[:, t, :],
-                lhsT=wa_codes[b][:, a, 2 * P * t : 2 * P * (t + 1)].bitcast(FP4X4),
-                lhsT_scale=wa_plane[b][:, a, P * t : P * (t + 1)],
+                lhsT=wa_codes[a, b][:, 2 * P * t : 2 * P * (t + 1)].bitcast(FP4X4),
+                lhsT_scale=wa_plane[a, b][:, P * t : P * (t + 1)],
                 rhs=v_words[a, j].bitcast(FP8X4),
-                rhs_scale=v_scale[a, j],
+                rhs_scale=v_plane[a][:, j : j + SUB] if a == 1 or j < S // 2 else v_plane[2][:, j - S // 2 : j - S // 2 + SUB],
                 start=start,
                 stop=stop,
             )
 
-        waiting = []
-
-        def quantise_h():
-            for batch, b, rounded in waiting:
-                cols = slice(b // 2 * 2 * BATCH, (b + 1) * BATCH)
-                nc.vector.quantize_mx(
-                    out=batch_codes[batch][:, cols].bitcast(FP8X4),
-                    scales=batch_plane[batch][:, cols],
-                    in_=rounded[:].rearrange("p j t -> p (j t)"),
-                )
-            waiting.clear()
-
-        def first_product(batch, passes, early=()):
+        def first_product(batch, passes, early=(), banks=range(FIRST_BANKS)):
             lo = batch * BATCH
             accs = {}
             for b in early:
                 for j in range(lo, lo + BATCH, SUB):
-                    accs[b, j] = psum.tile([P, PACK, SUB], F32, name="acc", tag=next_bank())
+                    accs[b, j] = psum.tile([P, PACK, SUB], F32, name="acc", tag=f"bank{banks[2 * b + (j - lo) // SUB]}")
                     for t in range(PACK):
                         first_matmul(accs[b, j], b, j, t, 0, t == 0, False)
             for b in passes:
-                if b == 0:
-                    batch_codes[batch] = sb([P, H_PASSES * BATCH], U32, f"h_codes{batch}")
-                h_codes[batch, b] = batch_codes[batch][:, b * BATCH : (b + 1) * BATCH]
-                if b == 0:
-                    batch_plane[batch] = sb([P, H_PASSES * BATCH], U8, f"h_plane{batch}")
-                h_plane[batch, b] = batch_plane[batch][:, b * BATCH : (b + 1) * BATCH]
                 if b != 1:
-                    rounded = sb([P, (2 - b // 2) * BATCH, PACK], BF16, f"h_bf{batch}_{b}")
-                h_bf = rounded[:, b % 2 * BATCH : (b % 2 + 1) * BATCH, :]
+                    h_rounded[batch, b // 2] = sb([P, (2 - b // 2) * BATCH, PACK], BF16, f"h_bf{batch}_{b}")
+                h_bf = h_rounded[batch, b // 2][:, b % 2 * BATCH : (b % 2 + 1) * BATCH, :]
                 for j in range(lo, lo + BATCH, SUB):
                     if b in early:
                         acc = accs[b, j]
                         for t in range(PACK):
                             first_matmul(acc, b, j, t, 1, False, t == PACK - 1)
                     else:
-                        acc = psum.tile([P, PACK, SUB], F32, name="acc", tag=next_bank())
+                        acc = psum.tile([P, PACK, SUB], F32, name="acc", tag=f"bank{banks[2 * b + (j - lo) // SUB]}")
                         for t in range(PACK):
                             first_matmul(acc, b, j, t, 1, True, False)
                             first_matmul(acc, b, j, t, 0, False, True)
@@ -255,34 +204,39 @@ def tile_list_armband_gain_sensitivity_kernel(
                         ACT.Relu,
                         bias=zero_bias[:] if (b, j) == (0, 0) else 0.0,
                     )
-                if b != 0:
-                    waiting.append((batch, b, rounded))
-                if batch != 0:
-                    quantise_h()
 
-        wb_codes, wb_plane = {}, {}
+        def quantise_h(batch, part):
+            if part == 0:
+                h_codes[batch] = sb([P, H_PASSES * BATCH], U32, f"h_codes{batch}")
+                h_plane[batch] = sb([P, H_PASSES * BATCH], U8, f"h_plane{batch}")
+            cols = slice(2 * part * BATCH, (2 + part) * BATCH)
+            nc.vector.quantize_mx(
+                out=h_codes[batch][:, cols].bitcast(FP8X4),
+                scales=h_plane[batch][:, cols],
+                in_=h_rounded[batch, part][:].rearrange("p j t -> p (j t)"),
+            )
 
-        def quantise_wb(*halves):
-            b, first_page = halves[0]
-            count = 2 * len(halves)
-            rounded = sb([P, count, P, PACK], BF16, f"wb_bf{b}_{first_page}")
-            for e, (c, page) in enumerate(halves):
-                nc.vector.tensor_scalar_mul(
-                    rounded[:, 2 * e : 2 * e + 2, :, :].rearrange("p i m t -> p m t i"),
-                    wb_raw[c][:].rearrange("p t (m i) -> p m t i", i=PACK)[:, :, :, page : page + 2],
-                    -1.0,
-                )
-            codes = sb([P, count * P], U32, f"wb_codes{b}_{first_page}")
-            plane = sb([P, count * P], U8, f"wb_plane{b}_{first_page}")
+        wb_rounded, wb_codes, wb_plane = {}, {}, {}
+
+        def round_wb(b, page):
+            wb_rounded[b, page] = sb([P, 2, P, PACK], BF16, f"wb_bf{b}_{page}")
+            nc.vector.tensor_scalar_mul(
+                wb_rounded[b, page][:].rearrange("p i m t -> p m t i"),
+                wb_raw[b][:].rearrange("p t (m i) -> p m t i", i=PACK)[:, :, :, page : page + 2],
+                -1.0,
+            )
+
+        def quantise_wb(b, page):
+            codes = sb([P, 2 * P], U32, f"wb_codes{b}_{page}")
+            plane = sb([P, 2 * P], U8, f"wb_plane{b}_{page}")
             nc.vector.quantize_mx(
                 out=codes[:].bitcast(FP8X4),
                 scales=plane[:],
-                in_=rounded[:].rearrange("p i m t -> p (i m t)"),
+                in_=wb_rounded[b, page][:].rearrange("p i m t -> p (i m t)"),
             )
-            for e in range(count):
-                c, page = halves[e // 2]
-                wb_codes[c, page + e % 2] = codes[:, P * e : P * (e + 1)]
-                wb_plane[c, page + e % 2] = plane[:, P * e : P * (e + 1)]
+            for e in range(2):
+                wb_codes[b, page + e] = codes[:, P * e : P * (e + 1)]
+                wb_plane[b, page + e] = plane[:, P * e : P * (e + 1)]
 
         out_pages = out.rearrange("(p i) t -> i p t", i=PACK)
         steps = []
@@ -294,31 +248,31 @@ def tile_list_armband_gain_sensitivity_kernel(
             u = psum.tile([P, len(parts), BATCH], F32, name="q", tag=f"bank{bank}")
             for part, (i, batch) in enumerate(parts):
                 for b in range(H_PASSES):
+                    cols = slice(b * BATCH, (b + 1) * BATCH)
                     nc.tensor.matmul_mx(
                         out=u[:, part, :],
                         lhsT=wb_codes[b, i].bitcast(FP8X4),
                         lhsT_scale=wb_plane[b, i],
-                        rhs=h_codes[batch, b].bitcast(FP8X4),
-                        rhs_scale=h_plane[batch, b],
+                        rhs=h_codes[batch][:, cols].bitcast(FP8X4),
+                        rhs_scale=h_plane[batch][:, cols],
                         start=(b == 0),
                         stop=(b == H_PASSES - 1),
                     )
             u_flat = u[:].rearrange("p e j -> p (e j)")
-            drive = sb([P, len(parts) * BATCH], F32, f"drive{n}", f"drive{n % 2}")
-            nc.scalar.activation(drive[:], u_flat, ACT.Tanh)
-            return n, parts, u_flat, drive
-
-        def slope_on_vector(n, parts, u_flat, drive):
-            square = sb([P, len(parts) * BATCH], F32, f"square{n}")
-            nc.scalar.activation(square[:], drive[:], ACT.Square)
-            slope = sb([P, len(parts) * BATCH], F32, f"slope{n}")
-            nc.vector.scalar_tensor_tensor(slope[:], square[:], 1.0, u_flat, ALU.subtract, ALU.mult)
-            return slope
-
-        def values_on_gpsimd(n, parts, u_flat, drive, weighted=True):
             width = len(parts) * BATCH
+            drive = sb([P, width], F32, f"drive{n}", f"drive{n}" if n < 4 else f"drive_late{n % 2}")
+            nc.scalar.activation(drive[:], u_flat, ACT.Tanh)
             gated = sb([P, width], F32, f"gated{n}")
             nc.scalar.activation(gated[:], u_flat, ACT.Silu, scale=-2.0)
+            return n, parts, drive, gated
+
+        def slope_on_vector(n, parts, drive, gated):
+            slope = sb([P, len(parts) * BATCH], F32, f"slope{n}")
+            nc.vector.scalar_tensor_tensor(slope[:], drive[:], 1.0, gated[:], ALU.add, ALU.mult)
+            return slope
+
+        def values_on_gpsimd(n, parts, drive, gated, weighted=True):
+            width = len(parts) * BATCH
             rest = sb([P, width], F32, f"rest{n}")
             nc.scalar.activation(rest[:], drive[:], ACT.Identity, bias=1.0)
             values = sb([P, width], F32, f"values{n}")
@@ -344,38 +298,60 @@ def tile_list_armband_gain_sensitivity_kernel(
                 nc.sync.dma_start(out_pages[i], pages[i][:])
 
         low, high = (0, 1), (2, 3)
+        spare = (FIRST_BANKS, FIRST_BANKS + 1)
         every_pass = range(H_PASSES)
 
-        first_product(0, every_pass, early=(0,))
-        quantise_wb((0, 0), (0, 2))
-        quantise_wb((1, 0))
-        move_late_scales()
-        quantise_h()
-        quantise_wb((2, 0))
-        opening = [slope_on_vector(*second_product((0,), (i,), FIRST_BANKS + i)) for i in low]
-        clear_page(3, 4, sb([P, T2], F32, "page3"))
-        quantise_wb((1, 2), (2, 2))
-        first_product(1, every_pass)
+        first_product(0, every_pass, early=EARLY)
+        for page in (0, 2):
+            round_wb(0, page)
+        weight = sb([P, S], F32, "weight", "scale_window")
+        nc.sync.dma_start(weight[:], wgo)
+        for page in (0, 2):
+            quantise_wb(0, page)
+        v_plane.append(sb([P, S // 2], U8, "v_plane_late", "wb_bf0_0"))
+        nc.sync.dma_start(v_plane[2][:].bitcast(I32)[0:MOVED, :], got32[SHIFT : SHIFT + MOVED, S // 8 :])
+        quantise_h(0, 0)
+        for page in (0, 2):
+            round_wb(1, page)
+        quantise_h(0, 1)
+        for page in (0, 2):
+            quantise_wb(1, page)
+        first_product(1, (0, 1))
+        round_wb(2, 0)
+        quantise_wb(2, 0)
+        opening = [second_product((0,), (i,), FIRST_BANKS - 2 + i) for i in low]
+        round_wb(2, 2)
+        quantise_wb(2, 2)
+        quantise_h(1, 0)
+        pages[3] = sb([P, T2], F32, "page3", "h_bf1_0")
+        clear_on_gpsimd(pages[3][:], T2 // 4)
         for i in low:
-            put(i, 0, opening[i][:], False)
-        slope = slope_on_vector(*second_product((0,), high, FIRST_BANKS))
+            put(i, 0, slope_on_vector(*opening[i])[:], False)
+        first_product(1, (2,))
+        quantise_h(1, 1)
+        slope = slope_on_vector(*second_product((0,), high, spare[0]))
         for part, i in enumerate(high):
             put(i, 0, slope[:, part * BATCH : (part + 1) * BATCH], False)
-        first_product(2, every_pass)
-        first_product(3, (0, 1))
-        bridge_slope = slope_on_vector(*second_product((1,), low, filled[-3]))
+        first_product(2, every_pass, banks=(0, 1, spare[1], 3, 4, 5))
+        bridge_slope = slope_on_vector(*second_product((1,), low, spare[1]))
         put(0, BATCH, bridge_slope[:, 0:BATCH], False)
-        first_product(3, (2,))
+        waiting = second_product((1,), high, spare[1])
+        quantise_h(2, 0)
+        quantise_h(2, 1)
+        first_product(3, every_pass)
+        quantise_h(3, 0)
+        quantise_h(3, 1)
         bridge = sb([P, BATCH], F32, "bridge")
         nc.vector.tensor_tensor(bridge[:], bridge_slope[:, BATCH:], weight[:, BATCH : 2 * BATCH], ALU.mult)
         put(1, BATCH, bridge[:], True)
 
-        for i, bank in ((2, filled[-3]), (3, filled[-2])):
-            put(i, BATCH, values_on_gpsimd(*second_product((1,), (i,), bank))[:], True)
-        for batch, bank in ((2, FIRST_BANKS + 1), (3, filled[-1])):
+        values = values_on_gpsimd(*waiting)
+        for part, i in enumerate(high):
+            put(i, BATCH, values[:, part * BATCH : (part + 1) * BATCH], True)
+        for batch, bank in ((2, 0), (3, 1)):
             values = values_on_gpsimd(*second_product((batch,), low, bank))
             for i in low:
                 put(i, batch * BATCH, values[:, i * BATCH : (i + 1) * BATCH], True)
-        put(2, 2 * BATCH, values_on_gpsimd(*second_product((2, 3), (2,), FIRST_BANKS))[:], True)
-        last = second_product((2, 3), (3,), filled[-4])
+        put(2, 2 * BATCH, values_on_gpsimd(*second_product((2, 3), (2,), 2))[:], True)
+        last = second_product((2, 3), (3,), 3)
         put(3, 2 * BATCH, values_on_gpsimd(*last, weighted=False)[:], False)

@@ -30,7 +30,6 @@ SHIFT = 14
 MOVED = 112
 SPARE = 3
 EARLY = (0,)
-VECTOR_CLEARS = 1280
 
 
 def tile_list_armband_gain_sensitivity_kernel(
@@ -44,8 +43,8 @@ def tile_list_armband_gain_sensitivity_kernel(
         spots = {}
         end = 0
         for chain in (
-            (("wb_bf2_0", 4 * P * PACK), ("h_codes1", 12 * BATCH)),
-            (("wa_raw0", 2 * H), ("silu_in", ALIGN * 2), ("wa_raw1", 2 * H), ("wb_raw2", 4 * PACK * N)),
+            (("wb_bf2_2", 4 * P * PACK), ("wb_bf2_0", 4 * P * PACK), ("h_codes1", 12 * BATCH)),
+            (("silu_in", ALIGN * 2), ("wa_raw1", 2 * H), ("wb_raw2", 4 * PACK * N)),
             (("zero_mid", ALIGN * 2), ("table1", 4 * T)),
             (("bridge", 4 * BATCH), ("h_bf3_2", 8 * BATCH), ("weighted4_0", 4 * BATCH)),
         ):
@@ -69,7 +68,7 @@ def tile_list_armband_gain_sensitivity_kernel(
         silu_in = sb([P, ALIGN // 2], F32, "silu_in")
         zero_mid = sb([P, ALIGN // 2], F32, "zero_mid")
         zero_bias = sb([P, 1], F32, "zero_bias")
-        pages = {i: sb([P, T2], F32, f"page{i}") for i in range(PACK - 1)}
+        pages = {i: sb([P, T2], F32, f"page{i}") for i in range(PACK)}
 
         def clear_on_vector(words):
             odd = words.shape[1] // 2 + 1
@@ -84,10 +83,18 @@ def tile_list_armband_gain_sensitivity_kernel(
         nc.gpsimd.memset(scale_window[:].bitcast(I32), 0)
         nc.gpsimd.tensor_copy(silu_in[:, 0:1], zero[:])
         clear_on_vector(wa_scale_raw[:].rearrange("p a c -> p (a c)").bitcast(I32))
-        clear_on_vector(pages[2][:, 0:VECTOR_CLEARS])
+        clear_on_vector(pages[2][:])
+        clear_on_vector(pages[3][:, 0 : T2 // 2])
 
         nc.sync.dma_start(pick[:], offs)
         nc.sync.dma_start(place[:], offs2)
+        wa_raw = []
+
+        def load_wa(a):
+            wa_raw.append(sb([P, H // 2], I32, f"wa_raw{a}"))
+            nc.sync.dma_start(wa_raw[a][:], wa_words.bitcast(I32)[a])
+
+        load_wa(0)
         tab_scale_rows = tab_scales.bitcast(I32)
         window32 = scale_window[:].bitcast(I32)
         nc.sync.dma_start(window32[SPARE:P:8, :], tab_scale_rows[1])
@@ -106,14 +113,12 @@ def tile_list_armband_gain_sensitivity_kernel(
         wa_scale32 = wa_scale_raw[:].bitcast(I32)
         for row in range(4):
             nc.sync.dma_start(wa_scale32[row:P:32, :, :], wa_scale_rows[row])
-        wa_raw = []
-        for a in range(K_PASSES):
-            wa_raw.append(sb([P, H // 2], I32, f"wa_raw{a}"))
-            nc.sync.dma_start(wa_raw[a][:], wa_words.bitcast(I32)[a])
+        load_wa(1)
         load_table(1)
 
         clear_on_gpsimd(pages[0][:], T2 // 2)
         clear_on_gpsimd(pages[1][:], T2 // 2)
+        clear_on_gpsimd(pages[3][:, T2 // 2 :], T2 // 4)
 
         nc.vector.tensor_copy(scale_got[:], scale_window[:].indirect(pick[:]))
         got32 = scale_got[:].bitcast(I32)
@@ -140,8 +145,6 @@ def tile_list_armband_gain_sensitivity_kernel(
                     wa_plane[a, b][:].rearrange("p (t g m) -> p g t m", t=PACK, m=16),
                     wa_scale_raw[:, a, 512 * b : 512 * (b + 1)].rearrange("p (g m t) -> p g t m", t=PACK, m=16),
                 )
-
-        clear_on_gpsimd(pages[2][:, VECTOR_CLEARS:], T2 - VECTOR_CLEARS)
 
         v_words = {}
 
@@ -311,20 +314,18 @@ def tile_list_armband_gain_sensitivity_kernel(
         v_plane.append(sb([P, S // 2], U8, "v_plane_late", "wb_bf0_0"))
         nc.sync.dma_start(v_plane[2][:].bitcast(I32)[0:MOVED, :], got32[SHIFT : SHIFT + MOVED, S // 8 :])
         quantise_h(0, 0)
-        for page in (0, 2):
-            round_wb(1, page)
+        round_wb(1, 0)
         quantise_h(0, 1)
-        for page in (0, 2):
-            quantise_wb(1, page)
+        quantise_wb(1, 0)
         first_product(1, (0, 1))
         round_wb(2, 0)
         quantise_wb(2, 0)
         opening = [second_product((0,), (i,), FIRST_BANKS - 2 + i) for i in low]
+        round_wb(1, 2)
+        quantise_wb(1, 2)
         round_wb(2, 2)
         quantise_wb(2, 2)
         quantise_h(1, 0)
-        pages[3] = sb([P, T2], F32, "page3", "h_bf1_0")
-        clear_on_gpsimd(pages[3][:], T2 // 4)
         for i in low:
             put(i, 0, slope_on_vector(*opening[i])[:], False)
         first_product(1, (2,))

@@ -30,6 +30,7 @@ SHIFT = 14
 MOVED = 112
 SPARE = 3
 EARLY = (0,)
+WARM_PASSES = 6
 
 
 def tile_list_armband_gain_sensitivity_kernel(
@@ -83,6 +84,8 @@ def tile_list_armband_gain_sensitivity_kernel(
         nc.gpsimd.memset(scale_window[:].bitcast(I32), 0)
         nc.gpsimd.tensor_copy(silu_in[:, 0:1], zero[:])
         clear_on_vector(wa_scale_raw[:].rearrange("p a c -> p (a c)").bitcast(I32))
+        first_codes = sb([P, H_PASSES * BATCH], U32, "h_codes0")
+        clear_on_vector(first_codes[:, 0:BATCH].bitcast(I32))
         clear_on_vector(pages[2][:])
         clear_on_vector(pages[3][:, 0 : T2 // 2])
 
@@ -155,6 +158,17 @@ def tile_list_armband_gain_sensitivity_kernel(
                 v_words[a, j] = got[:, j - lo : j - lo + SUB]
 
         gather_words(0, 0, BATCH)
+        warm = psum.tile([P, BATCH], F32, name="warm", tag=f"bank{FIRST_BANKS + 1}")
+        for e in range(WARM_PASSES):
+            nc.tensor.matmul_mx(
+                out=warm[:],
+                lhsT=wa_codes[0, 0][:, 0 : 2 * P].bitcast(FP4X4),
+                lhsT_scale=wa_plane[0, 0][:, 0:P],
+                rhs=first_codes[:, 0:BATCH].bitcast(FP8X4),
+                rhs_scale=wa_plane[0, 0][:, 0:BATCH],
+                start=True,
+                stop=True,
+            )
         gather_words(0, BATCH, S)
         gather_words(1, 0, BATCH)
         gather_words(1, BATCH, S)
@@ -210,7 +224,7 @@ def tile_list_armband_gain_sensitivity_kernel(
 
         def quantise_h(batch, part):
             if part == 0:
-                h_codes[batch] = sb([P, H_PASSES * BATCH], U32, f"h_codes{batch}")
+                h_codes[batch] = sb([P, H_PASSES * BATCH], U32, f"h_codes{batch}") if batch else first_codes
                 h_plane[batch] = sb([P, H_PASSES * BATCH], U8, f"h_plane{batch}")
             cols = slice(2 * part * BATCH, (2 + part) * BATCH)
             nc.vector.quantize_mx(

@@ -69,7 +69,7 @@ def tile_list_armband_gain_sensitivity_kernel(
         silu_in = sb([P, ALIGN // 2], F32, "silu_in")
         zero_mid = sb([P, ALIGN // 2], F32, "zero_mid")
         zero_bias = sb([P, 1], F32, "zero_bias")
-        pages = {i: sb([P, T2], F32, f"page{i}") for i in range(PACK)}
+        pages = {i: sb([P, T2], F32, f"page{i}") for i in range(PACK - 1)}
 
         def clear_on_vector(words):
             odd = words.shape[1] // 2 + 1
@@ -86,8 +86,7 @@ def tile_list_armband_gain_sensitivity_kernel(
         clear_on_vector(wa_scale_raw[:].rearrange("p a c -> p (a c)").bitcast(I32))
         first_codes = sb([P, H_PASSES * BATCH], U32, "h_codes0")
         clear_on_vector(first_codes[:, 0:BATCH].bitcast(I32))
-        clear_on_vector(pages[2][:])
-        clear_on_vector(pages[3][:, 0 : T2 // 2])
+        clear_on_vector(pages[2][:, 0 : T2 // 2])
 
         nc.sync.dma_start(pick[:], offs)
         nc.sync.dma_start(place[:], offs2)
@@ -121,7 +120,7 @@ def tile_list_armband_gain_sensitivity_kernel(
 
         clear_on_gpsimd(pages[0][:], T2 // 2)
         clear_on_gpsimd(pages[1][:], T2 // 2)
-        clear_on_gpsimd(pages[3][:, T2 // 2 :], T2 // 4)
+        clear_on_gpsimd(pages[2][:, T2 // 2 :], T2 // 4)
 
         nc.vector.tensor_copy(scale_got[:], scale_window[:].indirect(pick[:]))
         got32 = scale_got[:].bitcast(I32)
@@ -143,11 +142,14 @@ def tile_list_armband_gain_sensitivity_kernel(
                     wa_codes[a, b][:].bitcast(U16).rearrange("p (t g m) -> p g t m", t=PACK, m=8),
                     wa_raw[a][:, 256 * b : 256 * (b + 1)].bitcast(U16).rearrange("p (g m t) -> p g t m", t=PACK, m=8),
                 )
-                wa_plane[a, b] = sb([P, 512], U8, f"wa_plane{a}_{b}")
-                nc.gpsimd.tensor_copy(
-                    wa_plane[a, b][:].rearrange("p (t g m) -> p g t m", t=PACK, m=16),
-                    wa_scale_raw[:, a, 512 * b : 512 * (b + 1)].rearrange("p (g m t) -> p g t m", t=PACK, m=16),
-                )
+        for b in range(H_PASSES):
+            planes = sb([P, K_PASSES, 512], U8, f"wa_plane{b}")
+            nc.gpsimd.tensor_copy(
+                planes[:].rearrange("p a (t m) -> p a t m", t=PACK),
+                wa_scale_raw[:, :, 512 * b : 512 * (b + 1)].rearrange("p a (m t) -> p a t m", t=PACK),
+            )
+            for a in range(K_PASSES):
+                wa_plane[a, b] = planes[:, a, :]
 
         v_words = {}
 
@@ -340,6 +342,8 @@ def tile_list_armband_gain_sensitivity_kernel(
         round_wb(2, 2)
         quantise_wb(2, 2)
         quantise_h(1, 0)
+        pages[3] = sb([P, T2], F32, "page3", "h_bf1_0")
+        clear_on_gpsimd(pages[3][:], T2 // 8)
         for i in low:
             put(i, 0, slope_on_vector(*opening[i])[:], False)
         first_product(1, (2,))

@@ -46,7 +46,7 @@ def tile_list_armband_gain_sensitivity_kernel(
         for chain in (
             (("wb_bf2_2", 4 * P * PACK), ("wb_bf2_0", 4 * P * PACK), ("h_codes1", 12 * BATCH)),
             (("silu_in", ALIGN * 2), ("wa_raw1", 2 * H), ("wb_raw2", 4 * PACK * N)),
-            (("zero_mid", ALIGN * 2), ("table1", 4 * T)),
+            (("zero_mid", ALIGN * 2), ("table1", 4 * T), ("v_plane_late", 2 * BATCH)),
             (("bridge", 4 * BATCH), ("h_bf3_2", 8 * BATCH), ("weighted4_0", 4 * BATCH)),
         ):
             for name, size in chain:
@@ -80,8 +80,8 @@ def tile_list_armband_gain_sensitivity_kernel(
             for lo in range(0, words.shape[1], piece):
                 nc.gpsimd.memset(words[:, lo : lo + piece], 0.0)
 
-        nc.gpsimd.memset(zero[:], 0.0)
         nc.gpsimd.memset(scale_window[:].bitcast(I32), 0)
+        nc.vector.memset(zero[:], 0.0)
         nc.gpsimd.tensor_copy(silu_in[:, 0:1], zero[:])
         clear_on_vector(wa_scale_raw[:].rearrange("p a c -> p (a c)").bitcast(I32))
         first_codes = sb([P, H_PASSES * BATCH], U32, "h_codes0")
@@ -89,7 +89,6 @@ def tile_list_armband_gain_sensitivity_kernel(
         clear_on_vector(pages[2][:, 0 : T2 // 2])
 
         nc.sync.dma_start(pick[:], offs)
-        nc.sync.dma_start(place[:], offs2)
         wa_raw = []
 
         def load_wa(a):
@@ -111,6 +110,7 @@ def tile_list_armband_gain_sensitivity_kernel(
             nc.sync.dma_start(table[a][:], tab_words[a].rearrange("p t i -> p (t i)").bitcast(I32))
 
         load_table(0)
+        nc.sync.dma_start(place[:], offs2)
         wa_scale_rows = wa_scales.bitcast(I32).rearrange("a (d r) c -> r d a c", r=4)
         wa_scale32 = wa_scale_raw[:].bitcast(I32)
         for row in range(4):
@@ -320,6 +320,8 @@ def tile_list_armband_gain_sensitivity_kernel(
         spare = (FIRST_BANKS, FIRST_BANKS + 1)
         every_pass = range(H_PASSES)
 
+        v_plane.append(sb([P, S // 2], U8, "v_plane_late"))
+        nc.sync.dma_start(v_plane[2][:].bitcast(I32)[0:MOVED, :], got32[SHIFT : SHIFT + MOVED, S // 8 :])
         first_product(0, every_pass, early=EARLY)
         for page in (0, 2):
             round_wb(0, page)
@@ -327,8 +329,6 @@ def tile_list_armband_gain_sensitivity_kernel(
         nc.sync.dma_start(weight[:], wgo)
         for page in (0, 2):
             quantise_wb(0, page)
-        v_plane.append(sb([P, S // 2], U8, "v_plane_late", "wb_bf0_0"))
-        nc.sync.dma_start(v_plane[2][:].bitcast(I32)[0:MOVED, :], got32[SHIFT : SHIFT + MOVED, S // 8 :])
         quantise_h(0, 0)
         round_wb(1, 0)
         quantise_h(0, 1)

from contextlib import ExitStack

import concourse.mybir as mybir

K, H, N, T, S, T2 = 1024, 1536, 512, 2048, 1024, 2048
FLOPS = 2 * K * H * S + 2 * H * N * S

F32 = mybir.dt.float32
BF16 = mybir.dt.bfloat16
I32 = mybir.dt.int32
U32 = mybir.dt.uint32
U16 = mybir.dt.uint16
U8 = mybir.dt.uint8
FP8X4 = mybir.dt.float8_e4m3fn_x4
FP4X4 = mybir.dt.float4_e2m1fn_x4
ACT = mybir.ActivationFunctionType
ALU = mybir.AluOpType

P = 128
PACK = 4
GROUP = 16
QUADS = 4
K_PASSES = K // 512
H_PASSES = H // 512
BATCH = 256
SUB = 128
FIRST_BANKS = 6
ALIGN = 64
SHIFT = 14
MOVED = 112
SPARE = 3
EARLY = (0,)
WARM_PASSES = 6


def tile_list_armband_gain_sensitivity_kernel(
    tc, tab_words, tab_scales, wa_words, wa_scales, wb, wgo, offs, offs2, out
):
    nc = tc.nc
    with ExitStack() as ctx:
        lists = ctx.enter_context(tc.tile_pool(name="lists", bufs=1))
        keep = ctx.enter_context(tc.tile_pool(name="keep", bufs=1))
        held = ctx.enter_context(tc.tile_pool(name="held", bufs=1))
        spots = {}
        end = 0
        for chain in (
            (("wb_bf2_2", 4 * P * PACK), ("wb_bf2_0", 4 * P * PACK), ("h_codes1", 12 * BATCH)),
            (("silu_in", ALIGN * 2), ("wa_raw1", 2 * H), ("wb_raw2", 4 * PACK * N)),
            (("zero_mid", ALIGN * 2), ("table1", 4 * T), ("v_plane_late", 2 * BATCH)),
            (("bridge", 4 * BATCH), ("h_bf3_2", 8 * BATCH), ("weighted4_0", 4 * BATCH)),
        ):
            for name, size in chain:
                spots[name] = end
                end = end + size - ALIGN
            end = end + ALIGN
        psum = ctx.enter_context(tc.psum_pool(name="psum", bufs=1))

        def sb(shape, dtype, name, takes_over=None):
            if name in spots:
                return held.tile(shape, dtype, name=name, align_bytes=ALIGN, offset=spots[name])
            return keep.tile(shape, dtype, name=name, tag=takes_over or name, align_bytes=ALIGN)

        pick = lists.tile([P, S // GROUP], U16, name="pick")
        place = lists.tile([P, S // GROUP], U16, name="place")
        scale_window = sb([P, T], U8, "scale_window")
        wa_scale_raw = sb([P, K_PASSES, H], U8, "wa_scale_raw")
        scale_got = sb([P, S], U8, "scale_got")
        zero = sb([P, 1], F32, "zero", "table0")
        silu_in = sb([P, ALIGN // 2], F32, "silu_in")
        zero_mid = sb([P, ALIGN // 2], F32, "zero_mid")
        zero_bias = sb([P, 1], F32, "zero_bias")
        pages = {i: sb([P, T2], F32, f"page{i}") for i in range(PACK - 1)}

        def clear_on_vector(words):
            odd = words.shape[1] // 2 + 1
            nc.vector.memset(words[:, 0:odd], 0)
            nc.vector.memset(words[:, odd:], 0)

        def clear_on_gpsimd(words, piece):
            for lo in range(0, words.shape[1], piece):
                nc.gpsimd.memset(words[:, lo : lo + piece], 0.0)

        nc.gpsimd.memset(scale_window[:].bitcast(I32), 0)
        nc.vector.memset(zero[:], 0.0)
        nc.gpsimd.tensor_copy(silu_in[:, 0:1], zero[:])
        clear_on_vector(wa_scale_raw[:].rearrange("p a c -> p (a c)").bitcast(I32))
        first_codes = sb([P, H_PASSES * BATCH], U32, "h_codes0")
        clear_on_vector(first_codes[:, 0:BATCH].bitcast(I32))
        clear_on_vector(pages[2][:, 0 : T2 // 2])

        nc.sync.dma_start(pick[:], offs)
        wa_raw = []

        def load_wa(a):
            wa_raw.append(sb([P, H // 2], I32, f"wa_raw{a}"))
            nc.sync.dma_start(wa_raw[a][:], wa_words.bitcast(I32)[a])

        load_wa(0)
        tab_scale_rows = tab_scales.bitcast(I32)
        window32 = scale_window[:].bitcast(I32)
        nc.sync.dma_start(window32[SPARE:P:8, :], tab_scale_rows[1])
        for d in range(QUADS):
            nc.sync.dma_start(window32[32 * d + SHIFT : 32 * d + SHIFT + 4, :], tab_scale_rows[0, 4 * d : 4 * d + 4, :])
        nc.scalar.activation(zero_mid[:, 0:1], silu_in[:, 0:1], ACT.Silu)
        nc.scalar.activation(zero_bias[:], zero_mid[:, 0:1], ACT.Tanh)
        table = []

        def load_table(a):
            table.append(sb([P, T], I32, f"table{a}"))
            nc.sync.dma_start(table[a][:], tab_words[a].rearrange("p t i -> p (t i)").bitcast(I32))

        load_table(0)
        nc.sync.dma_start(place[:], offs2)
        wa_scale_rows = wa_scales.bitcast(I32).rearrange("a (d r) c -> r d a c", r=4)
        wa_scale32 = wa_scale_raw[:].bitcast(I32)
        for row in range(4):
            nc.sync.dma_start(wa_scale32[row:P:32, :, :], wa_scale_rows[row])
        load_wa(1)
        load_table(1)

        clear_on_gpsimd(pages[0][:], T2 // 2)
        clear_on_gpsimd(pages[1][:], T2 // 2)
        clear_on_gpsimd(pages[2][:, T2 // 2 :], T2 // 4)

        nc.vector.tensor_copy(scale_got[:], scale_window[:].indirect(pick[:]))
        got32 = scale_got[:].bitcast(I32)
        v_plane = []

        def move_scales():
            v_plane.extend((sb([P, S // 2], U8, "v_plane0"), sb([P, S], U8, "v_plane1")))
            nc.sync.dma_start(v_plane[0][:].bitcast(I32)[0:MOVED, :], got32[SHIFT : SHIFT + MOVED, 0 : S // 8])
            for row in range(4):
                nc.sync.dma_start(v_plane[1][:].bitcast(I32)[row:P:32, :], got32[8 * row + SPARE : P : 32, :])

        wa_codes, wa_plane = {}, {}
        for a in range(K_PASSES):
            if a == 1:
                move_scales()
            for b in range(H_PASSES):
                wa_codes[a, b] = sb([P, 1024], U8, f"wa_codes{a}_{b}")
                nc.scalar.copy(
                    wa_codes[a, b][:].bitcast(U16).rearrange("p (t g m) -> p g t m", t=PACK, m=8),
                    wa_raw[a][:, 256 * b : 256 * (b + 1)].bitcast(U16).rearrange("p (g m t) -> p g t m", t=PACK, m=8),
                )
        for b in range(H_PASSES):
            planes = sb([P, K_PASSES, 512], U8, f"wa_plane{b}")
            nc.gpsimd.tensor_copy(
                planes[:].rearrange("p a (t m) -> p a t m", t=PACK),
                wa_scale_raw[:, :, 512 * b : 512 * (b + 1)].rearrange("p a (m t) -> p a t m", t=PACK),
            )
            for a in range(K_PASSES):
                wa_plane[a, b] = planes[:, a, :]

        v_words = {}

        def gather_words(a, lo, hi):
            got = sb([P, hi - lo], U32, f"v_words{a}_{lo}")
            nc.vector.tensor_copy(got[:], table[a][:].bitcast(U32).indirect(pick[:, lo // GROUP : hi // GROUP]))
            for j in range(lo, hi, SUB):
                v_words[a, j] = got[:, j - lo : j - lo + SUB]

        gather_words(0, 0, BATCH)
        warm = psum.tile([P, BATCH], F32, name="warm", tag=f"bank{FIRST_BANKS + 1}")
        for e in range(WARM_PASSES):
            nc.tensor.matmul_mx(
                out=warm[:],
                lhsT=wa_codes[0, 0][:, 0 : 2 * P].bitcast(FP4X4),
                lhsT_scale=wa_plane[0, 0][:, 0:P],
                rhs=first_codes[:, 0:BATCH].bitcast(FP8X4),
                rhs_scale=wa_plane[0, 0][:, 0:BATCH],
                start=True,
                stop=True,
            )
        gather_words(0, BATCH, S)
        gather_words(1, 0, BATCH)
        gather_words(1, BATCH, S)

        wb_rows = wb.rearrange("(b p t) n -> b p t n", b=H_PASSES, t=PACK)
        wb_raw = []
        for b, tenant in enumerate(("scale_window", "table0", None)):
            wb_raw.append(sb([P, PACK, N], F32, f"wb_raw{b}", tenant))
            nc.sync.dma_start(wb_raw[b][:], wb_rows[b])

        h_codes, h_plane, h_rounded = {}, {}, {}


        def first_matmul(acc, b, j, t, a, start, stop):
            nc.tensor.matmul_mx(
                out=acc[:, t, :],
                lhsT=wa_codes[a, b][:, 2 * P * t : 2 * P * (t + 1)].bitcast(FP4X4),
                lhsT_scale=wa_plane[a, b][:, P * t : P * (t + 1)],
                rhs=v_words[a, j].bitcast(FP8X4),
                rhs_scale=v_plane[a][:, j : j + SUB] if a == 1 or j < S // 2 else v_plane[2][:, j - S // 2 : j - S // 2 + SUB],
                start=start,
                stop=stop,
            )

        def first_product(batch, passes, early=(), banks=range(FIRST_BANKS)):
            lo = batch * BATCH
            accs = {}
            for b in early:
                for j in range(lo, lo + BATCH, SUB):
                    accs[b, j] = psum.tile([P, PACK, SUB], F32, name="acc", tag=f"bank{banks[2 * b + (j - lo) // SUB]}")
                    for t in range(PACK):
                        first_matmul(accs[b, j], b, j, t, 0, t == 0, False)
            for b in passes:
                if b != 1:
                    h_rounded[batch, b // 2] = sb([P, (2 - b // 2) * BATCH, PACK], BF16, f"h_bf{batch}_{b}")
                h_bf = h_rounded[batch, b // 2][:, b % 2 * BATCH : (b % 2 + 1) * BATCH, :]
                for j in range(lo, lo + BATCH, SUB):
                    if b in early:
                        acc = accs[b, j]
                        for t in range(PACK):
                            first_matmul(acc, b, j, t, 1, False, t == PACK - 1)
                    else:
                        acc = psum.tile([P, PACK, SUB], F32, name="acc", tag=f"bank{banks[2 * b + (j - lo) // SUB]}")
                        for t in range(PACK):
                            first_matmul(acc, b, j, t, 1, True, False)
                            first_matmul(acc, b, j, t, 0, False, True)
                    nc.scalar.activation(
                        h_bf[:, j - lo : j - lo + SUB, :].rearrange("p (j e) t -> p j t e", e=2),
                        acc[:].rearrange("p t (j e) -> p j t e", e=2),
                        ACT.Relu,
                        bias=zero_bias[:] if (b, j) == (0, 0) else 0.0,
                    )

        def quantise_h(batch, part):
            if part == 0:
                h_codes[batch] = sb([P, H_PASSES * BATCH], U32, f"h_codes{batch}") if batch else first_codes
                h_plane[batch] = sb([P, H_PASSES * BATCH], U8, f"h_plane{batch}")
            cols = slice(2 * part * BATCH, (2 + part) * BATCH)
            nc.vector.quantize_mx(
                out=h_codes[batch][:, cols].bitcast(FP8X4),
                scales=h_plane[batch][:, cols],
                in_=h_rounded[batch, part][:].rearrange("p j t -> p (j t)"),
            )

        wb_rounded, wb_codes, wb_plane = {}, {}, {}

        def round_wb(b, page):
            wb_rounded[b, page] = sb([P, 2, P, PACK], BF16, f"wb_bf{b}_{page}")
            nc.vector.tensor_scalar_mul(
                wb_rounded[b, page][:].rearrange("p i m t -> p m t i"),
                wb_raw[b][:].rearrange("p t (m i) -> p m t i", i=PACK)[:, :, :, page : page + 2],
                -1.0,
            )

        def quantise_wb(b, page):
            codes = sb([P, 2 * P], U32, f"wb_codes{b}_{page}")
            plane = sb([P, 2 * P], U8, f"wb_plane{b}_{page}")
            nc.vector.quantize_mx(
                out=codes[:].bitcast(FP8X4),
                scales=plane[:],
                in_=wb_rounded[b, page][:].rearrange("p i m t -> p (i m t)"),
            )
            for e in range(2):
                wb_codes[b, page + e] = codes[:, P * e : P * (e + 1)]
                wb_plane[b, page + e] = plane[:, P * e : P * (e + 1)]

        out_pages = out.rearrange("(p i) t -> i p t", i=PACK)
        steps = []

        def second_product(batches, step_pages, bank):
            n = len(steps)
            steps.append(n)
            parts = [(i, batch) for i in step_pages for batch in batches]
            u = psum.tile([P, len(parts), BATCH], F32, name="q", tag=f"bank{bank}")
            for part, (i, batch) in enumerate(parts):
                for b in range(H_PASSES):
                    cols = slice(b * BATCH, (b + 1) * BATCH)
                    nc.tensor.matmul_mx(
                        out=u[:, part, :],
                        lhsT=wb_codes[b, i].bitcast(FP8X4),
                        lhsT_scale=wb_plane[b, i],
                        rhs=h_codes[batch][:, cols].bitcast(FP8X4),
                        rhs_scale=h_plane[batch][:, cols],
                        start=(b == 0),
                        stop=(b == H_PASSES - 1),
                    )
            u_flat = u[:].rearrange("p e j -> p (e j)")
            width = len(parts) * BATCH
            drive = sb([P, width], F32, f"drive{n}", f"drive{n}" if n < 4 else f"drive_late{n % 2}")
            nc.scalar.activation(drive[:], u_flat, ACT.Tanh)
            gated = sb([P, width], F32, f"gated{n}")
            nc.scalar.activation(gated[:], u_flat, ACT.Silu, scale=-2.0)
            return n, parts, drive, gated

        def slope_on_vector(n, parts, drive, gated):
            slope = sb([P, len(parts) * BATCH], F32, f"slope{n}")
            nc.vector.scalar_tensor_tensor(slope[:], drive[:], 1.0, gated[:], ALU.add, ALU.mult)
            return slope

        def values_on_gpsimd(n, parts, drive, gated, weighted=True):
            width = len(parts) * BATCH
            rest = sb([P, width], F32, f"rest{n}")
            nc.scalar.activation(rest[:], drive[:], ACT.Identity, bias=1.0)
            values = sb([P, width], F32, f"values{n}")
            lo = parts[0][1] * BATCH
            run = width if parts[0][0] == parts[-1][0] else BATCH
            for at in range(0, width, run):
                factor = gated[:, at : at + run]
                if weighted:
                    product = sb([P, run], F32, f"weighted{n}_{at}")
                    nc.gpsimd.tensor_tensor(product[:], factor, weight[:, lo : lo + run], ALU.mult)
                    factor = product[:]
                nc.gpsimd.tensor_tensor(values[:, at : at + run], factor, rest[:, at : at + run], ALU.mult)
            return values

        def put(i, lo, values, weighted):
            hi = lo + values.shape[1]
            slots = pages[i][:].indirect(place[:, lo // GROUP : hi // GROUP])
            if weighted:
                nc.vector.tensor_copy(slots, values)
            else:
                nc.vector.tensor_tensor(slots, values, weight[:, lo:hi], ALU.mult)
            if hi == S:
                nc.sync.dma_start(out_pages[i], pages[i][:])

        low, high = (0, 1), (2, 3)
        spare = (FIRST_BANKS, FIRST_BANKS + 1)
        every_pass = range(H_PASSES)

        v_plane.append(sb([P, S // 2], U8, "v_plane_late"))
        nc.sync.dma_start(v_plane[2][:].bitcast(I32)[0:MOVED, :], got32[SHIFT : SHIFT + MOVED, S // 8 :])
        first_product(0, every_pass, early=EARLY)
        for page in (0, 2):
            round_wb(0, page)
        weight = sb([P, S], F32, "weight", "scale_window")
        nc.sync.dma_start(weight[:], wgo)
        for page in (0, 2):
            quantise_wb(0, page)
        quantise_h(0, 0)
        round_wb(1, 0)
        quantise_h(0, 1)
        quantise_wb(1, 0)
        first_product(1, (0, 1))
        round_wb(2, 0)
        quantise_wb(2, 0)
        opening = [second_product((0,), (i,), FIRST_BANKS - 2 + i) for i in low]
        round_wb(1, 2)
        quantise_wb(1, 2)
        round_wb(2, 2)
        quantise_wb(2, 2)
        quantise_h(1, 0)
        pages[3] = sb([P, T2], F32, "page3", "h_bf1_0")
        clear_on_gpsimd(pages[3][:], T2 // 8)
        for i in low:
            put(i, 0, slope_on_vector(*opening[i])[:], False)
        first_product(1, (2,))
        quantise_h(1, 1)
        slope = slope_on_vector(*second_product((0,), high, spare[0]))
        for part, i in enumerate(high):
            put(i, 0, slope[:, part * BATCH : (part + 1) * BATCH], False)
        first_product(2, every_pass, banks=(0, 1, spare[1], 3, 4, 5))
        bridge_slope = slope_on_vector(*second_product((1,), low, spare[1]))
        put(0, BATCH, bridge_slope[:, 0:BATCH], False)
        waiting = second_product((1,), high, spare[1])
        quantise_h(2, 0)
        quantise_h(2, 1)
        first_product(3, every_pass)
        quantise_h(3, 0)
        quantise_h(3, 1)
        bridge = sb([P, BATCH], F32, "bridge")
        nc.vector.tensor_tensor(bridge[:], bridge_slope[:, BATCH:], weight[:, BATCH : 2 * BATCH], ALU.mult)
        put(1, BATCH, bridge[:], True)

        values = values_on_gpsimd(*waiting)
        for part, i in enumerate(high):
            put(i, BATCH, values[:, part * BATCH : (part + 1) * BATCH], True)
        for batch, bank in ((2, 0), (3, 1)):
            values = values_on_gpsimd(*second_product((batch,), low, bank))
            for i in low:
                put(i, batch * BATCH, values[:, i * BATCH : (i + 1) * BATCH], True)
        put(2, 2 * BATCH, values_on_gpsimd(*second_product((2, 3), (2,), 2))[:], True)
        last = second_product((2, 3), (3,), 3)
        put(3, 2 * BATCH, values_on_gpsimd(*last, weighted=False)[:], False)
